import numpy as np, ml_dtypes
CORES = [36,164,52,180,100,228,116,244]
N = 8
BF = ml_dtypes.bfloat16
def gentries(a):
    return np.ascontiguousarray(a.reshape(8, 16, -1).transpose(0, 2, 1)).reshape(8, -1)
def gtable(e):
    e = np.asarray(e); return np.ascontiguousarray(e.reshape(8, -1, 16).transpose(0, 2, 1)).reshape(128, -1).astype(np.int32)
V, NL, NB, L, CAP, T = 1024, 2048, 1024, 256, 96, 4
CN, Q = 128, NL // 64
D = np.arange(16)
def nearby(rng, J, K, P):
    a = 2 * int(rng.integers(0, 8)); x = int(rng.integers(0, 16))
    P[2, a] = rng.integers(1, 8); P[2, a + 1] = rng.integers(-7, 7); P[3] = P[2]; P[3, a] -= 8; P[3, a + 1] += 1
    P[6, x] = rng.integers(-5, 8); P[7] = P[6]; P[7, x] -= 2
    P[10, x] = rng.integers(-7, 7); P[11] = P[10]; P[11, x] += 1
    for r in range(8):
        c = 64 + r; o = rng.permutation(16); d = 2 * int(rng.integers(0, 8))
        J[c, o[:8]] = 7; J[c, o[8:15]] = 6; J[c, o[15]] = 0
        K[c] = rng.integers(0, Q, 16); K[c, d] = 6; K[c, d + 1] = 10; K[c, d ^ 2] = 2
        for k in range(1, 5): J[c + 8 * k] = J[c]; K[c + 8 * k] = K[c]
        J[c + 8, o[15]] = 1
        J[c + 16, o[0]] = 6; J[c + 16, o[8]] = 7
        K[c + 24, d ^ 2] = 3
        K[c + 32, d] = 7; K[c + 32, d + 1] = 11
def classes(rng, how):
    c = np.arange(CN); fam = (c // 8 % 4)[:, None]; q = np.arange(Q)[:, None]; bits = 1 << rng.integers(0, 4, 3)
    if how == "ends":
        k = rng.integers(0, 17, CN); k[[0, 8, 16, 24]] = (16, 0, 1, 15)
        J = 7 * (np.argsort(rng.random((CN, 16)), axis=1) < k[:, None]); K = rng.integers(0, 2, (CN, 16)); K[0] = 0; K[8] = 1
        P = 7 - 14 * rng.integers(0, 2, (Q, 16)); P[1] = 7
        return J, K, P
    J = rng.integers(0, 8, (CN, 16)); K = rng.integers(0, Q, (CN, 16)); P = rng.integers(-7, 8, (Q, 16))
    mk = np.where(c // 32 == 0, 15 - bits[0], 15)
    if how == "spread":
        J = (8 * rng.random((CN, 16)) ** 3).astype(np.int64); P = np.rint(rng.integers(1, 8, (Q, 1)) * (2 * rng.random((Q, 16)) - 1)).astype(np.int64)
    if how == "alike": mk = rng.choice(np.array([0, 1, 6, 8, 9, 15]), CN)
    K = np.where(fam == 0, K // 4 * 4, np.where(fam == 1, K // 4 * 4 + 1, K))
    if how == "alike": K[c // 32 == 1] = 0
    km = np.where(rng.random(CN) < 0.5, mk, 15)
    J = np.take_along_axis(J, D[None, :] & mk[:, None], 1); K = np.take_along_axis(K, D[None, :] & km[:, None], 1)
    P = np.where(q % 4 == 0, P[:, D & (15 - bits[1])], P)
    P = np.where(q % 4 == 1, P[:, D & (15 - bits[2])] * (1 - 2 * ((D & bits[2]) > 0)), P)
    if how == "alike":
        P[0] = 0; nearby(rng, J, K, P)
    else:
        pa = np.where(mk == 15, 1, 15 - mk); J[c, 0] = 0; J[c, pa] = 0
        x = (c - np.add.reduce(J, axis=1) // 2) % 8; J[c, 0] = x; J[c, pa] = x
    return J, K, P
def swap(p, i, x):
    j = int(np.flatnonzero(p == x)[0]); p[j] = p[i]; p[i] = x
def places(rng, J, K, P, faults, ends=False):
    idx = np.argsort(rng.random((N, 8, V)), axis=-1); cp = np.argsort(rng.random((N, 8, NL)), axis=-1)
    sh = rng.integers(0, 16, (N, 8, V)); lm = rng.integers(0, 16, (N, 8, V)); ls = rng.integers(0, 2, (N, 8, V))
    if ends:
        own = rng.random((N, 8, V)) < 0.75; own[..., 0] = True; own[..., V - 1] = True
        pm = 15 * rng.integers(0, 2, (N, 8, 1)); ps = rng.integers(0, 2, (N, 8, 1)); lm = np.where(own, pm, lm); ls = np.where(own, ps, ls)
        sh[..., 0] = 15 * rng.integers(0, 2, (N, 8)); sh[..., V - 1] = 15 * rng.integers(0, 2, (N, 8))
        for q in range(N):
            for h in range(8):
                z = rng.permutation(np.array([0, 8, 16, 24]))[:2] + CN * rng.integers(0, 2, 2)
                if q == N - 1 and h == 7: z = np.array([8, 0])
                swap(idx[q, h], 0, int(z[0])); swap(idx[q, h], V - 1, int(z[1]))
                tr = int(2 * pm[q, h, 0] + ps[q, h, 0]); swap(cp[q, h], tr, 0); swap(cp[q, h], 32 + tr, NL - 1)
    cls = (idx % CN)[:, :, None, :]; fault = np.where(idx // CN % 2 == 0, 0, rng.choice(np.array(faults), (N, 8, V)))[:, :, None, :]
    e = D[:, None] ^ sh[:, :, None, :]; iv = J[cls, e]; lc = K[cls, e]
    at = rng.integers(0, 16, (N, 8, 1, V)) == D[:, None]
    lc = np.where(at & (fault == 4), (lc + rng.integers(1, Q, (N, 8, 1, V))) % Q, lc)
    m = np.where(at & (fault == 2), (lm ^ rng.integers(1, 16, (N, 8, V)))[:, :, None, :], lm[:, :, None, :])
    s = np.where(at & (fault == 3), 1 - ls[:, :, None, :], ls[:, :, None, :])
    made = lc * 32 + m * 2 + s + (at & (fault == 1)) * (NL // 2)
    kids = np.take_along_axis(cp, made.reshape(N, 8, 16 * V), 2).reshape(N, 8, 16, V)
    i = np.arange(NL // 2); z = (P[i // 32, D[:, None] ^ (i % 32 // 2)] * (1 - 2 * (i % 2))).astype(np.int8)
    near = np.where(rng.integers(0, 16, (N, 8, 1, NL // 2)) == D[:, None], np.where(z > 0, z - 1, z + 1), z).astype(np.int8)
    x = np.concatenate([np.broadcast_to(z, near.shape), near], axis=3)
    lf = np.take_along_axis(x, np.argsort(cp, axis=-1)[:, :, None, :], 3)
    return lf, iv, kids, idx, np.argsort(idx, axis=-1)
def nodes(rng, inv, odd):
    c = np.arange(N)[:, None, None] + 8 * rng.integers(0, CN // 8, (N, 8, L))
    return np.take_along_axis(inv, (2 * rng.integers(0, V // CN // 2, (N, 8, L)) + (rng.random((N, 8, L)) < odd)) * CN + c, 2)
def cold(rng, inv):
    col = np.array([7 if N < 8 else (q + 1) % 8 for q in range(N)])[:, None, None]
    code = col + 8 * rng.integers(0, CN // 8, (N, 8, 16 * NB)) + CN * rng.integers(0, V // CN, (N, 8, 16 * NB))
    return np.take_along_axis(inv, code, 2).reshape(N, 8, 16, NB)
def buckets(rng, inv, idx, v, b, want, base, reps):
    bk = base.copy()
    for t in range(T):
        for q in range(N):
            for h in range(8):
                r, g = (q - t) % N, (h - t * (t + 1) // 2) % 8
                c = idx[r, g][v[r, g]] % CN; w = want[r, g, t]
                for j in range(reps):
                    odd = np.where(w == 3, rng.integers(0, 2, L), (w == 1).astype(np.int64))
                    n = inv[q, h][(2 * rng.integers(0, V // CN // 2, L) + odd) * CN + c]
                    on = (w > 0) & ((j == 0) | (rng.random(L) < 0.4))
                    bk[q, h, 3 * t + j, b[r, g][on]] = n[on]
    return np.take_along_axis(bk, np.argsort(rng.random(bk.shape), axis=2), 2)
def wish(rng, rates, values):
    rate = rng.choice(np.array(rates), (N, 8, T, 1))
    return np.where(rng.random((N, 8, T, L)) < rate, rng.choice(np.array(values), (N, 8, T, L)), 0)
def pack(lf, iv, kids, bk, v, b):
    return {"lf": lf.reshape(N, 128, NL).astype(np.float32).astype(BF), "iv": iv.reshape(N, 128, V).astype(np.float32).astype(BF), "kd": kids.reshape(N, 128, V).astype(np.int32),
            "bk": bk.reshape(N, 128, NB).astype(np.int32), "lv": np.stack([gtable(x) for x in v]), "lb": np.stack([gtable(x) for x in b])}
def setup_inputs(rng):
    lf, iv, kids, idx, inv = places(rng, *classes(rng, "plain"), (1, 2, 3, 4))
    v = nodes(rng, inv, 0.2); b = rng.integers(0, NB, (N, 8, L))
    bk = buckets(rng, inv, idx, v, b, wish(rng, [0.25, 0.5, 0.75, 0.97], [1, 2, 2, 3]), rng.integers(0, V, (N, 8, 16, NB)), 3)
    return pack(lf, iv, kids, bk, v, b)
def setup_inputs_spread(rng):
    lf, iv, kids, idx, inv = places(rng, *classes(rng, "spread"), (1, 2, 3, 4))
    v = nodes(rng, inv, 0.2); b = (NB * rng.random((N, 8, L)) ** 2).astype(np.int64)
    bk = buckets(rng, inv, idx, v, b, wish(rng, [0.1, 0.6, 0.9, 1.0], [1, 2, 2, 3]), (V * rng.random((N, 8, 16, NB)) ** 3).astype(np.int64), 3)
    return pack(lf, iv, kids, bk, v, b)
def setup_inputs_alike(rng):
    lf, iv, kids, idx, inv = places(rng, *classes(rng, "alike"), (1, 2, 3, 4))
    v = nodes(rng, inv, 0.2); b = rng.integers(0, NB, (N, 8, L)); want = wish(rng, [0.3, 0.6, 0.9], [1, 2, 2, 3]); n4 = L // 4
    v[..., 1::4] = np.take_along_axis(inv, 64 + np.arange(N)[:, None, None] + 2 * CN * rng.integers(0, V // CN // 2, (N, 8, n4)), 2); want[..., 1::4] = 0
    bk = buckets(rng, inv, idx, v, b, want, rng.integers(0, V, (N, 8, 16, NB)), 3)
    for r in range(N):
        for g in range(8):
            when = rng.integers(0, T, n4); how = rng.integers(1, 5, n4)
            for t in range(T):
                q, h = (r + t) % N, (g + t * (t + 1) // 2) % 8; on = np.flatnonzero(when == t)
                code = 64 + r + 2 * CN * rng.integers(0, V // CN // 2, (16, len(on))); code[:15] += 8 * how[on]
                bk[q, h][:, b[r, g, 1::4][on]] = inv[q, h][code]
    return pack(lf, iv, kids, bk, v, b)
def setup_inputs_corners(rng):
    lf, iv, kids, idx, inv = places(rng, *classes(rng, "plain"), (1,))
    v = nodes(rng, inv, 0.0); b = np.argsort(rng.random((N, 8, NB)), axis=-1)[..., :L]; want = np.zeros((N, 8, T, L), np.int64)
    counts = (0, 1, CAP - 1, CAP, CAP + 1, L)
    for r in range(N):
        full = (5 * r + 2) % 8
        for g in range(8):
            e = 7 * r + g - int(g > full)
            ts = e % T
            for t in range(T):
                n = counts[int(rng.integers(0, 6))]
                if t == ts: n = counts[(e // T + 2 * ts) % 6]
                want[r, g, t, rng.permutation(L)[:n]] = 1 if t < ts else 2
            if g == full:
                c = r + 8 * rng.integers(4, CN // 8, L); v[r, g] = inv[r, g][2 * CN * rng.integers(0, V // CN // 2, L) + c]
                want[r, g] = 2; want[r, g][:T - 1, rng.permutation(L)[:r % 4]] = 0
    return pack(lf, iv, kids, buckets(rng, inv, idx, v, b, want, cold(rng, inv), 3), v, b)
def setup_inputs_crowd(rng):
    lf, iv, kids, idx, inv = places(rng, *classes(rng, "plain"), (1,))
    v = nodes(rng, inv, 0.0); b = np.argsort(rng.random((N, 8, NB)), axis=-1)[..., :L].copy(); want = np.zeros((N, 8, T, L), np.int64)
    for r in range(N):
        for g in range(8):
            if g % 4 == 3:
                i = rng.integers(0, 3, L); v[r, g] = v[r, g, :3][i]; b[r, g] = b[r, g, :3][i]; want[r, g] = rng.integers(0, 3, (T, 3))[:, i]
                continue
            x = (r + g // 2) % T; v0, v1, b0 = int(v[r, g, 0]), int(v[r, g, 1]), int(b[r, g, 0]); e = int(rng.integers(0, L))
            v[r, g] = v0; b[r, g] = b0; want[r, g, :x] = 1; want[r, g, x:] = 2
            if g % 2 == 1: v[r, g, e] = v1; b[r, g, e] = (b0 + 1) % NB; want[r, g, :, e] = 0
    return pack(lf, iv, kids, buckets(rng, inv, idx, v, b, want, cold(rng, inv), 3), v, b)
def setup_inputs_ends(rng):
    lf, iv, kids, idx, inv = places(rng, *classes(rng, "ends"), (1, 2, 3), True)
    u = rng.random((N, 8, L)); v = np.where(u < 0.35, 0, np.where(u < 0.7, V - 1, nodes(rng, inv, 0.2)))
    u = rng.random((N, 8, L)); b = np.where(u < 0.35, 0, np.where(u < 0.7, NB - 1, rng.integers(0, NB, (N, 8, L))))
    v[..., 0] = 0; b[..., 0] = 0; v[..., L - 1] = V - 1; b[..., L - 1] = NB - 1
    base = (V - 1) * np.where(rng.random((N, 8, 1, NB)) < 0.25, rng.integers(0, 2, (N, 8, 16, NB)), rng.integers(0, 2, (N, 8, 1, NB)))
    bk = buckets(rng, inv, idx, v, b, wish(rng, [0.4, 0.7], [1, 2, 2]), base, 1)
    bk[:, :, :15, 0] = V - 1; bk[:, :, 15, 0] = 0; bk[:, :, :15, NB - 1] = 0; bk[:, :, 15, NB - 1] = V - 1
    return pack(lf, iv, kids, bk, v, b)
def check_inputs(d):
    bad = []
    for k, lo, hi in (("lf", -7, 7), ("iv", 0, 7), ("kd", 0, NL - 1), ("bk", 0, V - 1), ("lv", 0, V - 1), ("lb", 0, NB - 1)):
        x = np.asarray(d[k]).astype(np.float64)
        if not (np.min(x) >= lo and np.max(x) <= hi): bad.append("range of " + k)
        if np.any(x != np.floor(x)): bad.append("whole numbers of " + k)
    return bad
def codes(x, base):
    return np.matmul(np.swapaxes(x, -1, -2), base ** (D[:, None] ^ D[None, :]))
def reference(lf, iv, kd, bk, lv, lb):
    x = lf.astype(np.float32).astype(np.int64).reshape(N, 8, 16, NL); inv = iv.astype(np.float32).astype(np.int64).reshape(N, 8, 16, V)
    kids = kd.astype(np.int64).reshape(N, 8, 16, V); slots = bk.astype(np.int64).reshape(N, 8, 16, NB)
    v = np.stack([gentries(e) for e in lv]).astype(np.int64); b = np.stack([gentries(e) for e in lb]).astype(np.int64)
    node = codes(inv, 8)
    leaf = np.stack([codes(7 + x, 15), codes(7 - x, 15)], axis=-1)
    live = np.ones((N, 8, L), bool); out = np.zeros((N, 8, 5, L), np.int64); out[:, :, 0] = -1
    for t in range(T):
        for r in range(N):
            for g in range(8):
                q, h = (r + t) % N, (g + t * (t + 1) // 2) % 8; vv = v[r, g]
                w = slots[q, h][:, b[r, g]].T
                hit = (node[q, h][w] == node[r, g][vv, 0][:, None, None]).reshape(L, 256) & live[r, g][:, None]
                lanes = np.flatnonzero(np.any(hit, axis=1))[:CAP]
                first = np.argmax(hit[lanes], axis=1); w = w[lanes, first >> 4]; M = first & 15
                A = leaf[r, g][kids[r, g][:, vv[lanes]], 0, 0]
                B = leaf[q, h][kids[q, h][D[:, None] ^ M[None, :], w[None, :]]]
                same = np.all(B == A[:, :, None, None], axis=0).reshape(len(lanes), 32)
                won = np.any(same, axis=1); s = np.argmax(same, axis=1)[won]; j = lanes[won]
                out[r, g][:, j] = np.stack([np.full(len(j), q), w[won], M[won], s >> 1, 1 - 2 * (s & 1)])
                live[r, g, j] = False
    return {"y": out.reshape(N, 40, L).astype(np.float32)}

@@ -1,0 +1,606 @@
+import numpy as np
+from concourse.mybir import AluOpType, AxisListType, ActivationFunctionType
+from concourse.bass import DstId, RemoteDMATransfer
+
+A = AluOpType
+F = ActivationFunctionType
+N, NT, PW, WIN, CH = 8, 4, 684, 1120, 1024
+SHIFT = [0, 1, 3, 6]
+MAGIC = 12582912.0
+
+_B = {}
+for _d, _l in (
+    ("bfloat16", dict(lf=2048, ivs=1024, bdw=256, ident=128, i16=128, i256=128, i64k=128, ni256=128, hw=256, nhw=256,
+                      sc0=128, sc1=(32, 4), sc2=(16, 8), sc3=(8, 16), f0=128, f1=128, f2=128, f3=128, n3=(8, 16), w8=(8, 16), w8s=(8, 16),
+                      w8x=(8, 16), wd=64, wp=64, ones=256, cneg=64, tneg=256, wn1=256, wn2=256, e2=144, pm=136, tt=128, nu=128, nui=128,
+                      t2k=128, e1=256, e1m=256, e3=256, ez=144, xx=(2, 128), yy=(2, 128), ww=(2, 128), l1=128, l2=128, rp=(8, 16), rm=(8, 16),
+                      ni1=128, ni64k=128, ll=16, sel=(5, 40),
+                      dt3=(64, 16), ct=1024, req=256, rq=(3, 256), tb=(4, 2048), ga=(2, 4096), ta=1536, tc=1536, sq=512, fit=256,
+                      iw=256, sg=256, fitm=256, ohm=256, chi=256, ned=1152, nee=1152, rr=192, fpm=384, oh=384, rw=(8, 16), rs2=208,
+                      zm=(4, 256), nbd=128, m512=128, mneg=128)),
+    ("float32", dict(cc=256, gc=256, ln=256, pn=16, pf=12, col=40, oh16=16, q4=4, e8=8, rs=512, pm1=512, dl=512, pm2=512, ck=(64, 2),
+                     h32=256, pr=256, xs=1152, res=208, cres=192, kx=256, ysb=256)),
+    ("float16", dict(pk=PW, pl=(3, PW), y1=PW, y2=PW, wh=(4, 256), val=256, kw=256, rt=(4, 128), ka8=256, kb=256, cz=256, d0=256,
+                     zin=(6, 256), zo=(4, 256), zs=256)),
+    ("int32", dict(kds=1024, bks=1024, lvi=16, lbi=64, pi=12, sw=WIN, bi=192)),
+    ("uint16", dict(lvu=16, lbu=64, lbr=(3, 16), wu=(4, 256), wl=16, kr=(4, 384), kl=(3, 384), off=(4, 16), ofc=(4, 16), ab=384)),
+):
+    for _k, _s in _l.items():
+        _B["lfs" if _k == "lf" else _k] = ("sbuf", [128] + (list(_s) if isinstance(_s, tuple) else [_s]), _d)
+MATS = [k for k, v in _B.items() if v[1:] == ([128, 128], "bfloat16")]
+TWICE = ("sq", "fit", "val", "wl", "iw", "kw", "sg", "fitm", "ohm", "chi", "pr", "y1", "y2")
+LAST = ()
+for _k in TWICE + LAST:
+    _B[_k] = ("sbuf", [128, 2, _B[_k][1][1]], _B[_k][2])
+for _k in MATS:
+    del _B[_k]
+_B["mats"] = ("sbuf", [128, len(MATS), 128], "bfloat16")
+for _k in range(8):
+    _B["p%d" % _k] = ("psum", [128, 512], "float32")
+SCRATCH = _B
+SEMAPHORES = (["v", "s", "t", "p", "snt", "st"] + ["ld%d" % i for i in range(12)] +
+              [x + str(t) for x in ("lb", "rq", "pk", "kr") for t in (1, 2, 3)])
+
+CY, PC, LAT, GC = 1.04, 0.55, 120.0, 1.56
+SCT, TRIES, CUT, CUT3 = 3.8, 600, ((0, 64), (64, 96)), ((0, 80), (80, 160), (160, 192))
+VB = [1.0, 1.5, 2.0, 3.0]
+ORD, BONUS = (1, 1), {"c0": 18000.0, "c1": 12000.0, "c2": 12000.0, "c3": 12000.0}
+INFO = {}
+
+
+def rank_program(g, core, T, topo):
+    rank = T.rank_of(core)
+    if rank is None:
+        return
+    Q = {"v": g.vector, "s": g.scalar, "t": g.tensor, "p": g, "y": g.sync}
+    V, S, P = g.vector, g.scalar, g.tensor
+    ops, acc, par = [], {}, [0, 0, ""]
+
+    def R(name, *idx, part=slice(None)):
+        if name in TWICE:
+            idx = (par[0],) + idx
+        if name in LAST:
+            idx = (par[1],) + idx
+        if name in MATS:
+            name, idx = "mats", (MATS.index(name),) + idx
+        shape = SCRATCH[name][1][1:]
+        el = np.arange(int(np.prod(shape))).reshape(shape)[idx].ravel()
+        m = 0
+        if el[-1] - el[0] + 1 == len(el):
+            m = ((1 << len(el)) - 1) << int(el[0])
+        else:
+            for k in el.tolist():
+                m |= 1 << k
+        return dict(ap=T[name][(part,) + idx], b=name, m=m, n=len(el), w=2 if "16" in SCRATCH[name][2] else 4, off=None)
+
+    def C(name, a, b=None, s=None):
+        return R(name, slice(a, a + 1 if b is None else b, s))
+
+    def IX(win, off):
+        return dict(win, ap=win["ap"].indirect(off["ap"]), n=16 * off["n"], off=off)
+
+    def op(var, reads, writes, sem=None, after=(), tag=""):
+        i, deps = len(ops), {}
+        reads = [r for r in reads if isinstance(r, dict)]
+        reads = reads + [r["off"] for r in reads if r["off"]]
+        for x, wr in [(r, False) for r in reads] + [(w, True) for w in writes]:
+            l = acc.setdefault(x["b"], [])
+            if SCRATCH[x["b"]][0] == "psum":
+                for j, m, pw in l[::-1]:
+                    if j != i:
+                        deps[j] = deps.get(j, False) or pw or wr
+                        break
+                for j, m, pw in l[::-1]:
+                    if j != i and pw and not wr:
+                        deps[j] = True
+                        break
+            else:
+                for j, m, pw in l:
+                    if j != i and (pw or wr) and m & x["m"]:
+                        deps[j] = True
+                if wr:
+                    l[:] = [e for e in l if e[1] & ~x["m"]]
+            l.append((i, x["m"], wr))
+        for j in after:
+            deps[j] = True
+        ops.append(dict(ph=par[2], var=var, deps=deps, sem=sem, tag=tag or (writes[0]["b"] if writes else "")))
+        return i
+
+    def ap(x):
+        return x["ap"] if isinstance(x, dict) else x
+
+    def vc(o, i, m=1.0):
+        if i["off"]:
+            return 60 + GC * CY * i["n"]
+        return 30 + CY * max(64, m * i["n"] * (0.5 if m == 1.0 and o["w"] == 2 and i["w"] == 2 else 1.0))
+
+    def sc(i):
+        return 70 + CY * (GC * i["n"] if i["off"] else max(64, i["n"]))
+
+    def ts(o, i, a, b, op0, op1=None, act=None):
+        var = {"v": (vc(o, i), lambda: V.tensor_scalar(o["ap"], i["ap"], ap(a), ap(b), op0, op1) if op1 else
+                     V.tensor_scalar(o["ap"], i["ap"], ap(a), None, op0))}
+        if act:
+            var["s"] = (sc(i), lambda: S.activation(o["ap"], i["ap"], act[0], bias=ap(act[1]), scale=ap(act[2])))
+        return op(var, [i, a, b], [o])
+
+    def mul(o, i, a):
+        return ts(o, i, a, None, A.mult, act=(F.Copy, 0.0, a))
+
+    def cp(o, i, s=True):
+        var = {"v": (vc(o, i), lambda: V.tensor_copy(o["ap"], i["ap"]))}
+        if s:
+            var["s"] = (sc(i), lambda: S.activation(o["ap"], i["ap"], F.Identity))
+        return op(var, [i], [o])
+
+    def tt(o, a, b, alu):
+        ps = a["b"][0] == "p" and len(a["b"]) == 2 and a["b"][1].isdigit()
+        return op({"v": (vc(o, a, 1.001 if ps else 2.0), lambda: V.tensor_tensor(o["ap"], a["ap"], b["ap"], alu))}, [a, b], [o])
+
+    def scan(o, a, b, init, op0, op1):
+        return op({"v": (vc(o, b), lambda: V.tensor_tensor_scan(o["ap"], a["ap"], b["ap"], init, op0, op1))}, [a, b], [o])
+
+    def ms(o, c):
+        var = {"v": (vc(o, o), lambda: V.memset(o["ap"], c))}
+        if abs(c) <= 1:
+            var["p"] = (130 + 2 * CY * o["n"], lambda: g.iota(o["ap"], [[0, o["n"]]], int(c), 0, allow_small_or_imprecise_dtypes=True))
+        return op(var, [], [o])
+
+    def asel(o, i, cmp, fill):
+        return op({"p": (170 + 2 * CY * 128, lambda: g.affine_select(o["ap"], i["ap"], [[1, 128]], cmp, fill, 0, -1))}, [i], [o])
+
+    def mm(l):
+        return mmg([l])
+
+    def mmg(gs, start=True, stop=True):
+        def f():
+            for q in gs:
+                for k, (o, a, b) in enumerate(q):
+                    r = P.matmul(o["ap"], a["ap"], b["ap"], start and k == 0, stop and k == len(q) - 1)
+            return r
+        l = [x for q in gs for x in q]
+        c = 30 + sum(PC * max(64, b["n"]) * (4 if b["w"] == 4 else 1) for o, a, b in l)
+        return op({"t": (c, f)}, [x for o, a, b in l for x in (a, b)], [l[0][0]])
+
+    def iota(o, pat, base, cm):
+        fl = SCRATCH[o["b"]][2] != "int32"
+        return op({"p": (130 + 2 * CY * o["n"], lambda: g.iota(o["ap"], pat, base, cm, allow_small_or_imprecise_dtypes=True) if fl
+                         else g.iota(o["ap"], pat, base, cm))}, [], [o])
+
+    nld = [0]
+
+    def load(pairs, o, lat):
+        s = T.sem["ld%d" % nld[0]]
+        nld[0] += 1
+
+        def f():
+            for a, b in pairs:
+                g.sync.dma_start(a, b).then_inc(s, 16)
+        return op({"y": (60.0 * len(pairs), f)}, [], [o], sem=(s, 16 * len(pairs), lat))
+
+    sent = [0]
+
+    def peer(d):
+        return T.cores[(rank + d) % N]
+
+    def emask(d, a, b):
+        return sum(1 << e for e in topo.engines(core, peer(d))[a:b])
+
+    def send(src, trs, lat):
+        def f():
+            l = []
+            for d, s, dst, sem, a, b in trs:
+                rid, pid = topo.addr(peer(d), core)
+                l.append(RemoteDMATransfer(dst_ids=[DstId(rid=rid, pnc=pid)], dma_engine_mask=emask(d, a, b), remote_sem=T.sem[sem],
+                                           srcs=[s["ap"]], dsts=[dst["ap"]]))
+            g.remote_dma_fused(l, local_sem=T.sem.snt)
+        i = op({"p": (500.0, f)}, src, [], tag="send")
+        for d, s, dst, sem, a, b in trs:
+            sent[0] += b - a
+            op({"n": (0.0, None)}, [], [dst], sem=(T.sem[sem], b - a, lat), after=[i], tag="arr")
+
+    load([(T.ivs[:], T.iv[:])], R("ivs"), 3000)
+    load([(T.lvi[:], T.lv[:])], R("lvi"), 2500)
+    lb = [(T.lbi[:, 0:16], T.lb[:])]
+    for t in (1, 2, 3):
+        s = 16 * SHIFT[t]
+        lb += [(T.lbi[s:128, 16 * t:16 * t + 16], T.lb[0:128 - s, :]), (T.lbi[0:s, 16 * t:16 * t + 16], T.lb[128 - s:128, :])]
+    load([(T.lfs[:], T.lf[:])], R("lfs"), 4500)
+    load(lb, R("lbi"), 4500)
+    load([(T.bks[:], T.bk[:])], R("bks"), 6000)
+    load([(T.kds[:], T.kd[:])], R("kds"), 7500)
+
+    iota(C("pi", 0), [[0, 1]], 0, 1)
+    iota(R("gc"), [[0, 2], [1, 8], [0, 16]], 0, 0)
+    iota(R("cc"), [[0, 2], [1, 128]], 0, 0)
+    for k, (sh, m) in enumerate([(0, 1), (1, 1), (2, 1), (3, 1), (4, 7), (0, 15), (1, 7), (2, 3), (1, 63)]):
+        ts(C("pi", k + 1), C("pi", 0), sh, m, A.arith_shift_right, A.bitwise_and)
+    cp(C("pf", 0, 10), C("pi", 0, 10), s=False)
+    p_, pg, p16, p8, p4 = C("pf", 0), C("pf", 5), C("pf", 6), C("pf", 7), C("pf", 8)
+    ms(R("sc0"), 1.0), ms(C("sc0", 1, 128, 2), -1.0)
+    for b in (1, 2, 3):
+        ms(R("sc%d" % b), 1.0), ms(R("sc%d" % b, slice(None), slice(1 << b, 2 << b)), -1.0)
+    sig = [R("sc%d" % b) for b in range(4)]
+    ts(C("col", 0, 4), C("pf", 1, 5), -2.0, 1.0, A.mult, A.add)
+    ts(C("col", 4, 8), C("pf", 1, 5), -1.0, 1.0, A.mult, A.add)
+    ts(R("bdw"), R("gc"), pg, None, A.is_equal)
+    bd, bdc = C("bdw", 0, 128), C("bdw", 0, 128, 16)
+    for b, v in enumerate((8.0, 64.0, 4096.0)):
+        ts(C("col", 8 + b), C("col", b), -(v - 1) / 2, None, A.mult)
+        ts(R("f%d" % b), sig[b], C("col", 8 + b), (v + 1) / 2, A.mult, A.add)
+    tt(R("f0"), R("f0"), R("f1"), A.mult), tt(R("f2"), R("f2"), bd, A.mult), tt(R("n3"), R("f0"), R("f2"), A.mult)
+    lo8, hi8, al = slice(0, 8), slice(8, 16), slice(None)
+    n8, b3, nb3 = R("n3", al, lo8), C("pf", 4), C("col", 7)
+    mul(R("w8", al, lo8), n8, nb3), mul(R("w8", al, hi8), n8, b3)
+    mul(R("w8s"), R("w8"), 2.0 ** 24), mul(R("wd"), n8, C("col", 3))
+    ms(R("ones"), 1.0), ms(R("cneg"), -2.0 ** 41)
+    op({"v": (100.0, lambda: V.tensor_reduce(T.col[:, 11:12], T.n3[:, :, 0], AxisListType.X, A.add))}, [R("n3")], [C("col", 11)])
+    ts(R("wp"), C("cc", 0, 64), C("pf", 9), C("col", 11), A.is_equal, A.mult)
+    ts(R("ident"), C("cc", 0, 128), p_, None, A.is_equal)
+    ms(R("rs"), 0.0), ms(C("rs", 0, 512, 8), 1e20)
+    ms(R("dt3", al, slice(3, 8, 4)), 0.0)
+    for b in range(4):
+        ts(R("f%d" % b), sig[b], C("pf", 1 + b), C("col", 4 + b), A.mult, A.add)
+    tt(R("f0"), R("f0"), R("f1"), A.mult), tt(R("f2"), R("f2"), R("f3"), A.mult), tt(R("f0"), R("f0"), R("f2"), A.mult)
+    tt(C("hw", 0, 128), R("f0"), bd, A.mult), cp(C("hw", 128, 256), C("hw", 0, 128))
+    hh = C("hw", 0, 128)
+    mul(R("nhw"), R("hw"), -1.0), mul(R("h32"), R("hw"), 0.0625)
+    for k, v in (("i16", 16.0), ("i256", 256.0), ("i64k", 65536.0), ("ni1", -1.0), ("ni256", -256.0), ("ni64k", -65536.0)):
+        mul(R(k), R("ident"), v)
+    ts(R("q4"), C("cc", 0, 4), p4, None, A.is_equal)
+    ts(R("oh16"), C("cc", 0, 16), p16, None, A.is_equal)
+    for k in (0, 1):
+        ts(C("tneg", k, 256, 2), C("bdw", k, 256, 2), C("q4", k), -1.0, A.mult, A.mult)
+    ts(R("wn1"), R("bdw"), C("q4", 2), -1.0, A.mult, A.mult), ts(R("wn2"), R("bdw"), C("q4", 3), -2.0, A.mult, A.mult)
+    ts(R("w8x", al, lo8), n8, b3, 2.0, A.mult, A.mult), ts(R("w8x", al, hi8), n8, nb3, 2.0, A.mult, A.mult)
+    ts(C("col", 12), pg, 16.0, 15.0, A.mult, A.add)
+    ts(C("col", 13), C("col", 12), p4, -1.0, A.add, A.add)
+    ts(C("col", 14), C("col", 12), p8, -7.0, A.add, A.add)
+    ts(C("col", 16), pg, 5.0, p16, A.mult, A.add)
+    ts(C("col", 16), C("col", 16), -8.0, None, A.add)
+    ms(C("e2", 128, 144), 0.0), ms(C("pm", 128, 136), 0.0)
+    ts(C("e2", 0, 128), C("cc", 0, 128), C("col", 13), nb3, A.is_equal, A.mult)
+    ts(C("pm", 0, 128), C("cc", 0, 128), C("col", 14), None, A.is_equal)
+    ts(R("e1"), R("cc"), C("col", 12), None, A.is_equal), mul(R("e1m"), R("e1"), p16)
+    mul(R("nbd"), bd, -1.0)
+    asel(R("nu"), R("nbd"), A.is_gt, 0.0), asel(R("nui"), R("nbd"), A.is_ge, 0.0), asel(R("tt"), R("nu"), A.not_equal, 1.0)
+    mul(R("t2k"), R("tt"), 2048.0)
+    ts(R("e8"), C("cc", 0, 8), p8, None, A.is_equal)
+    oh, e8, c128 = (lambda k: C("oh16", k)), (lambda k: C("e8", k)), C("cc", 0, 128)
+    iota(R("pn"), [[1, 16]], -8, 1)
+    for h in (0, 1):
+        ts(R("xx", h), c128, C("pn", 8 - 8 * h), e8(4 * h), A.is_equal, A.mult)
+        ts(R("yy", h), c128, C("pn", 15 - 8 * h), e8(4 * h + 1), A.is_equal, A.mult)
+    ts(R("ww", 0), c128, C("pn", 4), e8(2), A.is_equal, A.mult), mul(R("ww", 1), R("ident"), e8(2))
+    ms(R("e3"), 0.0)
+    for k in (13, 14, 15):
+        cp(C("e3", k, 256, 16), C("bdw", 0, 256, 16))
+    mul(R("f2"), hh, -256.0), mul(R("f3"), hh, 256.0)
+    tt(R("l1"), hh, R("f2"), A.max), tt(R("l2"), C("nhw", 0, 128), R("f3"), A.max)
+    ms(R("rp"), 0.0)
+    bd2 = C("bdw", 0, 128, 8)
+    mul(R("rw"), bd, -2048.0), mul(R("rw", al, slice(9, 11)), bd2, 2048.0), mul(R("rw", al, slice(11, 13)), bd2, 0.0)
+    ms(R("rm"), 0.0), mul(R("rp", al, 11), bdc, p16), mul(R("rm", al, 11), bdc, p16)
+    cp(R("rp", al, 12), bdc), mul(R("rm", al, 12), bdc, -1.0)
+    tt(C("col", 24), e8(0), e8(4), A.add)
+    ts(C("col", 17), C("col", 24), -4095.0, 4096.0, A.mult, A.add)
+    ts(C("col", 18), oh(2), oh(10), -1.0, A.add, A.mult)
+    ts(C("col", 25), oh(1), oh(9), 1023.0, A.add, A.mult)
+    ts(C("col", 26), C("col", 25), C("col", 24), -1.0, A.add, A.mult)
+    ts(C("col", 25), C("col", 25), 1.0, None, A.add)
+    ts(C("col", 27), oh(0), oh(1), None, A.subtract)
+    ms(C("ez", 128, 144), 0.0), mul(C("ez", 0, 128), C("e1", 0, 128), C("col", 27))
+    ts(R("ll"), C("cc", 0, 16), 16.0, p16, A.mult, A.add)
+    mul(R("d0"), R("ones"), oh(0))
+    ts(C("col", 30), oh(1), -1.0, None, A.mult)
+    ts(C("col", 28), oh(1), -767.0, -1.0, A.mult, A.add), ts(C("col", 28), oh(5), -1023.0, C("col", 28), A.mult, A.add)
+    ts(C("cres", 0, 96), C("cc", 0, 96), C("col", 30), C("col", 28), A.mult, A.add)
+    ts(C("col", 29), e8(2), -2048.0, oh(0), A.mult, A.subtract), ts(C("col", 29), oh(1), -256.0, C("col", 29), A.mult, A.add)
+    iota(R("ln"), [[1, 256]], 0, 0)
+    iota(C("sw", 0, 96), [[0, 96]], 0, 0), ms(C("res", 96, 112), 0.0), ms(C("rs2", 96, 112), 0.0)
+    ts(R("cz"), R("ln"), C("col", 30), C("col", 29), A.mult, A.add)
+    ts(C("col", 19), p16, 13.0, b3, A.is_lt, A.mult)
+    for t in range(NT + 1):
+        if t < NT:
+            ts(C("col", 32 + t), oh(8), -2.0 - float((rank + t) % N), C("col", 19), A.mult, A.add)
+        else:
+            ts(C("col", 32 + t), oh(8), -1.0, None, A.mult)
+        ts(R("sel", t), C("cc", 0, 40), C("col", 16), C("col", 32 + t), A.is_equal, A.mult)
+
+    cp(R("lbu"), R("lbi"), s=False), cp(R("lvu"), R("lvi"), s=False)
+    send([R("lbu")], [(t, C("lbu", 16 * t, 16 * t + 16), R("lbr", t - 1), "lb%d" % t, 2 * t, 2 * t + 2) for t in (1, 2, 3)], 4000)
+    for a, b, pb in ((0, 512, "p4"), (512, PW, "p5")):
+        e = min(b, 2048 - 2 * PW)
+        mm([(C(pb, 0, b - a), R("ident"), C("lfs", a, b)), (C(pb, 0, b - a), R("i16"), C("lfs", PW + a, PW + b)),
+            (C(pb, 0, e - a), R("i256"), C("lfs", 2 * PW + a, 2 * PW + e))])
+        cp(C("pk", a, b), C(pb, 0, b - a))
+    for t in (1, 2, 3):
+        send([R("pk")], [(-t, R("pk"), R("pl", t - 1), "pk%d" % t, 0, 4)], 3000 + 4000 * t)
+
+    ivc = [C("ivs", 128 * c, 128 * c + 128) for c in range(8)]
+    mmg([[(C("p0", 64 * c, 64 * c + 64), a, b) for a, b in ((ivc[c], R("w8s", al, lo8)), (C("ones", 0, 128), R("cneg")), (ivc[c], R("w8s", al, hi8)))]
+         for c in range(8)])
+    mmg([[(C("p2", 64 * c, 64 * c + 64), ivc[c], R("wd"))] for c in range(8)])
+    mmg([[(C("p1", 64 * c, 64 * c + 64), ivc[c], R("wp"))] for c in range(8)])
+    scan(R("pm1"), R("rs"), R("p0"), 0.0, A.add, A.min)
+    op({"s": (sc(R("p2")), lambda: S.activation(T.p2[:], T.p2[:], F.Abs))}, [R("p2")], [R("p2")])
+    for i in range(8):
+        tt(C("dl", i, 512, 8), C("p0", i, 512, 8), C("pm1", 7, 512, 8), A.subtract)
+    tt(R("dl"), R("p2"), R("dl"), A.add)
+    scan(R("pm2"), R("rs"), R("dl"), 0.0, A.add, A.min)
+    cp(R("dt3", al, hi8), R("p1"))
+    cp(R("ck", al, 0), C("pm1", 7, 512, 8)), cp(R("ck", al, 1), C("pm2", 7, 512, 8))
+    dg = [R("dt3", al, slice(j, 8, 4)) for j in range(3)]
+    cp(dg[0], R("ck"), s=False), tt(R("ck"), R("ck"), dg[0], A.subtract)
+    cp(dg[1], R("ck"), s=False), tt(dg[2], R("ck"), dg[1], A.subtract)
+    for h, pb in enumerate(("p0", "p2")):
+        mmg([[(C(pb, 128 * c, 128 * c + 128), R("dt3", slice(32 * h + 8 * c, 32 * h + 8 * c + 8)), R("ident"))] for c in range(4)])
+        cp(C("ct", 512 * h, 512 * h + 512), R(pb))
+    cp(R("req"), IX(R("ct"), R("lvu")))
+    for t in (1, 2, 3):
+        send([R("req")], [(t, R("req"), R("rq", t - 1), "rq%d" % t, 4, 8)], 2500 + 800 * t)
+
+    bank = [0]
+
+    def nextbank(first=4):
+        bank[0] ^= 1
+        return "p%d" % (first + bank[0])
+
+    def own_table():
+        for c in range(4):
+            pb = nextbank()
+            mm([(R(pb), hh, C("lfs", 512 * c, 512 * c + 512))])
+            cp(R("tb", 0, slice(512 * c, 512 * c + 512)), R(pb))
+
+    def unpack(t, first=4):
+        s = 16 * SHIFT[t]
+        par[0], par[2] = t % 2, "u%d" % t
+        h, nh, x = C("hw", s, s + 128), C("nhw", s, s + 128), R("pl", t - 1)
+        ts(R("y1"), x, 16 * MAGIC, 16 * MAGIC, A.add, A.subtract), ts(R("y2"), x, 256 * MAGIC, 256 * MAGIC, A.add, A.subtract)
+        for k, scale in enumerate((1.0, 0.0625, 1.0 / 256)):
+            for a, b in ((0, 342), (342, PW)):
+                e = min(b, 2048 - k * PW)
+                pb = nextbank(first)
+                o = C(pb, 0, e - a)
+                src = [R("pl", t - 1, slice(a, e)), C("y1", a, e), C("y2", a, e)]
+                mm([(o, h, src[k])] + ([(o, nh, src[k + 1])] if k < 2 else []))
+                mul(R("tb", t, slice(k * PW + a, k * PW + e)), o, scale)
+
+    def sums(pb, buf, a, b, ids):
+        w = 2 * (b - a)
+        mmg([[(C(pb, w * j, w * j + w), R(ids[d - 3 * j]), buf(16 * a + d, 16 * b, 8)) for d in range(3 * j, min(8, 3 * j + 3))]
+             for j in range(3)])
+        return C(pb, 0, 3 * w)
+
+    def claim(t):
+        s = 16 * SHIFT[t]
+        r, par[0], par[2] = (128 - s) % 128, t % 2, "c%d" % t
+        rq = (lambda a, b: C("req", a, b)) if t == 0 else (lambda a, b: R("rq", t - 1, slice(a, b)))
+        cp(R("wu", t), IX(R("bks"), C("lbu", 0, 16) if t == 0 else R("lbr", t - 1)), s=False)
+        ts(R("wh", t), R("wu", t), 1.0, None, A.mult)
+        for c in range(0, 4096, CH):
+            cp(R("ga", t % 2, slice(c, c + CH)), IX(R("ct"), R("wu", t, slice(c // 16, (c + CH) // 16))))
+        for h in range(4):
+            for u in (0, 1):
+                o = C("p0", 256 * u + 64 * h, 256 * u + 64 * h + 64)
+                mm([(o, C("tneg", r, r + 128), rq(64 * h, 64 * h + 64))] +
+                   [(o, C("e2", 14 - 2 * k, 142 - 2 * k), R("ga", t % 2, slice(1024 * h + 8 * u + k, 1024 * h + 1024, 16))) for k in range(8)])
+        ts(R("sq"), R("p0"), 0.0, None, A.not_equal, act=(F.Square, 0.0, 1.0))
+        a, b = C("p1", 0, 256), C("p1", 256, 512)
+        mm([(a, C("pm", 8, 136), C("sq", 0, 256)), (a, C("pm", 0, 128), C("sq", 256, 512))])
+        ts(R("fit"), a, 0.0, None, A.is_equal, act=(F.Relu, 1.0, -1.0))
+        mm([(b, R("t2k"), R("fit")), (b, R("ident"), R("wh", t))])
+        ts(R("val"), b, -2047.0, 0.0, A.add, A.max, act=(F.Relu, -2047.0, 1.0))
+        mm([(C("p1", 0, 16), C("e1", 15 - l, 143 - l), C("val", l, 256, 16)) for l in range(16)])
+        ts(R("wl"), C("p1", 0, 16), -1.0, 0.0, A.add, A.max)
+        cp(R("iw"), IX(R("ivs"), R("wl"))), cp(R("kw"), IX(R("kds"), R("wl")))
+        a, b = C("p2", 0, 256), C("p2", 256, 512)
+        mm([(a, R("w8"), R("iw")), (a, C("wn1", r, r + 128), rq(0, 256))])
+        mm([(b, R("w8x"), R("iw")), (b, C("wn2", r, r + 128), rq(0, 256))])
+        ts(R("sg"), a, 0.0, None, A.not_equal, act=(F.Sign, 0.0, 1.0))
+        tt(R("fitm"), b, R("sg"), A.is_equal)
+        c, d = C("p3", 0, 256), C("p3", 256, 512)
+        mm([(c, R("tt"), R("fitm"))])
+        mm([(a, hh, R("kw"))])
+        ts(R("ohm"), c, 0.0, None, A.max, act=(F.Relu, 0.0, 1.0))
+        mm([(d, hh, R("ohm"))])
+        cp(R("chi"), d)
+        tt(R("pr"), a, R("chi"), A.mult)
+        mm([(c, C("h32", s, s + 128), R("pr"))])
+        e = C("p2", 256, 384)
+        mm([(e, C(m, 15 - 8 * h - f + s, 143 - 8 * h - f + s), C(x, 128 * h, 128 * h + 128))
+            for h in (0, 1) for f, m, x in ((2, "e3", "val"), (3, "e1m", "ohm"))])
+        ts(R("kr", t, slice(256, 384)), e, C("col", 17), C("col", 18), A.min, A.add)
+        cp(R("kr", t, slice(0, 256)), c, s=False)
+        if t:
+            send([R("kr", t)], [(-t, R("kr", t), R("kl", t - 1), "kr%d" % t, 4 if t == 1 else 0, 8)], 4000)
+
+    def reply(t, pb):
+        kl = (lambda a, b: R("kr", 0, slice(a, b))) if t == 0 else (lambda a, b: R("kl", t - 1, slice(a, b)))
+        ts(R("rt", t), kl(256, 384), C("col", 25), C("col", 26), A.mult, A.add)
+        ts(R("kb"), kl(0, 256), 1.0, None, A.mult)
+        o = C(pb, 256, 512)
+        mm([(o, R("i256"), R("ka8")), (o, R("ident"), R("kb"))])
+        cp(R("kx"), o)
+
+    def state(z, pb, nxt, cur, old):
+        mmg([([(o, R("xx", h), R("rt", nxt))] if nxt is not None else []) + ([(o, R("yy", h), R("rt", cur))] if cur is not None else []) +
+             ([(o, R("ww", u), R("zo", old, slice(128 * h, 128 * h + 128))) for u in (0, 1)] if old is not None else [])
+             for h in (0, 1) for o in [C(pb, 128 * h, 128 * h + 128)]])
+        tt(R("zin", z), C(pb, 0, 256), R("cz"), A.max)
+
+    def places(t, z, pb, cap):
+        scan(R("zs"), R("d0"), z, 0.0, A.mult, A.add)
+        o = C(pb, 0, 16)
+        mm([(o, R("ident"), R("ll"))] + [(o, C("ez", 15 - l, 143 - l), C("zs", l, 256, 16)) for l in range(16)])
+        cp(R("off", t), o, s=False)
+        ts(R("ofc", t), R("off", t), float(cap), None, A.min)
+
+    def test(t, n, cut, pa, pb, pc, pd):
+        sw, kx, par[2] = IX(R("sw"), R("off", t)), R("kx"), "t%d" % t
+        ta, tc = ((lambda a, b, s=None: C("ta", a, b, s)), (lambda a, b, s=None: C("tc", a, b, s))) if n == 96 else (
+            (lambda a, b, s=None: R("ga", 0, slice(a, b, s))), (lambda a, b, s=None: R("ga", 1, slice(a, b, s))))
+        op({"v": (60 + SCT * CY * 256, lambda: V.tensor_copy(sw["ap"], kx["ap"]))}, [kx, R("off", t)], [R("sw")])
+        ts(C("ab", 0, n), C("sw", 0, n), 1.0 / 2048, -1023.5 / 2048, A.mult, A.add)
+        ts(C("bi", 0, n), C("sw", 0, n), 2047, None, A.bitwise_and)
+        cp(C("ab", n, 2 * n), C("bi", 0, n), s=False)
+        for a, b in cut:
+            cp(ta(16 * a, 16 * b), IX(R("tb", 0), C("ab", a, b)))
+            cp(tc(16 * a, 16 * b), IX(R("tb", t), C("ab", n + a, n + b)))
+        if t < NT - 1:
+            reply(t + 1, pd)
+        state(t + 1, pd, t + 1 if t + 1 < NT else None, t, t - 1 if 0 < t < NT - 1 else None)
+        for a, b in cut:
+            xs = C("xs", 6 * a, 6 * b)
+            cp(xs, sums(pa, ta, a, b, ("ident", "i256", "i64k")))
+            tt(C("ned", 6 * a, 6 * b), sums(pb, tc, a, b, ("ident", "i256", "i64k")), xs, A.not_equal)
+            tt(C("nee", 6 * a, 6 * b), sums(pc, tc, a, b, ("ni1", "ni256", "ni64k")), xs, A.not_equal)
+        for a, b in cut:
+            w = 2 * (b - a)
+            mm([(C(pd, a, b), R(m), C(x, 6 * a + w * j + h, 6 * a + w * j + w, 2))
+                for m, x in (("l1", "ned"), ("l2", "nee")) for j in range(3) for h in (0, 1)])
+        a, fp, fm, rr = C(pd, 0, n), C("fpm", 0, n), C("fpm", n, 2 * n), C("rr", 0, n)
+        ts(rr, a, 256 * MAGIC, 256 * MAGIC, A.add, A.subtract)
+        tt(fp, a, rr, A.is_equal)
+        ts(fm, rr, 1.0, None, A.is_lt, act=(F.Relu, 1.0, -1.0))
+        a = C(pb, 0, n)
+        mm([(a, R("rw"), fm), (a, R("rw"), fp)])
+        tt(C("res", 0, n), a, C("cres", 0, n), A.max)
+        tt(R("zo", t), IX(C("res", 0, n + 16), R("ofc", t)), R("zin", t + 1), A.min)
+        a, b = C(pa, 0, n), C(pa, n, 2 * n)
+        mmg([[(a, R("tt"), fp), (a, R("nu"), fm)], [(b, R("tt"), fm), (b, R("nui"), fp)]])
+        ts(C("oh", 0, 2 * n), C(pa, 0, 2 * n), 0.0, None, A.max, act=(F.Relu, 0.0, 1.0))
+        a = C(pd, 0, n)
+        mm([(a, R("rp"), C("oh", 0, n)), (a, R("rm"), C("oh", n, 2 * n))])
+        cp(C("rs2", 0, n), a)
+        cp(R("zm", t), IX(C("rs2", 0, n + 16), R("ofc", t)))
+        if t < NT - 1:
+            places(t + 1, R("zo", t), pc, 96)
+
+    ts(R("ka8"), IX(R("kds"), R("lvu")), 8.0, None, A.mult)
+    home = (96, CUT, "p4", "p5", "p6", "p7")
+    own_table()
+    if ORD[0] == 0:
+        unpack(1)
+    claim(0)
+    reply(0, "p7"), state(0, "p7", 0, None, None), places(0, R("zin", 0), "p6", 96)
+    claim(1)
+    if ORD[0] == 1:
+        unpack(1, 2)
+    test(0, *home)
+    claim(2)
+    if ORD[1] == 0:
+        unpack(2, 2)
+    test(1, *home)
+    claim(3)
+    if ORD[1] == 1:
+        unpack(2, 0)
+    unpack(3, 2)
+    test(2, *home)
+    test(3, *home)
+    o = R("p1", slice(0, 256), part=slice(0, 40))
+    mmg([[(o, R("sel", NT), R("ones"))] + [(o, R("sel", t), R(z, t)) for t in range(NT - 1) for z in ("zo", "zm")]], stop=False)
+    mmg([[(o, R("sel", NT - 1), R("zo", NT - 1))]], start=False, stop=False)
+    mmg([[(o, R("sel", NT - 1), R("zm", NT - 1))]], start=False)
+    ysb = R("ysb", part=slice(0, 40))
+    cp(ysb, o)
+    op({"y": (60.0, lambda: g.sync.dma_start(T.y[:], ysb["ap"]).then_inc(T.sem.st, 16))}, [ysb], [], sem=(T.sem.st, 16, 2000))
+
+    n = len(ops)
+    succ = [[] for _ in ops]
+    for i, o in enumerate(ops):
+        for j in o["deps"]:
+            succ[j].append(i)
+    cost = [{e: c for e, (c, f) in o["var"].items()} for o in ops]
+    lat = [o["sem"][2] if o["sem"] else LAT for o in ops]
+
+    pred = [list(o["deps"]) for o in ops]
+
+    def place(key, back, vbias):
+        before, behind = (succ, pred) if back else (pred, succ)
+        left = [len(x) for x in before]
+        ready = [i for i in range(n) if not left[i]]
+        busy, eng, start, fin = {e: [] for e in "vstpyn"}, [""] * n, [0.0] * n, [0.0] * n
+        while ready:
+            i = min(ready, key=lambda k: key[k])
+            ready.remove(i)
+            best = None
+            for e, c in cost[i].items():
+                t = 0.0
+                for j in before[i]:
+                    a, b = (i, j) if back else (j, i)
+                    hard = ops[a]["sem"] or eng[j] != e or (ops[b]["deps"][a] and e != "t")
+                    t = max(t, fin[j] + (lat[a] if hard else 0.0))
+                k = 0
+                for k, (s0, s1) in enumerate(busy[e] + [(1e18, 1e18)]):
+                    if t + c <= s0:
+                        break
+                    t = max(t, s1)
+                if best is None or t + c * (vbias if e == "v" else 1.0) < best[0]:
+                    best = (t + c * (vbias if e == "v" else 1.0), e, t, k)
+            x, e, t, k = best
+            busy[e].insert(k, (t, t + cost[i][e]))
+            eng[i], start[i], fin[i] = e, t, t + cost[i][e]
+            for j in behind[i]:
+                left[j] -= 1
+                if not left[j]:
+                    ready.append(j)
+        return max(fin), eng, start, fin
+
+    if "plan" not in INFO:
+        rs, plan = np.random.RandomState(1), None
+        prio = [0.0] * n
+        for i in range(n - 1, -1, -1):
+            prio[i] = min(cost[i].values()) + lat[i] + max([prio[j] for j in succ[i]] + [0.0])
+        key = [-x - BONUS.get(o["ph"], 0.0) for x, o in zip(prio, ops)]
+        INFO["g"] = (prio, succ, [o["tag"] for o in ops])
+        for k in range(TRIES):
+            vb = float(rs.choice(VB))
+            r = place(key, False, vb)
+            if plan is None or r[0] < plan[0]:
+                plan = r
+            if k % 3 == 0:
+                sh = rs.randn(40) * float(rs.choice([0, 1000, 3000])) * (rs.rand(40) < 0.3)
+                key = list(rs.rand(n) * float(rs.choice([100, 300, 1000])) + np.array(plan[2]) + sh[np.arange(n) * 40 // n])
+            else:
+                b = place([-x for x in r[3]], True, vb)
+                key = list(-np.array(b[3]))
+        INFO["plan"] = (plan[0], plan[1], sorted(((i, plan[2][i]) for i in range(n)), key=lambda x: (x[1], x[0])))
+    end, eng, order = INFO["plan"]
+    INFO["order"] = [(st, eng[i], ops[i]["tag"], cost[i][eng[i]]) for i, st in order]
+
+    pos, seen, waits, need = {}, {}, [], set()
+    for k, (i, st) in enumerate(order):
+        pos[i] = k
+        e, w = eng[i], {}
+        if e != "n":
+            for j, raw in ops[i]["deps"].items():
+                if ops[j]["sem"]:
+                    if (e, j) not in seen:
+                        seen[(e, j)] = 1
+                        w[("sem", j)] = j
+                elif (eng[j] != e or (raw and e != "t")) and pos[j] > seen.get((e, eng[j]), -1):
+                    if ("q", eng[j]) not in w or pos[w[("q", eng[j])]] < pos[j]:
+                        w[("q", eng[j])] = j
+            for (kind, x), j in w.items():
+                if kind == "q":
+                    seen[(e, x)] = pos[j]
+                    need.add(j)
+        waits.append(w)
+    count, cnt = {}, dict.fromkeys("vstp", 0)
+    for (i, st), w in zip(order, waits):
+        e = eng[i]
+        if e == "n":
+            continue
+        for (kind, x), j in w.items():
+            if kind == "q":
+                Q[e].wait_ge(T.sem[x], count[j])
+            else:
+                Q[e].wait_ge(ops[j]["sem"][0], ops[j]["sem"][1])
+        r = ops[i]["var"][e][1]()
+        if i in need:
+            cnt[e] += 1
+            count[i] = cnt[e]
+            r.then_inc(T.sem[e], 1)
+    g.wait_ge(T.sem.snt, sent[0])
+    g.sync.wait_ge(T.sem.st, 16)

@@ -13,7 +13,7 @@ for _d, _l in (
     ("bfloat16", dict(lf=2048, ivs=1024, bdw=256, ident=128, i16=128, i256=128, i64k=128, ni256=128, hw=256, nhw=256,
                       sc0=128, sc1=(32, 4), sc2=(16, 8), sc3=(8, 16), f0=128, f1=128, f2=128, f3=128, n3=(8, 16), w8=(8, 16), w8s=(8, 16),
                       w8x=(8, 16), wd=64, wp=64, ones=256, cneg=64, tneg=256, wn1=256, wn2=256, e2=144, pm=136, tt=128, nu=128, nui=128,
-                      t2k=128, e1=256, e1m=256, e3=256, ez=144, xx=(2, 128), yy=(2, 128), ww=(2, 128), l1=128, l2=128, rp=(8, 16), rm=(8, 16),
+                      t2k=128, e1=256, e1m=256, e3=256, ez=144, xx=(2, 8, 16), yy=(2, 8, 16), ww=(8, 16), l1=128, l2=128, rp=(8, 16), rm=(8, 16),
                       ni1=128, ni64k=128, ll=16, sel=(5, 40),
                       dt3=(64, 16), ct=1024, req=256, rq=(3, 256), tb=(4, 2048), ga=(2, 4096), ta=1536, tc=1536, sq=512, fit=256,
                       iw=256, sg=256, fitm=256, ohm=256, chi=256, ned=1152, nee=1152, rr=192, fpm=384, oh=384, rw=(8, 16), rs2=208,
@@ -29,7 +29,7 @@ for _d, _l in (
         _B["lfs" if _k == "lf" else _k] = ("sbuf", [128] + (list(_s) if isinstance(_s, tuple) else [_s]), _d)
 MATS = [k for k, v in _B.items() if v[1:] == ([128, 128], "bfloat16")]
 TWICE = ("sq", "fit", "val", "wl", "iw", "kw", "sg", "fitm", "ohm", "chi", "pr", "y1", "y2")
-LAST = ()
+LAST = ("kb", "kx")
 for _k in TWICE + LAST:
     _B[_k] = ("sbuf", [128, 2, _B[_k][1][1]], _B[_k][2])
 for _k in MATS:
@@ -41,10 +41,10 @@ SCRATCH = _B
 SEMAPHORES = (["v", "s", "t", "p", "snt", "st"] + ["ld%d" % i for i in range(12)] +
               [x + str(t) for x in ("lb", "rq", "pk", "kr") for t in (1, 2, 3)])
 
-CY, PC, LAT, GC = 1.04, 0.55, 120.0, 1.56
+CY, PC, LAT, GC = 0.9, 0.45, 150.0, 1.56
 SCT, TRIES, CUT, CUT3 = 3.8, 600, ((0, 64), (64, 96)), ((0, 80), (80, 160), (160, 192))
 VB = [1.0, 1.5, 2.0, 3.0]
-ORD, BONUS = (1, 1), {"c0": 18000.0, "c1": 12000.0, "c2": 12000.0, "c3": 12000.0}
+ORD, BONUS = (1, 1), {}
 INFO = {}
 
 
@@ -146,8 +146,15 @@ def rank_program(g, core, T, topo):
             var["p"] = (130 + 2 * CY * o["n"], lambda: g.iota(o["ap"], [[0, o["n"]]], int(c), 0, allow_small_or_imprecise_dtypes=True))
         return op(var, [], [o])
 
-    def asel(o, i, cmp, fill):
-        return op({"p": (170 + 2 * CY * 128, lambda: g.affine_select(o["ap"], i["ap"], [[1, 128]], cmp, fill, 0, -1))}, [i], [o])
+    def asel(o, i, cmp, fill, pat=((1, 128),), base=0, cm=-1):
+        return op({"p": (170 + 2 * CY * o["n"], lambda: g.affine_select(o["ap"], i["ap"], [list(x) for x in pat], cmp, fill, base, cm))}, [i], [o])
+
+    def zero(o, c=0):
+        return iota(o, [[0, o["n"]]], c, 0)
+
+    def band(o, i, pat, lo, hi):
+        asel(o, i, A.is_ge, 0.0, pat, -lo, 1)
+        return asel(o, o, A.is_ge, 0.0, [[-a, b] for a, b in pat], hi, -1)
 
     def mm(l):
         return mmg([l])
@@ -212,7 +219,7 @@ def rank_program(g, core, T, topo):
 
     iota(C("pi", 0), [[0, 1]], 0, 1)
     iota(R("gc"), [[0, 2], [1, 8], [0, 16]], 0, 0)
-    iota(R("cc"), [[0, 2], [1, 128]], 0, 0)
+    iota(C("cc", 0, 128), [[1, 128]], 0, 0)
     for k, (sh, m) in enumerate([(0, 1), (1, 1), (2, 1), (3, 1), (4, 7), (0, 15), (1, 7), (2, 3), (1, 63)]):
         ts(C("pi", k + 1), C("pi", 0), sh, m, A.arith_shift_right, A.bitwise_and)
     cp(C("pf", 0, 10), C("pi", 0, 10), s=False)
@@ -253,34 +260,32 @@ def rank_program(g, core, T, topo):
         ts(C("tneg", k, 256, 2), C("bdw", k, 256, 2), C("q4", k), -1.0, A.mult, A.mult)
     ts(R("wn1"), R("bdw"), C("q4", 2), -1.0, A.mult, A.mult), ts(R("wn2"), R("bdw"), C("q4", 3), -2.0, A.mult, A.mult)
     ts(R("w8x", al, lo8), n8, b3, 2.0, A.mult, A.mult), ts(R("w8x", al, hi8), n8, nb3, 2.0, A.mult, A.mult)
-    ts(C("col", 12), pg, 16.0, 15.0, A.mult, A.add)
-    ts(C("col", 13), C("col", 12), p4, -1.0, A.add, A.add)
-    ts(C("col", 14), C("col", 12), p8, -7.0, A.add, A.add)
-    ts(C("col", 16), pg, 5.0, p16, A.mult, A.add)
-    ts(C("col", 16), C("col", 16), -8.0, None, A.add)
-    ms(C("e2", 128, 144), 0.0), ms(C("pm", 128, 136), 0.0)
-    ts(C("e2", 0, 128), C("cc", 0, 128), C("col", 13), nb3, A.is_equal, A.mult)
+    ts(C("col", 12), pg, 16.0, 8.0, A.mult, A.add)
+    ts(C("col", 14), C("col", 12), p8, None, A.add)
+    zero(R("e2")), ms(C("pm", 128, 136), 0.0), zero(R("e1")), zero(R("e1m"))
+    mul(C("e2", 14, 128, 16), bdc, C("q4", 0)), mul(C("e2", 15, 128, 16), bdc, C("q4", 1))
     ts(C("pm", 0, 128), C("cc", 0, 128), C("col", 14), None, A.is_equal)
-    ts(R("e1"), R("cc"), C("col", 12), None, A.is_equal), mul(R("e1m"), R("e1"), p16)
+    cp(C("e1", 15, 256, 16), C("bdw", 0, 256, 16)), mul(C("e1m", 15, 256, 16), C("bdw", 0, 256, 16), p16)
     mul(R("nbd"), bd, -1.0)
     asel(R("nu"), R("nbd"), A.is_gt, 0.0), asel(R("nui"), R("nbd"), A.is_ge, 0.0), asel(R("tt"), R("nu"), A.not_equal, 1.0)
     mul(R("t2k"), R("tt"), 2048.0)
     ts(R("e8"), C("cc", 0, 8), p8, None, A.is_equal)
     oh, e8, c128 = (lambda k: C("oh16", k)), (lambda k: C("e8", k)), C("cc", 0, 128)
-    iota(R("pn"), [[1, 16]], -8, 1)
+    two, o16 = [[-16, 8], [-1, 2]], C("ones", 0, 16)
+    zero(R("xx")), zero(R("yy")), zero(R("ww"))
     for h in (0, 1):
-        ts(R("xx", h), c128, C("pn", 8 - 8 * h), e8(4 * h), A.is_equal, A.mult)
-        ts(R("yy", h), c128, C("pn", 15 - 8 * h), e8(4 * h + 1), A.is_equal, A.mult)
-    ts(R("ww", 0), c128, C("pn", 4), e8(2), A.is_equal, A.mult), mul(R("ww", 1), R("ident"), e8(2))
-    ms(R("e3"), 0.0)
+        asel(R("xx", h, al, slice(0, 2)), o16, A.is_equal, 0.0, two, -8 * h, 1)
+        asel(R("yy", h, al, slice(9, 11)), o16, A.is_equal, 0.0, two, -8 * h - 2, 1)
+        asel(R("ww", al, slice(4 * h, 4 * h + 2)), o16, A.is_equal, 0.0, two, -4, 1)
+    zero(R("e3"))
     for k in (13, 14, 15):
         cp(C("e3", k, 256, 16), C("bdw", 0, 256, 16))
-    mul(R("f2"), hh, -256.0), mul(R("f3"), hh, 256.0)
-    tt(R("l1"), hh, R("f2"), A.max), tt(R("l2"), C("nhw", 0, 128), R("f3"), A.max)
-    ms(R("rp"), 0.0)
+    for k, v in (("l1", -127.5), ("l2", 127.5)):
+        ts(R(k), R("f0"), v, 128.5, A.mult, A.add), band(R(k), R(k), [[-16, 8], [0, 16]], 0, 15)
+    zero(R("rp"))
     bd2 = C("bdw", 0, 128, 8)
     mul(R("rw"), bd, -2048.0), mul(R("rw", al, slice(9, 11)), bd2, 2048.0), mul(R("rw", al, slice(11, 13)), bd2, 0.0)
-    ms(R("rm"), 0.0), mul(R("rp", al, 11), bdc, p16), mul(R("rm", al, 11), bdc, p16)
+    zero(R("rm")), mul(R("rp", al, 11), bdc, p16), mul(R("rm", al, 11), bdc, p16)
     cp(R("rp", al, 12), bdc), mul(R("rm", al, 12), bdc, -1.0)
     tt(C("col", 24), e8(0), e8(4), A.add)
     ts(C("col", 17), C("col", 24), -4095.0, 4096.0, A.mult, A.add)
@@ -288,8 +293,9 @@ def rank_program(g, core, T, topo):
     ts(C("col", 25), oh(1), oh(9), 1023.0, A.add, A.mult)
     ts(C("col", 26), C("col", 25), C("col", 24), -1.0, A.add, A.mult)
     ts(C("col", 25), C("col", 25), 1.0, None, A.add)
-    ts(C("col", 27), oh(0), oh(1), None, A.subtract)
-    ms(C("ez", 128, 144), 0.0), mul(C("ez", 0, 128), C("e1", 0, 128), C("col", 27))
+    zero(R("ez"))
+    ez = C("ez", 15, 128, 16)
+    asel(ez, C("ones", 0, 8), A.is_equal, 0.0, [[-16, 8]], 0, 1), asel(ez, ez, A.not_equal, -1.0, [[-16, 8]], -1, 1)
     ts(R("ll"), C("cc", 0, 16), 16.0, p16, A.mult, A.add)
     mul(R("d0"), R("ones"), oh(0))
     ts(C("col", 30), oh(1), -1.0, None, A.mult)
@@ -299,13 +305,9 @@ def rank_program(g, core, T, topo):
     iota(R("ln"), [[1, 256]], 0, 0)
     iota(C("sw", 0, 96), [[0, 96]], 0, 0), ms(C("res", 96, 112), 0.0), ms(C("rs2", 96, 112), 0.0)
     ts(R("cz"), R("ln"), C("col", 30), C("col", 29), A.mult, A.add)
-    ts(C("col", 19), p16, 13.0, b3, A.is_lt, A.mult)
     for t in range(NT + 1):
-        if t < NT:
-            ts(C("col", 32 + t), oh(8), -2.0 - float((rank + t) % N), C("col", 19), A.mult, A.add)
-        else:
-            ts(C("col", 32 + t), oh(8), -1.0, None, A.mult)
-        ts(R("sel", t), C("cc", 0, 40), C("col", 16), C("col", 32 + t), A.is_equal, A.mult)
+        zero(R("sel", t), int(t < NT)), zero(R("sel", t, slice(0, 40, 5)), -1 - (rank + t) % N if t < NT else -1)
+        asel(R("sel", t), R("sel", t), A.is_equal, 0.0, [[-16, 8], [-1, 5]], -8, 1)
 
     cp(R("lbu"), R("lbi"), s=False), cp(R("lvu"), R("lvi"), s=False)
     send([R("lbu")], [(t, C("lbu", 16 * t, 16 * t + 16), R("lbr", t - 1), "lb%d" % t, 2 * t, 2 * t + 2) for t in (1, 2, 3)], 4000)
@@ -417,6 +419,7 @@ def rank_program(g, core, T, topo):
 
     def reply(t, pb):
         kl = (lambda a, b: R("kr", 0, slice(a, b))) if t == 0 else (lambda a, b: R("kl", t - 1, slice(a, b)))
+        par[1], par[2] = t % 2, "r%d" % t
         ts(R("rt", t), kl(256, 384), C("col", 25), C("col", 26), A.mult, A.add)
         ts(R("kb"), kl(0, 256), 1.0, None, A.mult)
         o = C(pb, 256, 512)
@@ -425,7 +428,7 @@ def rank_program(g, core, T, topo):
 
     def state(z, pb, nxt, cur, old):
         mmg([([(o, R("xx", h), R("rt", nxt))] if nxt is not None else []) + ([(o, R("yy", h), R("rt", cur))] if cur is not None else []) +
-             ([(o, R("ww", u), R("zo", old, slice(128 * h, 128 * h + 128))) for u in (0, 1)] if old is not None else [])
+             ([(o, R("ww"), R("zo", old, slice(128 * h, 128 * h + 128)))] if old is not None else [])
              for h in (0, 1) for o in [C(pb, 128 * h, 128 * h + 128)]])
         tt(R("zin", z), C(pb, 0, 256), R("cz"), A.max)
 
@@ -437,7 +440,8 @@ def rank_program(g, core, T, topo):
         ts(R("ofc", t), R("off", t), float(cap), None, A.min)
 
     def test(t, n, cut, pa, pb, pc, pd):
-        sw, kx, par[2] = IX(R("sw"), R("off", t)), R("kx"), "t%d" % t
+        par[1], par[2] = t % 2, "t%d" % t
+        sw, kx = IX(R("sw"), R("off", t)), R("kx")
         ta, tc = ((lambda a, b, s=None: C("ta", a, b, s)), (lambda a, b, s=None: C("tc", a, b, s))) if n == 96 else (
             (lambda a, b, s=None: R("ga", 0, slice(a, b, s))), (lambda a, b, s=None: R("ga", 1, slice(a, b, s))))
         op({"v": (60 + SCT * CY * 256, lambda: V.tensor_copy(sw["ap"], kx["ap"]))}, [kx, R("off", t)], [R("sw")])
@@ -447,9 +451,8 @@ def rank_program(g, core, T, topo):
         for a, b in cut:
             cp(ta(16 * a, 16 * b), IX(R("tb", 0), C("ab", a, b)))
             cp(tc(16 * a, 16 * b), IX(R("tb", t), C("ab", n + a, n + b)))
-        if t < NT - 1:
-            reply(t + 1, pd)
-        state(t + 1, pd, t + 1 if t + 1 < NT else None, t, t - 1 if 0 < t < NT - 1 else None)
+        if t == NT - 1:
+            state(t + 1, pd, None, t, None)
         for a, b in cut:
             xs = C("xs", 6 * a, 6 * b)
             cp(xs, sums(pa, ta, a, b, ("ident", "i256", "i64k")))
@@ -457,20 +460,20 @@ def rank_program(g, core, T, topo):
             tt(C("nee", 6 * a, 6 * b), sums(pc, tc, a, b, ("ni1", "ni256", "ni64k")), xs, A.not_equal)
         for a, b in cut:
             w = 2 * (b - a)
-            mm([(C(pd, a, b), R(m), C(x, 6 * a + w * j + h, 6 * a + w * j + w, 2))
+            mm([(C(pa, a, b), R(m), C(x, 6 * a + w * j + h, 6 * a + w * j + w, 2))
                 for m, x in (("l1", "ned"), ("l2", "nee")) for j in range(3) for h in (0, 1)])
-        a, fp, fm, rr = C(pd, 0, n), C("fpm", 0, n), C("fpm", n, 2 * n), C("rr", 0, n)
+        a, fp, fm, rr = C(pa, 0, n), C("fpm", 0, n), C("fpm", n, 2 * n), C("rr", 0, n)
         ts(rr, a, 256 * MAGIC, 256 * MAGIC, A.add, A.subtract)
         tt(fp, a, rr, A.is_equal)
         ts(fm, rr, 1.0, None, A.is_lt, act=(F.Relu, 1.0, -1.0))
-        a = C(pb, 0, n)
+        a = C(pc, 0, n)
         mm([(a, R("rw"), fm), (a, R("rw"), fp)])
         tt(C("res", 0, n), a, C("cres", 0, n), A.max)
         tt(R("zo", t), IX(C("res", 0, n + 16), R("ofc", t)), R("zin", t + 1), A.min)
-        a, b = C(pa, 0, n), C(pa, n, 2 * n)
+        a, b = C(pb, 0, n), C(pb, n, 2 * n)
         mmg([[(a, R("tt"), fp), (a, R("nu"), fm)], [(b, R("tt"), fm), (b, R("nui"), fp)]])
-        ts(C("oh", 0, 2 * n), C(pa, 0, 2 * n), 0.0, None, A.max, act=(F.Relu, 0.0, 1.0))
-        a = C(pd, 0, n)
+        ts(C("oh", 0, 2 * n), C(pb, 0, 2 * n), 0.0, None, A.max, act=(F.Relu, 0.0, 1.0))
+        a = C(pa, 0, n)
         mm([(a, R("rp"), C("oh", 0, n)), (a, R("rm"), C("oh", n, 2 * n))])
         cp(C("rs2", 0, n), a)
         cp(R("zm", t), IX(C("rs2", 0, n + 16), R("ofc", t)))
@@ -487,15 +490,18 @@ def rank_program(g, core, T, topo):
     claim(1)
     if ORD[0] == 1:
         unpack(1, 2)
+    reply(1, "p7"), state(1, "p7", 1, 0, None)
     test(0, *home)
     claim(2)
     if ORD[1] == 0:
         unpack(2, 2)
+    reply(2, "p7"), state(2, "p7", 2, 1, 0)
     test(1, *home)
     claim(3)
     if ORD[1] == 1:
         unpack(2, 0)
-    unpack(3, 2)
+    reply(3, "p7"), state(3, "p7", 3, 2, 1)
+    unpack(3, 1)
     test(2, *home)
     test(3, *home)
     o = R("p1", slice(0, 256), part=slice(0, 40))
@@ -567,6 +573,7 @@ def rank_program(g, core, T, topo):
                 key = list(-np.array(b[3]))
         INFO["plan"] = (plan[0], plan[1], sorted(((i, plan[2][i]) for i in range(n)), key=lambda x: (x[1], x[0])))
     end, eng, order = INFO["plan"]
+    INFO["r"] = (ops, cost, lat)
     INFO["order"] = [(st, eng[i], ops[i]["tag"], cost[i][eng[i]]) for i, st in order]
 
     pos, seen, waits, need = {}, {}, [], set()

@@ -1,68 +1,49 @@
 import numpy as np
-from concourse.mybir import AluOpType, AxisListType, ActivationFunctionType
+from concourse.mybir import AluOpType, ActivationFunctionType
 from concourse.bass import DstId, RemoteDMATransfer
 
 A = AluOpType
 F = ActivationFunctionType
-N, NT, PW, WIN, CH = 8, 4, 684, 1120, 1024
+N, NT, PW, WIN = 8, 4, 342, 1120
 SHIFT = [0, 1, 3, 6]
-MAGIC = 12582912.0
+KID = [(0, 1), (0, 240), (0, 65536), (1, 1), (1, 240), (1, 65536), (2, 241), (2, 65536)]
+HM = [1, 240, 241, 65536, -1, -240, -241, -65536]
+OFFS = 112.0 * 65777
 
 _B = {}
 for _d, _l in (
-    ("bfloat16", dict(lf=2048, ivs=1024, bdw=256, ident=128, i16=128, i256=128, i64k=128, ni256=128, hw=256, nhw=256,
-                      sc0=128, sc1=(32, 4), sc2=(16, 8), sc3=(8, 16), f0=128, f1=128, f2=128, f3=128, n3=(8, 16), w8=(8, 16), w8s=(8, 16),
-                      w8x=(8, 16), wd=64, wp=64, ones=256, cneg=64, tneg=256, wn1=256, wn2=256, e2=144, pm=136, tt=128, nu=128, nui=128,
-                      t2k=128, e1=256, e1m=256, e3=256, ez=144, xx=(2, 8, 16), yy=(2, 8, 16), ww=(8, 16), l1=128, l2=128, rp=(8, 16), rm=(8, 16),
-                      ni1=128, ni64k=128, ll=16, sel=(5, 40),
-                      dt3=(64, 16), ct=1024, req=256, rq=(3, 256), tb=(4, 2048), ga=(2, 4096), ta=1536, tc=1536, sq=512, fit=256,
-                      iw=256, sg=256, fitm=256, ohm=256, chi=256, ned=1152, nee=1152, rr=192, fpm=384, oh=384, rw=(8, 16), rs2=208,
-                      zm=(4, 256), nbd=128, m512=128, mneg=128)),
-    ("float32", dict(cc=256, gc=256, ln=256, pn=16, pf=12, col=40, oh16=16, q4=4, e8=8, rs=512, pm1=512, dl=512, pm2=512, ck=(64, 2),
-                     h32=256, pr=256, xs=1152, res=208, cres=192, kx=256, ysb=256)),
-    ("float16", dict(pk=PW, pl=(3, PW), y1=PW, y2=PW, wh=(4, 256), val=256, kw=256, rt=(4, 128), ka8=256, kb=256, cz=256, d0=256,
-                     zin=(6, 256), zo=(4, 256), zs=256)),
-    ("int32", dict(kds=1024, bks=1024, lvi=16, lbi=64, pi=12, sw=WIN, bi=192)),
-    ("uint16", dict(lvu=16, lbu=64, lbr=(3, 16), wu=(4, 256), wl=16, kr=(4, 384), kl=(3, 384), off=(4, 16), ofc=(4, 16), ab=384)),
+    ("bfloat16", dict(lfs=2048, ivs=1024, ones=512, bd8=8, bdw=256, n8=(8, 8), w3=(2, 8, 16), wd=64, wp=64, cneg=128, tp=256, wn1=256, wn2=256,
+                      e2=144, pm=136, tt=128, nu=128, nui=128, nbd=(8, 16), e1=256, e1m=256, ez=144, xx=(2, 8, 16), yy=(2, 8, 16), ww=(8, 16),
+                      rw=(8, 16), l1=128, l2=128, hm=(8, 8, 16), ids=(6, 128), zt=128, sel=(6, 8, 5), dt3=(64, 16), ct=1024, req=256,
+                      rq=(3, 256), ga=(4, 4096), ta=(4, 1536), tc=(4, 1536), sq=(4, 512), fit=(4, 256), iw=(4, 256), sg=(4, 256),
+                      fitm=(4, 256), ohm=(4, 256), nd=(2, 6, 96, 2), fpm=(4, 2, 96), oh=(4, 192), rs2=(4, 112), zm=(3, 256))),
+    ("float32", dict(cc=136, gc=256, ln=256, lm=96, pf=8, col=24, q4=4, oh2=2, rs=512, pm1=512, dl=512, pm2=512, ck=(64, 2), h32=(16, 16),
+                     hk=(4, 256), pr=(4, 256), res=112, cres=96, cz=256, kx=(4, 256), zin=(5, 256), ysb=256)),
+    ("float16", dict(wh=(4, 256), val=(4, 256), kw=(4, 256), ka=256, d0=256, z0=256, zo=(4, 256), zs=256, kr=(4, 384), kl=(3, 384))),
+    ("int32", dict(kds=1024, bks=1024, lvi=16, lbi=64, pi=8, sw=WIN, bi=96, pk=PW, pl=(3, PW), tb=(3, 2048))),
+    ("uint16", dict(lvu=16, lbu=64, lbr=(3, 16), wu=(4, 256), wl=(4, 16), off=(4, 16), ofc=(4, 16), ab=(4, 192))),
 ):
     for _k, _s in _l.items():
-        _B["lfs" if _k == "lf" else _k] = ("sbuf", [128] + (list(_s) if isinstance(_s, tuple) else [_s]), _d)
-MATS = [k for k, v in _B.items() if v[1:] == ([128, 128], "bfloat16")]
-TWICE = ("sq", "fit", "val", "wl", "iw", "kw", "sg", "fitm", "ohm", "chi", "pr", "y1", "y2")
-LAST = ("kb", "kx")
-for _k in TWICE + LAST:
-    _B[_k] = ("sbuf", [128, 2, _B[_k][1][1]], _B[_k][2])
-for _k in MATS:
-    del _B[_k]
-_B["mats"] = ("sbuf", [128, len(MATS), 128], "bfloat16")
+        _B[_k] = ("sbuf", [128] + (list(_s) if isinstance(_s, tuple) else [_s]), _d)
+_B["pd"] = ("dram", [128 + 16 * SHIFT[-1], PW], "int32")
 for _k in range(8):
     _B["p%d" % _k] = ("psum", [128, 512], "float32")
 SCRATCH = _B
-SEMAPHORES = (["v", "s", "t", "p", "snt", "st"] + ["ld%d" % i for i in range(12)] +
+SEMAPHORES = (["v", "s", "t", "p", "snt"] + ["ld%d" % i for i in range(12)] +
               [x + str(t) for x in ("lb", "rq", "pk", "kr") for t in (1, 2, 3)])
 
-CY, PC, LAT, GC = 0.9, 0.45, 150.0, 1.56
-SCT, TRIES, CUT, CUT3 = 3.8, 600, ((0, 64), (64, 96)), ((0, 80), (80, 160), (160, 192))
+CY, PC, LAT, GC, SCT = 0.9, 0.45, 150.0, 1.56, 3.8
+CH, CUT, ROUNDS, TRIES = 1024, ((0, 32), (32, 64), (64, 96)), 8, 150
 VB = [1.0, 1.5, 2.0, 3.0]
-ORD, BONUS = (1, 1), {}
 INFO = {}
 
 
-def rank_program(g, core, T, topo):
-    rank = T.rank_of(core)
-    if rank is None:
-        return
-    Q = {"v": g.vector, "s": g.scalar, "t": g.tensor, "p": g, "y": g.sync}
+def record(g, core, rank, T, topo):
     V, S, P = g.vector, g.scalar, g.tensor
-    ops, acc, par = [], {}, [0, 0, ""]
+    ops, acc, uses, sent, nld = [], {}, {}, [0], [0]
+    al = slice(None)
 
-    def R(name, *idx, part=slice(None)):
-        if name in TWICE:
-            idx = (par[0],) + idx
-        if name in LAST:
-            idx = (par[1],) + idx
-        if name in MATS:
-            name, idx = "mats", (MATS.index(name),) + idx
+    def R(name, *idx, part=al):
         shape = SCRATCH[name][1][1:]
         el = np.arange(int(np.prod(shape))).reshape(shape)[idx].ravel()
         m = 0
@@ -71,21 +52,28 @@ def rank_program(g, core, T, topo):
         else:
             for k in el.tolist():
                 m |= 1 << k
-        return dict(ap=T[name][(part,) + idx], b=name, m=m, n=len(el), w=2 if "16" in SCRATCH[name][2] else 4, off=None)
+        return dict(ap=T[name][(part,) + idx], b=name, m=m, n=len(el), w=2 if "16" in SCRATCH[name][2] else 4, off=None, ps=False)
 
     def C(name, a, b=None, s=None):
         return R(name, slice(a, a + 1 if b is None else b, s))
 
+    def D(name, k, a, b, s=None):
+        return R(name, k, slice(a, b, s))
+
+    def B(use, a, b, part=al, step=1):
+        return dict(ap=T[INFO.get("bank", {}).get(use, "p0")][part, a:b:step], b=use, m=1, n=len(range(a, b, step)), w=4, off=None, ps=True)
+
     def IX(win, off):
         return dict(win, ap=win["ap"].indirect(off["ap"]), n=16 * off["n"], off=off)
 
-    def op(var, reads, writes, sem=None, after=(), tag=""):
+    def op(var, reads, writes, sem=None, after=(), behind=(), tag=""):
         i, deps = len(ops), {}
         reads = [r for r in reads if isinstance(r, dict)]
         reads = reads + [r["off"] for r in reads if r["off"]]
         for x, wr in [(r, False) for r in reads] + [(w, True) for w in writes]:
             l = acc.setdefault(x["b"], [])
-            if SCRATCH[x["b"]][0] == "psum":
+            if x["ps"]:
+                uses.setdefault(x["b"], []).append(i)
                 for j, m, pw in l[::-1]:
                     if j != i:
                         deps[j] = deps.get(j, False) or pw or wr
@@ -103,7 +91,9 @@ def rank_program(g, core, T, topo):
             l.append((i, x["m"], wr))
         for j in after:
             deps[j] = True
-        ops.append(dict(ph=par[2], var=var, deps=deps, sem=sem, tag=tag or (writes[0]["b"] if writes else "")))
+        for j in behind:
+            deps.setdefault(j, None)
+        ops.append(dict(var=var, deps=deps, sem=sem, tag=tag or (writes[0]["b"] if writes else "")))
         return i
 
     def ap(x):
@@ -117,15 +107,20 @@ def rank_program(g, core, T, topo):
     def sc(i):
         return 70 + CY * (GC * i["n"] if i["off"] else max(64, i["n"]))
 
-    def ts(o, i, a, b, op0, op1=None, act=None):
+    def ts(o, i, a, b, op0, op1=None, act=None, more=None):
         var = {"v": (vc(o, i), lambda: V.tensor_scalar(o["ap"], i["ap"], ap(a), ap(b), op0, op1) if op1 else
                      V.tensor_scalar(o["ap"], i["ap"], ap(a), None, op0))}
         if act:
             var["s"] = (sc(i), lambda: S.activation(o["ap"], i["ap"], act[0], bias=ap(act[1]), scale=ap(act[2])))
-        return op(var, [i, a, b], [o])
+        if more:
+            var["p"] = more[0]
+        return op(var, [i, a, b] + list(act[1:] if act else []) + (more[1] if more else []), [o])
 
-    def mul(o, i, a):
-        return ts(o, i, a, None, A.mult, act=(F.Copy, 0.0, a))
+    def mul(o, i, a, more=None):
+        return ts(o, i, a, None, A.mult, act=(F.Copy, 0.0, a), more=more)
+
+    def lin(o, i, a, b):
+        return ts(o, i, a, b, A.mult, A.add, act=(F.Identity, b, a))
 
     def cp(o, i, s=True):
         var = {"v": (vc(o, i), lambda: V.tensor_copy(o["ap"], i["ap"]))}
@@ -134,32 +129,32 @@ def rank_program(g, core, T, topo):
         return op(var, [i], [o])
 
     def tt(o, a, b, alu):
-        ps = a["b"][0] == "p" and len(a["b"]) == 2 and a["b"][1].isdigit()
-        return op({"v": (vc(o, a, 1.001 if ps else 2.0), lambda: V.tensor_tensor(o["ap"], a["ap"], b["ap"], alu))}, [a, b], [o])
+        return op({"v": (vc(o, a, 1.001 if a["ps"] else 2.0), lambda: V.tensor_tensor(o["ap"], a["ap"], b["ap"], alu))}, [a, b], [o])
 
-    def scan(o, a, b, init, op0, op1):
-        return op({"v": (vc(o, b), lambda: V.tensor_tensor_scan(o["ap"], a["ap"], b["ap"], init, op0, op1))}, [a, b], [o])
+    def scan(o, a, b, op0, op1):
+        return op({"v": (vc(o, b), lambda: V.tensor_tensor_scan(o["ap"], a["ap"], b["ap"], 0.0, op0, op1))}, [a, b], [o])
 
-    def ms(o, c):
+    def io(o, pat, base, cm):
+        fl = SCRATCH[o["b"]][2] != "int32"
+        return (130 + 2 * CY * o["n"], lambda: g.iota(o["ap"], pat, base, cm, allow_small_or_imprecise_dtypes=True) if fl
+                else g.iota(o["ap"], pat, base, cm))
+
+    def iota(o, pat, base, cm):
+        return op({"p": io(o, pat, base, cm)}, [], [o])
+
+    def ms(o, c=0.0):
         var = {"v": (vc(o, o), lambda: V.memset(o["ap"], c))}
-        if abs(c) <= 1:
-            var["p"] = (130 + 2 * CY * o["n"], lambda: g.iota(o["ap"], [[0, o["n"]]], int(c), 0, allow_small_or_imprecise_dtypes=True))
+        if abs(c) < 2 ** 24:
+            var["p"] = io(o, [[0, o["n"]]], int(c), 0)
         return op(var, [], [o])
 
+    def se(o, i, cmp, fill, pat, base, cm):
+        return (170 + 2 * CY * o["n"], lambda: g.affine_select(o["ap"], i["ap"], [list(x) for x in pat], cmp, fill, base, cm))
+
     def asel(o, i, cmp, fill, pat=((1, 128),), base=0, cm=-1):
-        return op({"p": (170 + 2 * CY * o["n"], lambda: g.affine_select(o["ap"], i["ap"], [list(x) for x in pat], cmp, fill, base, cm))}, [i], [o])
+        return op({"p": se(o, i, cmp, fill, pat, base, cm)}, [i], [o])
 
-    def zero(o, c=0):
-        return iota(o, [[0, o["n"]]], c, 0)
-
-    def band(o, i, pat, lo, hi):
-        asel(o, i, A.is_ge, 0.0, pat, -lo, 1)
-        return asel(o, o, A.is_ge, 0.0, [[-a, b] for a, b in pat], hi, -1)
-
-    def mm(l):
-        return mmg([l])
-
-    def mmg(gs, start=True, stop=True):
+    def mmg(gs, start=True, stop=True, after=()):
         def f():
             for q in gs:
                 for k, (o, a, b) in enumerate(q):
@@ -167,25 +162,22 @@ def rank_program(g, core, T, topo):
             return r
         l = [x for q in gs for x in q]
         c = 30 + sum(PC * max(64, b["n"]) * (4 if b["w"] == 4 else 1) for o, a, b in l)
-        return op({"t": (c, f)}, [x for o, a, b in l for x in (a, b)], [l[0][0]])
+        return op({"t": (c, f)}, [x for o, a, b in l for x in (a, b)], [l[0][0]], after=after)
 
-    def iota(o, pat, base, cm):
-        fl = SCRATCH[o["b"]][2] != "int32"
-        return op({"p": (130 + 2 * CY * o["n"], lambda: g.iota(o["ap"], pat, base, cm, allow_small_or_imprecise_dtypes=True) if fl
-                         else g.iota(o["ap"], pat, base, cm))}, [], [o])
+    def mm(l, **k):
+        return mmg([l], **k)
 
-    nld = [0]
+    last = []
 
-    def load(pairs, o, lat):
+    def dma(pairs, reads, writes, lat, tag=""):
         s = T.sem["ld%d" % nld[0]]
         nld[0] += 1
 
         def f():
             for a, b in pairs:
                 g.sync.dma_start(a, b).then_inc(s, 16)
-        return op({"y": (60.0 * len(pairs), f)}, [], [o], sem=(s, 16 * len(pairs), lat))
-
-    sent = [0]
+        last[:] = [op({"y": (60.0 * len(pairs), f)}, reads, writes, sem=(s, 16 * len(pairs), lat), behind=last, tag=tag)]
+        return last[0]
 
     def peer(d):
         return T.cores[(rank + d) % N]
@@ -193,337 +185,290 @@ def rank_program(g, core, T, topo):
     def emask(d, a, b):
         return sum(1 << e for e in topo.engines(core, peer(d))[a:b])
 
+    sends = []
+
     def send(src, trs, lat):
         def f():
             l = []
             for d, s, dst, sem, a, b in trs:
                 rid, pid = topo.addr(peer(d), core)
                 l.append(RemoteDMATransfer(dst_ids=[DstId(rid=rid, pnc=pid)], dma_engine_mask=emask(d, a, b), remote_sem=T.sem[sem],
-                                           srcs=[s["ap"]], dsts=[dst["ap"]]))
+                                           srcs=[s], dsts=[dst["ap"]]))
             g.remote_dma_fused(l, local_sem=T.sem.snt)
-        i = op({"p": (500.0, f)}, src, [], tag="send")
+        i = op({"p": (500.0, f)}, src, [], tag="send", behind=sends[-1:])
+        sends.append(i)
         for d, s, dst, sem, a, b in trs:
             sent[0] += b - a
             op({"n": (0.0, None)}, [], [dst], sem=(T.sem[sem], b - a, lat), after=[i], tag="arr")
 
-    load([(T.ivs[:], T.iv[:])], R("ivs"), 3000)
-    load([(T.lvi[:], T.lv[:])], R("lvi"), 2500)
-    lb = [(T.lbi[:, 0:16], T.lb[:])]
+    dma([(T.ivs[:], T.iv[:])], [], [R("ivs")], 2700)
+    dma([(T.lvi[:], T.lv[:]), (T.lbi[:, 0:16], T.lb[:])], [], [R("lvi"), C("lbi", 0, 16)], 3000)
+    dma([(T.bks[:], T.bk[:])], [], [R("bks")], 4300)
+    lb = []
     for t in (1, 2, 3):
         s = 16 * SHIFT[t]
         lb += [(T.lbi[s:128, 16 * t:16 * t + 16], T.lb[0:128 - s, :]), (T.lbi[0:s, 16 * t:16 * t + 16], T.lb[128 - s:128, :])]
-    load([(T.lfs[:], T.lf[:])], R("lfs"), 4500)
-    load(lb, R("lbi"), 4500)
-    load([(T.bks[:], T.bk[:])], R("bks"), 6000)
-    load([(T.kds[:], T.kd[:])], R("kds"), 7500)
+    dma(lb, [], [C("lbi", 16, 64)], 4500)
+    dma([(T.lfs[:], T.lf[:])], [], [R("lfs")], 5700)
+    dma([(T.kds[:], T.kd[:])], [], [R("kds")], 7200)
+
+    def col(k):
+        return C("col", k)
 
     iota(C("pi", 0), [[0, 1]], 0, 1)
-    iota(R("gc"), [[0, 2], [1, 8], [0, 16]], 0, 0)
-    iota(C("cc", 0, 128), [[1, 128]], 0, 0)
-    for k, (sh, m) in enumerate([(0, 1), (1, 1), (2, 1), (3, 1), (4, 7), (0, 15), (1, 7), (2, 3), (1, 63)]):
+    iota(R("bd8"), [[0, 8]], 1, 0)
+    asel(R("bd8"), R("bd8"), A.is_ge, 0.0, [[-16, 8]], 0, 1), asel(R("bd8"), R("bd8"), A.is_ge, 0.0, [[16, 8]], 15, -1)
+    bd8 = R("bd8")
+    iota(R("cc"), [[1, 136]], -8, 0)
+    for k, (sh, m) in enumerate([(0, 1), (1, 1), (2, 1), (3, 1), (4, 7), (0, 15), (2, 3)]):
         ts(C("pi", k + 1), C("pi", 0), sh, m, A.arith_shift_right, A.bitwise_and)
-    cp(C("pf", 0, 10), C("pi", 0, 10), s=False)
-    p_, pg, p16, p8, p4 = C("pf", 0), C("pf", 5), C("pf", 6), C("pf", 7), C("pf", 8)
-    ms(R("sc0"), 1.0), ms(C("sc0", 1, 128, 2), -1.0)
-    for b in (1, 2, 3):
-        ms(R("sc%d" % b), 1.0), ms(R("sc%d" % b, slice(None), slice(1 << b, 2 << b)), -1.0)
-    sig = [R("sc%d" % b) for b in range(4)]
-    ts(C("col", 0, 4), C("pf", 1, 5), -2.0, 1.0, A.mult, A.add)
-    ts(C("col", 4, 8), C("pf", 1, 5), -1.0, 1.0, A.mult, A.add)
-    ts(R("bdw"), R("gc"), pg, None, A.is_equal)
-    bd, bdc = C("bdw", 0, 128), C("bdw", 0, 128, 16)
+    cp(C("pf", 0, 4), C("pi", 1, 5), s=False), cp(C("pf", 4, 7), C("pi", 5, 8), s=False)
+    ts(C("pi", 1), C("pi", 0), 1, None, A.arith_shift_right), cp(C("pf", 7), C("pi", 1), s=False)
+    b3, pg, p16, p4, ph = C("pf", 3), C("pf", 4), C("pf", 5), C("pf", 6), C("pf", 7)
     for b, v in enumerate((8.0, 64.0, 4096.0)):
-        ts(C("col", 8 + b), C("col", b), -(v - 1) / 2, None, A.mult)
-        ts(R("f%d" % b), sig[b], C("col", 8 + b), (v + 1) / 2, A.mult, A.add)
-    tt(R("f0"), R("f0"), R("f1"), A.mult), tt(R("f2"), R("f2"), bd, A.mult), tt(R("n3"), R("f0"), R("f2"), A.mult)
-    lo8, hi8, al = slice(0, 8), slice(8, 16), slice(None)
-    n8, b3, nb3 = R("n3", al, lo8), C("pf", 4), C("col", 7)
-    mul(R("w8", al, lo8), n8, nb3), mul(R("w8", al, hi8), n8, b3)
-    mul(R("w8s"), R("w8"), 2.0 ** 24), mul(R("wd"), n8, C("col", 3))
+        lin(col(b), C("pf", b), v - 1, 1.0), lin(col(3 + b), C("pf", b), 1 - v, v)
+    lin(C("col", 6, 10), C("pf", 0, 4), -2.0, 1.0)
+    lin(col(10), b3, -2.0 ** 24, 2.0 ** 24)
+    for m in range(4):
+        ts(R("n8", al, m), bd8, col(3 * (m & 1)), col(1 + 3 * (m >> 1)), A.mult, A.mult)
+    mul(R("n8", al, slice(4, 8)), R("n8", al, slice(0, 4)), col(5)), mul(R("n8", al, slice(0, 4)), R("n8", al, slice(0, 4)), col(2))
+    lo, hi = (R("w3", 0, al, slice(8 * k, 8 * k + 8)) for k in range(2))
+    mul(lo, R("n8"), col(10)), ts(hi, R("n8"), b3, 2.0 ** 24, A.mult, A.mult), mul(R("wd"), R("n8"), col(9))
+    cp(R("w3", 1, al, slice(8, 16)), lo), cp(R("w3", 1, al, slice(0, 8)), hi)
+    ts(col(11), col(0), col(1), col(2), A.mult, A.mult)
+    ts(R("wp"), C("cc", 8, 72), ph, col(11), A.is_equal, A.mult)
     ms(R("ones"), 1.0), ms(R("cneg"), -2.0 ** 41)
-    op({"v": (100.0, lambda: V.tensor_reduce(T.col[:, 11:12], T.n3[:, :, 0], AxisListType.X, A.add))}, [R("n3")], [C("col", 11)])
-    ts(R("wp"), C("cc", 0, 64), C("pf", 9), C("col", 11), A.is_equal, A.mult)
-    ts(R("ident"), C("cc", 0, 128), p_, None, A.is_equal)
-    ms(R("rs"), 0.0), ms(C("rs", 0, 512, 8), 1e20)
-    ms(R("dt3", al, slice(3, 8, 4)), 0.0)
-    for b in range(4):
-        ts(R("f%d" % b), sig[b], C("pf", 1 + b), C("col", 4 + b), A.mult, A.add)
-    tt(R("f0"), R("f0"), R("f1"), A.mult), tt(R("f2"), R("f2"), R("f3"), A.mult), tt(R("f0"), R("f0"), R("f2"), A.mult)
-    tt(C("hw", 0, 128), R("f0"), bd, A.mult), cp(C("hw", 128, 256), C("hw", 0, 128))
-    hh = C("hw", 0, 128)
-    mul(R("nhw"), R("hw"), -1.0), mul(R("h32"), R("hw"), 0.0625)
-    for k, v in (("i16", 16.0), ("i256", 256.0), ("i64k", 65536.0), ("ni1", -1.0), ("ni256", -256.0), ("ni64k", -65536.0)):
-        mul(R(k), R("ident"), v)
-    ts(R("q4"), C("cc", 0, 4), p4, None, A.is_equal)
-    ts(R("oh16"), C("cc", 0, 16), p16, None, A.is_equal)
+    ms(R("rs")), ms(C("rs", 0, 512, 8), 1e20)
+    ms(R("dt3", al, slice(3, 8, 4)))
+    ms(R("zt"))
+    asel(R("ids", 0), R("zt"), A.not_equal, 1.0)
+    ident = R("ids", 0)
+
+    iota(R("gc"), [[0, 2], [1, 8], [0, 16]], 0, 0)
+    ts(R("bdw"), R("gc"), pg, None, A.is_equal)
+    ts(R("q4"), C("cc", 8, 12), p4, None, A.is_equal), ts(R("oh2"), C("cc", 8, 10), p16, None, A.is_equal)
+    oh0, oh1 = C("oh2", 0), C("oh2", 1)
     for k in (0, 1):
-        ts(C("tneg", k, 256, 2), C("bdw", k, 256, 2), C("q4", k), -1.0, A.mult, A.mult)
-    ts(R("wn1"), R("bdw"), C("q4", 2), -1.0, A.mult, A.mult), ts(R("wn2"), R("bdw"), C("q4", 3), -2.0, A.mult, A.mult)
-    ts(R("w8x", al, lo8), n8, b3, 2.0, A.mult, A.mult), ts(R("w8x", al, hi8), n8, nb3, 2.0, A.mult, A.mult)
-    ts(C("col", 12), pg, 16.0, 8.0, A.mult, A.add)
-    ts(C("col", 14), C("col", 12), p8, None, A.add)
-    zero(R("e2")), ms(C("pm", 128, 136), 0.0), zero(R("e1")), zero(R("e1m"))
-    mul(C("e2", 14, 128, 16), bdc, C("q4", 0)), mul(C("e2", 15, 128, 16), bdc, C("q4", 1))
-    ts(C("pm", 0, 128), C("cc", 0, 128), C("col", 14), None, A.is_equal)
-    cp(C("e1", 15, 256, 16), C("bdw", 0, 256, 16)), mul(C("e1m", 15, 256, 16), C("bdw", 0, 256, 16), p16)
-    mul(R("nbd"), bd, -1.0)
+        mul(C("tp", k, 256, 2), C("bdw", k, 256, 2), C("q4", k))
+        ts(R("wn%d" % (k + 1)), R("bdw"), C("q4", 2 + k), 2.0 ** 24, A.mult, A.mult)
+    asel(R("e2"), C("tp", 0, 144), A.is_ge, 0.0, [[0, 9], [1, 16]], -14, 0)
+    ts(col(12), pg, 8.0, ph, A.mult, A.add), ts(R("pm"), R("cc"), col(12), None, A.is_equal)
+    mul(R("nbd"), C("bdw", 0, 128), -1.0)
     asel(R("nu"), R("nbd"), A.is_gt, 0.0), asel(R("nui"), R("nbd"), A.is_ge, 0.0), asel(R("tt"), R("nu"), A.not_equal, 1.0)
-    mul(R("t2k"), R("tt"), 2048.0)
-    ts(R("e8"), C("cc", 0, 8), p8, None, A.is_equal)
-    oh, e8, c128 = (lambda k: C("oh16", k)), (lambda k: C("e8", k)), C("cc", 0, 128)
-    two, o16 = [[-16, 8], [-1, 2]], C("ones", 0, 16)
-    zero(R("xx")), zero(R("yy")), zero(R("ww"))
+    asel(R("e1"), R("bdw"), A.is_equal, 0.0, [[0, 16], [1, 16]], -15, 0), mul(R("e1m"), R("e1"), p16)
+    cp(R("hm", 0, al, 0), bd8)
+    for b in range(4):
+        mul(R("hm", 0, al, slice(1 << b, 2 << b)), R("hm", 0, al, slice(0, 1 << b)), col(6 + b))
+    hh = R("hm", 0)
+    for k in (0, 1):
+        mul(R("h32", slice(8 * k, 8 * k + 8)), hh, 0.0625)
+    for k in range(1, 6):
+        mul(R("ids", k), ident, 16.0 ** k, more=(se(R("ids", k), R("zt"), A.not_equal, 16.0 ** k, ((1, 128),), 0, -1), [R("zt")]))
+
+    for k in range(1, 8):
+        mul(R("hm", k), hh, float(HM[k]))
+    ts(R("l1"), hh, 0.0, None, A.max, act=(F.Relu, 0.0, 1.0)), ts(R("l2"), R("hm", 4), 0.0, None, A.max, act=(F.Relu, 0.0, 1.0))
+    mul(col(13), oh0, OFFS), mul(col(14), oh0, -OFFS)
+    two, s2 = [[-16, 8], [0, 2]], slice(0, 2)
+    ms(R("xx")), ms(R("yy")), ms(R("ww")), ms(R("rw")), ms(R("ez"))
+    iota(R("xx", 1, al, s2), [[0, 8], [1023, 2]], 1, 0), iota(R("ww", al, s2), [[0, 16]], -2 ** 21, 0)
+    asel(R("ww", al, s2), R("ww", al, s2), A.is_equal, 0.0, two, -3, 1)
     for h in (0, 1):
-        asel(R("xx", h, al, slice(0, 2)), o16, A.is_equal, 0.0, two, -8 * h, 1)
-        asel(R("yy", h, al, slice(9, 11)), o16, A.is_equal, 0.0, two, -8 * h - 2, 1)
-        asel(R("ww", al, slice(4 * h, 4 * h + 2)), o16, A.is_equal, 0.0, two, -4, 1)
-    zero(R("e3"))
-    for k in (13, 14, 15):
-        cp(C("e3", k, 256, 16), C("bdw", 0, 256, 16))
-    for k, v in (("l1", -127.5), ("l2", 127.5)):
-        ts(R(k), R("f0"), v, 128.5, A.mult, A.add), band(R(k), R(k), [[-16, 8], [0, 16]], 0, 15)
-    zero(R("rp"))
-    bd2 = C("bdw", 0, 128, 8)
-    mul(R("rw"), bd, -2048.0), mul(R("rw", al, slice(9, 11)), bd2, 2048.0), mul(R("rw", al, slice(11, 13)), bd2, 0.0)
-    zero(R("rm")), mul(R("rp", al, 11), bdc, p16), mul(R("rm", al, 11), bdc, p16)
-    cp(R("rp", al, 12), bdc), mul(R("rm", al, 12), bdc, -1.0)
-    tt(C("col", 24), e8(0), e8(4), A.add)
-    ts(C("col", 17), C("col", 24), -4095.0, 4096.0, A.mult, A.add)
-    ts(C("col", 18), oh(2), oh(10), -1.0, A.add, A.mult)
-    ts(C("col", 25), oh(1), oh(9), 1023.0, A.add, A.mult)
-    ts(C("col", 26), C("col", 25), C("col", 24), -1.0, A.add, A.mult)
-    ts(C("col", 25), C("col", 25), 1.0, None, A.add)
-    zero(R("ez"))
+        asel(R("xx", h, al, s2), R("xx", 1, al, s2), A.is_equal, 0.0, two, -8 * h, 1)
+        asel(R("yy", h, al, slice(3, 5)), C("ones", 0, 16), A.is_equal, 0.0, [[-16, 8], [-1, 2]], -8 * h, 1)
+    mul(R("rw", al, slice(0, 3)), R("nbd", al, slice(0, 3)), 2048.0), mul(R("rw", al, slice(3, 5)), R("nbd", al, slice(3, 5)), -2048.0)
     ez = C("ez", 15, 128, 16)
     asel(ez, C("ones", 0, 8), A.is_equal, 0.0, [[-16, 8]], 0, 1), asel(ez, ez, A.not_equal, -1.0, [[-16, 8]], -1, 1)
-    ts(R("ll"), C("cc", 0, 16), 16.0, p16, A.mult, A.add)
-    mul(R("d0"), R("ones"), oh(0))
-    ts(C("col", 30), oh(1), -1.0, None, A.mult)
-    ts(C("col", 28), oh(1), -767.0, -1.0, A.mult, A.add), ts(C("col", 28), oh(5), -1023.0, C("col", 28), A.mult, A.add)
-    ts(C("cres", 0, 96), C("cc", 0, 96), C("col", 30), C("col", 28), A.mult, A.add)
-    ts(C("col", 29), e8(2), -2048.0, oh(0), A.mult, A.subtract), ts(C("col", 29), oh(1), -256.0, C("col", 29), A.mult, A.add)
-    iota(R("ln"), [[1, 256]], 0, 0)
-    iota(C("sw", 0, 96), [[0, 96]], 0, 0), ms(C("res", 96, 112), 0.0), ms(C("rs2", 96, 112), 0.0)
-    ts(R("cz"), R("ln"), C("col", 30), C("col", 29), A.mult, A.add)
-    for t in range(NT + 1):
-        zero(R("sel", t), int(t < NT)), zero(R("sel", t, slice(0, 40, 5)), -1 - (rank + t) % N if t < NT else -1)
-        asel(R("sel", t), R("sel", t), A.is_equal, 0.0, [[-16, 8], [-1, 5]], -8, 1)
+    mul(R("d0"), C("ones", 0, 256), oh0)
+    iota(R("ln"), [[-1, 256]], 767, 0), iota(R("lm"), [[-1, 96]], 255, 0)
+    ts(col(15), p16, 5.0, 16.0, A.is_ge, A.mult), ts(col(16), p16, 2.0, -1.0, A.is_ge, A.mult), ts(col(17), oh1, 1024.0, oh0, A.mult, A.add)
+    lin(R("cz"), R("ln"), oh1, col(15)), lin(R("cres"), R("lm"), oh1, col(16))
+    mul(C("res", 96, 112), C("ones", 0, 16), col(17)), ms(R("rs2", al, slice(96, 112)))
+    iota(C("sw", 0, 96), [[0, 96]], 0, 0)
+    one, far = R("sel", NT), [[-16, 8], [200, 5]]
+    iota(one, [[0, 40]], 1, 0), iota(R("sel", NT, al, 4), [[0, 8]], 2, 0)
+    asel(one, one, A.is_equal, 0.0, [[-16, 8], [-1, 5]], -2, 1)
+    asel(R("sel", NT, al, slice(1, 5, 3)), R("sel", NT, al, slice(1, 5, 3)), A.not_equal, 1.0, two, -2, 1)
+    for t in range(NT):
+        asel(R("sel", t), one, A.not_equal, -1.0 - (rank + t) % N, far, -2, 1)
+    asel(R("sel", NT + 1), C("zt", 0, 40), A.not_equal, -1.0, far, 0, 1)
 
-    cp(R("lbu"), R("lbi"), s=False), cp(R("lvu"), R("lvi"), s=False)
-    send([R("lbu")], [(t, C("lbu", 16 * t, 16 * t + 16), R("lbr", t - 1), "lb%d" % t, 2 * t, 2 * t + 2) for t in (1, 2, 3)], 4000)
-    for a, b, pb in ((0, 512, "p4"), (512, PW, "p5")):
-        e = min(b, 2048 - 2 * PW)
-        mm([(C(pb, 0, b - a), R("ident"), C("lfs", a, b)), (C(pb, 0, b - a), R("i16"), C("lfs", PW + a, PW + b)),
-            (C(pb, 0, e - a), R("i256"), C("lfs", 2 * PW + a, 2 * PW + e))])
-        cp(C("pk", a, b), C(pb, 0, b - a))
-    for t in (1, 2, 3):
-        send([R("pk")], [(-t, R("pk"), R("pl", t - 1), "pk%d" % t, 0, 4)], 3000 + 4000 * t)
+    cp(C("lbu", 0, 16), C("lbi", 0, 16), s=False), cp(C("lbu", 16, 64), C("lbi", 16, 64), s=False), cp(R("lvu"), R("lvi"), s=False)
+    send([C("lbu", 16, 64)], [(t, T.lbu[:, 16 * t:16 * t + 16], R("lbr", t - 1), "lb%d" % t, 2 * t, 2 * t + 2) for t in (1, 2, 3)], 4000)
 
     ivc = [C("ivs", 128 * c, 128 * c + 128) for c in range(8)]
-    mmg([[(C("p0", 64 * c, 64 * c + 64), a, b) for a, b in ((ivc[c], R("w8s", al, lo8)), (C("ones", 0, 128), R("cneg")), (ivc[c], R("w8s", al, hi8)))]
-         for c in range(8)])
-    mmg([[(C("p2", 64 * c, 64 * c + 64), ivc[c], R("wd"))] for c in range(8)])
-    mmg([[(C("p1", 64 * c, 64 * c + 64), ivc[c], R("wp"))] for c in range(8)])
-    scan(R("pm1"), R("rs"), R("p0"), 0.0, A.add, A.min)
-    op({"s": (sc(R("p2")), lambda: S.activation(T.p2[:], T.p2[:], F.Abs))}, [R("p2")], [R("p2")])
+    ks, kd_, kp = B("ks", 0, 512), B("kd", 0, 512), B("kp", 0, 512)
+    mm([(ks, R("cneg"), R("ones"))], stop=False)
+    mm([(B("ks", 64 * c, 64 * c + 64), ivc[c], w) for c in range(8) for w in (lo, hi)], start=False)
+    mmg([[(B("kd", 64 * c, 64 * c + 64), ivc[c], R("wd"))] for c in range(8)])
+    mmg([[(B("kp", 64 * c, 64 * c + 64), ivc[c], R("wp"))] for c in range(8)])
+    scan(R("pm1"), R("rs"), ks, A.add, A.min)
+    op({"s": (sc(kd_), lambda: S.activation(kd_["ap"], kd_["ap"], F.Abs))}, [kd_], [kd_])
     for i in range(8):
-        tt(C("dl", i, 512, 8), C("p0", i, 512, 8), C("pm1", 7, 512, 8), A.subtract)
-    tt(R("dl"), R("p2"), R("dl"), A.add)
-    scan(R("pm2"), R("rs"), R("dl"), 0.0, A.add, A.min)
-    cp(R("dt3", al, hi8), R("p1"))
-    cp(R("ck", al, 0), C("pm1", 7, 512, 8)), cp(R("ck", al, 1), C("pm2", 7, 512, 8))
-    dg = [R("dt3", al, slice(j, 8, 4)) for j in range(3)]
-    cp(dg[0], R("ck"), s=False), tt(R("ck"), R("ck"), dg[0], A.subtract)
-    cp(dg[1], R("ck"), s=False), tt(dg[2], R("ck"), dg[1], A.subtract)
-    for h, pb in enumerate(("p0", "p2")):
-        mmg([[(C(pb, 128 * c, 128 * c + 128), R("dt3", slice(32 * h + 8 * c, 32 * h + 8 * c + 8)), R("ident"))] for c in range(4)])
-        cp(C("ct", 512 * h, 512 * h + 512), R(pb))
-    cp(R("req"), IX(R("ct"), R("lvu")))
+        tt(C("dl", i, 512, 8), B("ks", i, 512, step=8), C("pm1", 7, 512, 8), A.subtract)
+    tt(R("dl"), kd_, R("dl"), A.add)
+    scan(R("pm2"), R("rs"), R("dl"), A.add, A.min)
+    cp(R("dt3", al, slice(8, 16)), kp)
+    for k, x in enumerate(("pm1", "pm2")):
+        x, r = C(x, 7, 512, 8), R("ck", al, k)
+        dg = [R("dt3", al, 4 * k + j) for j in range(3)]
+        cp(dg[0], x), tt(r, x, dg[0], A.subtract), cp(dg[1], r), tt(dg[2], r, dg[1], A.subtract)
+    for h in (0, 1):
+        mmg([[(B("kt%d" % h, 128 * c, 128 * c + 128), R("dt3", slice(32 * h + 8 * c, 32 * h + 8 * c + 8)), ident)] for c in range(4)])
+        cp(C("ct", 512 * h, 512 * h + 512), B("kt%d" % h, 0, 512))
+    mul(R("req"), IX(R("ct"), R("lvu")), -1.0)
     for t in (1, 2, 3):
-        send([R("req")], [(t, R("req"), R("rq", t - 1), "rq%d" % t, 4, 8)], 2500 + 800 * t)
+        send([R("req")], [(t, T.req[:], R("rq", t - 1), "rq%d" % t, 0, 8)], 2600 + 400 * t)
 
-    bank = [0]
+    mm([(B("pk", 0, min(PW, 2048 - PW * j)), R("ids", j), C("lfs", PW * j, min(PW * j + PW, 2048))) for j in range(6)])
+    ts(R("pk"), B("pk", 0, PW), 7.0 * 0x111111, None, A.add)
+    pd = dict(R("pk"), b="pd")
+    dma([(T.pd[0:128, :], T.pk[:]), (T.pd[128:128 + 16 * SHIFT[-1], :], T.pk[0:16 * SHIFT[-1], :])], [R("pk")], [pd], 2800)
+    for t in (1, 2, 3):
+        send([pd], [(-t, T.pd[16 * SHIFT[t]:16 * SHIFT[t] + 128, :], R("pl", t - 1), "pk%d" % t, 0, 8)], 2500 + 2500 * t)
 
-    def nextbank(first=4):
-        bank[0] ^= 1
-        return "p%d" % (first + bank[0])
-
-    def own_table():
-        for c in range(4):
-            pb = nextbank()
-            mm([(R(pb), hh, C("lfs", 512 * c, 512 * c + 512))])
-            cp(R("tb", 0, slice(512 * c, 512 * c + 512)), R(pb))
-
-    def unpack(t, first=4):
-        s = 16 * SHIFT[t]
-        par[0], par[2] = t % 2, "u%d" % t
-        h, nh, x = C("hw", s, s + 128), C("nhw", s, s + 128), R("pl", t - 1)
-        ts(R("y1"), x, 16 * MAGIC, 16 * MAGIC, A.add, A.subtract), ts(R("y2"), x, 256 * MAGIC, 256 * MAGIC, A.add, A.subtract)
-        for k, scale in enumerate((1.0, 0.0625, 1.0 / 256)):
-            for a, b in ((0, 342), (342, PW)):
-                e = min(b, 2048 - k * PW)
-                pb = nextbank(first)
-                o = C(pb, 0, e - a)
-                src = [R("pl", t - 1, slice(a, e)), C("y1", a, e), C("y2", a, e)]
-                mm([(o, h, src[k])] + ([(o, nh, src[k + 1])] if k < 2 else []))
-                mul(R("tb", t, slice(k * PW + a, k * PW + e)), o, scale)
-
-    def sums(pb, buf, a, b, ids):
-        w = 2 * (b - a)
-        mmg([[(C(pb, w * j, w * j + w), R(ids[d - 3 * j]), buf(16 * a + d, 16 * b, 8)) for d in range(3 * j, min(8, 3 * j + 3))]
-             for j in range(3)])
-        return C(pb, 0, 3 * w)
+    def unpack(t):
+        for j in range(6):
+            w = min(PW, 2048 - PW * j)
+            ts(D("tb", t - 1, PW * j, PW * j + w), D("pl", t - 1, 0, w), 4 * j, 15, A.arith_shift_right, A.bitwise_and)
 
     def claim(t):
         s = 16 * SHIFT[t]
-        r, par[0], par[2] = (128 - s) % 128, t % 2, "c%d" % t
-        rq = (lambda a, b: C("req", a, b)) if t == 0 else (lambda a, b: R("rq", t - 1, slice(a, b)))
+        r = (128 - s) % 128
+        rq = (lambda a, b: C("req", a, b)) if t == 0 else (lambda a, b: D("rq", t - 1, a, b))
+        u0, u1, u2, u3 = ("c%d%d" % (k, t) for k in range(4))
         cp(R("wu", t), IX(R("bks"), C("lbu", 0, 16) if t == 0 else R("lbr", t - 1)), s=False)
         ts(R("wh", t), R("wu", t), 1.0, None, A.mult)
         for c in range(0, 4096, CH):
-            cp(R("ga", t % 2, slice(c, c + CH)), IX(R("ct"), R("wu", t, slice(c // 16, (c + CH) // 16))))
+            cp(D("ga", t, c, c + CH), IX(R("ct"), D("wu", t, c // 16, (c + CH) // 16)))
         for h in range(4):
-            for u in (0, 1):
-                o = C("p0", 256 * u + 64 * h, 256 * u + 64 * h + 64)
-                mm([(o, C("tneg", r, r + 128), rq(64 * h, 64 * h + 64))] +
-                   [(o, C("e2", 14 - 2 * k, 142 - 2 * k), R("ga", t % 2, slice(1024 * h + 8 * u + k, 1024 * h + 1024, 16))) for k in range(8)])
-        ts(R("sq"), R("p0"), 0.0, None, A.not_equal, act=(F.Square, 0.0, 1.0))
-        a, b = C("p1", 0, 256), C("p1", 256, 512)
-        mm([(a, C("pm", 8, 136), C("sq", 0, 256)), (a, C("pm", 0, 128), C("sq", 256, 512))])
-        ts(R("fit"), a, 0.0, None, A.is_equal, act=(F.Relu, 1.0, -1.0))
-        mm([(b, R("t2k"), R("fit")), (b, R("ident"), R("wh", t))])
-        ts(R("val"), b, -2047.0, 0.0, A.add, A.max, act=(F.Relu, -2047.0, 1.0))
-        mm([(C("p1", 0, 16), C("e1", 15 - l, 143 - l), C("val", l, 256, 16)) for l in range(16)])
-        ts(R("wl"), C("p1", 0, 16), -1.0, 0.0, A.add, A.max)
-        cp(R("iw"), IX(R("ivs"), R("wl"))), cp(R("kw"), IX(R("kds"), R("wl")))
-        a, b = C("p2", 0, 256), C("p2", 256, 512)
-        mm([(a, R("w8"), R("iw")), (a, C("wn1", r, r + 128), rq(0, 256))])
-        mm([(b, R("w8x"), R("iw")), (b, C("wn2", r, r + 128), rq(0, 256))])
-        ts(R("sg"), a, 0.0, None, A.not_equal, act=(F.Sign, 0.0, 1.0))
-        tt(R("fitm"), b, R("sg"), A.is_equal)
-        c, d = C("p3", 0, 256), C("p3", 256, 512)
-        mm([(c, R("tt"), R("fitm"))])
-        mm([(a, hh, R("kw"))])
-        ts(R("ohm"), c, 0.0, None, A.max, act=(F.Relu, 0.0, 1.0))
-        mm([(d, hh, R("ohm"))])
-        cp(R("chi"), d)
-        tt(R("pr"), a, R("chi"), A.mult)
-        mm([(c, C("h32", s, s + 128), R("pr"))])
-        e = C("p2", 256, 384)
-        mm([(e, C(m, 15 - 8 * h - f + s, 143 - 8 * h - f + s), C(x, 128 * h, 128 * h + 128))
-            for h in (0, 1) for f, m, x in ((2, "e3", "val"), (3, "e1m", "ohm"))])
-        ts(R("kr", t, slice(256, 384)), e, C("col", 17), C("col", 18), A.min, A.add)
-        cp(R("kr", t, slice(0, 256)), c, s=False)
+            mmg([[(o, C("tp", r, r + 128), rq(64 * h, 64 * h + 64))] +
+                 [(o, C("e2", 14 - 2 * k, 142 - 2 * k), D("ga", t, 1024 * h + 8 * u + k, 1024 * h + 1024, 16)) for k in range(8)]
+                 for u in (0, 1) for o in [B(u0, 256 * u + 64 * h, 256 * u + 64 * h + 64)]])
+        ts(R("sq", t), B(u0, 0, 512), 0.0, None, A.not_equal, act=(F.Square, 0.0, 1.0))
+        a, b = B(u1, 0, 256), B(u1, 256, 512)
+        mm([(a, C("pm", 8, 136), D("sq", t, 0, 256)), (a, C("pm", 0, 128), D("sq", t, 256, 512))])
+        ts(R("fit", t), a, 0.0, 2048.0, A.is_equal, A.mult, act=(F.Relu, 2048.0, -2048.0))
+        mm([(b, ident, R("wh", t)), (b, R("tt"), R("fit", t))])
+        ts(R("val", t), b, -2047.0, 0.0, A.add, A.max, act=(F.Relu, -2047.0, 1.0))
+        mm([(B(u1, 0, 16), C("e1", 15 - l, 143 - l), D("val", t, l, 256, 16)) for l in range(16)])
+        ts(R("wl", t), B(u1, 0, 16), -1.0, 0.0, A.add, A.max)
+        cp(R("iw", t), IX(R("ivs"), R("wl", t))), cp(R("kw", t), IX(R("kds"), R("wl", t)))
+        a, b = B(u2, 0, 256), B(u2, 256, 512)
+        mmg([[(a, C("wn1", r, r + 128), rq(0, 256)), (a, R("w3", 0), R("iw", t))],
+             [(b, C("wn2", r, r + 128), rq(0, 256)), (b, R("w3", 1), R("iw", t))]])
+        ts(R("sg", t), a, 0.0, None, A.not_equal, act=(F.Sign, 0.0, 1.0))
+        tt(R("fitm", t), b, R("sg", t), A.is_equal)
+        c = B(u3, 0, 256)
+        mm([(c, hh, R("kw", t))])
+        cp(R("hk", t), c)
+        mm([(a, R("tt"), R("fitm", t))])
+        ts(R("ohm", t), a, 0.0, None, A.max, act=(F.Relu, 0.0, 1.0))
+        mm([(b, hh, R("ohm", t))])
+        tt(R("pr", t), b, R("hk", t), A.mult)
+        e = B(u3, 256, 384)
+        mm([(e, C(m, 15 - 8 * h - f + s, 143 - 8 * h - f + s), D(x, t, 128 * h, 128 * h + 128))
+            for h in (0, 1) for f, m, x in ((0, "e1", "val"), (1, "e1m", "ohm"))])
+        mm([(c, R("h32", slice(SHIFT[t], SHIFT[t] + 8)), R("pr", t))])
+        cp(R("kr", t), B(u3, 0, 384))
         if t:
-            send([R("kr", t)], [(-t, R("kr", t), R("kl", t - 1), "kr%d" % t, 4 if t == 1 else 0, 8)], 4000)
+            send([R("kr", t)], [(-t, T.kr[:, t], R("kl", t - 1), "kr%d" % t, 0, 8)], 3500)
 
-    def reply(t, pb):
-        kl = (lambda a, b: R("kr", 0, slice(a, b))) if t == 0 else (lambda a, b: R("kl", t - 1, slice(a, b)))
-        par[1], par[2] = t % 2, "r%d" % t
-        ts(R("rt", t), kl(256, 384), C("col", 25), C("col", 26), A.mult, A.add)
-        ts(R("kb"), kl(0, 256), 1.0, None, A.mult)
-        o = C(pb, 256, 512)
-        mm([(o, R("i256"), R("ka8")), (o, R("ident"), R("kb"))])
-        cp(R("kx"), o)
+    def kl(t, a, b):
+        return D("kr", 0, a, b) if t == 0 else D("kl", t - 1, a, b)
 
-    def state(z, pb, nxt, cur, old):
-        mmg([([(o, R("xx", h), R("rt", nxt))] if nxt is not None else []) + ([(o, R("yy", h), R("rt", cur))] if cur is not None else []) +
-             ([(o, R("ww"), R("zo", old, slice(128 * h, 128 * h + 128)))] if old is not None else [])
-             for h in (0, 1) for o in [C(pb, 128 * h, 128 * h + 128)]])
-        tt(R("zin", z), C(pb, 0, 256), R("cz"), A.max)
+    def kids(t):
+        o = B("x%d" % t, 0, 256)
+        mm([(o, R("ids", 3), R("ka")), (o, ident, kl(t, 0, 256))])
+        cp(R("kx", t), o)
 
-    def places(t, z, pb, cap):
-        scan(R("zs"), R("d0"), z, 0.0, A.mult, A.add)
-        o = C(pb, 0, 16)
-        mm([(o, R("ident"), R("ll"))] + [(o, C("ez", 15 - l, 143 - l), C("zs", l, 256, 16)) for l in range(16)])
-        cp(R("off", t), o, s=False)
-        ts(R("ofc", t), R("off", t), float(cap), None, A.min)
+    def state(z):
+        mmg([([(o, R("xx", h), kl(z, 256, 384))] if z < NT else []) + ([(o, R("yy", h), kl(z - 1, 256, 384))] if z else []) +
+             [(o, R("ww"), D("zo", old, 128 * h, 128 * h + 128)) for old in range(z - 1) if z < NT]
+             for h in (0, 1) for o in [B("z%d" % z, 128 * h, 128 * h + 128)]])
+        tt(R("zin", z), B("z%d" % z, 0, 256), R("cz"), A.max)
 
-    def test(t, n, cut, pa, pb, pc, pd):
-        par[1], par[2] = t % 2, "t%d" % t
-        sw, kx = IX(R("sw"), R("off", t)), R("kx")
-        ta, tc = ((lambda a, b, s=None: C("ta", a, b, s)), (lambda a, b, s=None: C("tc", a, b, s))) if n == 96 else (
-            (lambda a, b, s=None: R("ga", 0, slice(a, b, s))), (lambda a, b, s=None: R("ga", 1, slice(a, b, s))))
-        op({"v": (60 + SCT * CY * 256, lambda: V.tensor_copy(sw["ap"], kx["ap"]))}, [kx, R("off", t)], [R("sw")])
-        ts(C("ab", 0, n), C("sw", 0, n), 1.0 / 2048, -1023.5 / 2048, A.mult, A.add)
-        ts(C("bi", 0, n), C("sw", 0, n), 2047, None, A.bitwise_and)
-        cp(C("ab", n, 2 * n), C("bi", 0, n), s=False)
-        for a, b in cut:
-            cp(ta(16 * a, 16 * b), IX(R("tb", 0), C("ab", a, b)))
-            cp(tc(16 * a, 16 * b), IX(R("tb", t), C("ab", n + a, n + b)))
-        if t == NT - 1:
-            state(t + 1, pd, None, t, None)
-        for a, b in cut:
-            xs = C("xs", 6 * a, 6 * b)
-            cp(xs, sums(pa, ta, a, b, ("ident", "i256", "i64k")))
-            tt(C("ned", 6 * a, 6 * b), sums(pb, tc, a, b, ("ident", "i256", "i64k")), xs, A.not_equal)
-            tt(C("nee", 6 * a, 6 * b), sums(pc, tc, a, b, ("ni1", "ni256", "ni64k")), xs, A.not_equal)
-        for a, b in cut:
+    def places(t, z):
+        scan(R("zs"), R("d0"), z, A.mult, A.add)
+        o = B("l%d" % t, 0, 16)
+        mm([(o, C("ez", 15 - l, 143 - l), C("zs", l, 256, 16)) for l in range(16)])
+        ts(R("off", t), o, 1023.0, None, A.add)
+        ts(R("ofc", t), R("off", t), 96.0, None, A.min)
+
+    def test(t):
+        sw, kx, n = IX(R("sw"), R("off", t)), R("kx", t), 96
+        i0 = op({"v": (60 + SCT * CY * 256, lambda: V.tensor_copy(sw["ap"], kx["ap"]))}, [kx, R("off", t)], [R("sw")])
+        ts(D("ab", t, 0, n), C("sw", 0, n), 1.0 / 2048, -1023.5 / 2048, A.mult, A.add)
+        ts(R("bi"), C("sw", 0, n), 2047, None, A.bitwise_and)
+        cp(D("ab", t, n, 2 * n), R("bi"), s=False)
+        for a, b in CUT:
+            cp(D("ta", t, 16 * a, 16 * b), IX(R("lfs"), D("ab", t, a, b)))
+            cp(D("tc", t, 16 * a, 16 * b), IX(R("tb", t - 1) if t else R("lfs"), D("ab", t, n + a, n + b)))
+        for a, b in CUT:
             w = 2 * (b - a)
-            mm([(C(pa, a, b), R(m), C(x, 6 * a + w * j + h, 6 * a + w * j + w, 2))
-                for m, x in (("l1", "ned"), ("l2", "nee")) for j in range(3) for h in (0, 1)])
-        a, fp, fm, rr = C(pa, 0, n), C("fpm", 0, n), C("fpm", n, 2 * n), C("rr", 0, n)
-        ts(rr, a, 256 * MAGIC, 256 * MAGIC, A.add, A.subtract)
-        tt(fp, a, rr, A.is_equal)
-        ts(fm, rr, 1.0, None, A.is_lt, act=(F.Relu, 1.0, -1.0))
-        a = C(pc, 0, n)
-        mm([(a, R("rw"), fm), (a, R("rw"), fp)])
-        tt(C("res", 0, n), a, C("cres", 0, n), A.max)
-        tt(R("zo", t), IX(C("res", 0, n + 16), R("ofc", t)), R("zin", t + 1), A.min)
-        a, b = C(pb, 0, n), C(pb, n, 2 * n)
-        mmg([[(a, R("tt"), fp), (a, R("nu"), fm)], [(b, R("tt"), fm), (b, R("nui"), fp)]])
-        ts(C("oh", 0, 2 * n), C(pb, 0, 2 * n), 0.0, None, A.max, act=(F.Relu, 0.0, 1.0))
-        a = C(pa, 0, n)
-        mm([(a, R("rp"), C("oh", 0, n)), (a, R("rm"), C("oh", n, 2 * n))])
-        cp(C("rs2", 0, n), a)
-        cp(R("zm", t), IX(C("rs2", 0, n + 16), R("ofc", t)))
+            for sn in (0, 1):
+                u = "d%d%d%d" % (t, sn, a)
+                for x, neg in (("ta", 1), ("tc", 2 * sn - 1)):
+                    mm([(B(u, w * j, w * j + w), R("hm", HM.index(neg * v)), D(x, t, 16 * a + d, 16 * b, 8)) for d, (j, v) in enumerate(KID)],
+                       start=x == "ta", stop=x == "tc")
+                ts(R("nd", t % 2, slice(sn, 6, 2), slice(a, b)), B(u, 0, 3 * w), col(14 - sn) if t else 0.0, None, A.not_equal,
+                   act=(F.Square, col(13 + sn) if t else 0.0, 1.0))
+            u = "n%d%d" % (t, a)
+            both, plus, minus = B(u, 0, w), B(u, 0, w // 2), B(u, w // 2, w)
+            mm([(both, R("l1"), R("nd", t % 2, slice(2 * j, 2 * j + 2), slice(a, b), h)) for h in (0, 1) for j in range(3)] +
+               [(both, R("l2"), R("nd", t % 2, slice(2 * j + 1, 2 * j + 3), slice(a, b), h)) for h in (0, 1) for j in range(2)] +
+               [(o, R("l2"), R("nd", t % 2, k, slice(a, b), h)) for h in (0, 1) for o, k in ((plus, 5), (minus, 0))])
+            ts(R("fpm", t, al, slice(a, b)), both, 0.5, None, A.is_lt, act=(F.Relu, 1.0, -1.0))
+        fp, fm, op_, om = R("fpm", t, 0), R("fpm", t, 1), D("oh", t, 0, n), D("oh", t, n, 2 * n)
+        r = B("r%d" % t, 0, n)
         if t < NT - 1:
-            places(t + 1, R("zo", t), pc, 96)
+            mm([(r, R("xx", 0), C("ones", 0, n))], stop=False, after=[i0])
+            mm([(r, R("rw"), fm), (r, R("rw"), fp)], start=False)
+            tt(C("res", 0, n), r, R("cres"), A.max)
+            tt(R("zo", t), IX(R("res"), R("ofc", t)), R("zin", t + 1), A.min)
+            places(t + 1, R("zo", t))
+        a, b = B("f%d" % t, 0, n), B("f%d" % t, n, 2 * n)
+        mmg([[(a, R("tt"), fp), (a, R("nu"), fm)], [(b, R("tt"), fm), (b, R("nui"), fp)]])
+        ts(R("oh", t), B("f%d" % t, 0, 2 * n), 0.0, None, A.max, act=(F.Relu, 0.0, 1.0))
+        first = [(a, C("e1m", 10, 138), op_), (a, C("e1m", 10, 138), om), (a, C("e1", 9, 137), op_)]
+        if t < NT - 1:
+            mm(first)
+            cp(D("rs2", t, 0, n), a)
+            cp(R("zm", t), IX(R("rs2", t), R("ofc", t)))
+        else:
+            mm(first + [(a, R("rw"), op_), (a, R("rw"), om)])
+            tt(C("res", 0, n), a, R("cres"), A.max)
+            tt(R("zo", t), IX(R("res"), R("ofc", t)), R("zin", t + 1), A.min)
 
-    ts(R("ka8"), IX(R("kds"), R("lvu")), 8.0, None, A.mult)
-    home = (96, CUT, "p4", "p5", "p6", "p7")
-    own_table()
-    if ORD[0] == 0:
-        unpack(1)
-    claim(0)
-    reply(0, "p7"), state(0, "p7", 0, None, None), places(0, R("zin", 0), "p6", 96)
-    claim(1)
-    if ORD[0] == 1:
-        unpack(1, 2)
-    reply(1, "p7"), state(1, "p7", 1, 0, None)
-    test(0, *home)
-    claim(2)
-    if ORD[1] == 0:
-        unpack(2, 2)
-    reply(2, "p7"), state(2, "p7", 2, 1, 0)
-    test(1, *home)
-    claim(3)
-    if ORD[1] == 1:
-        unpack(2, 0)
-    reply(3, "p7"), state(3, "p7", 3, 2, 1)
-    unpack(3, 1)
-    test(2, *home)
-    test(3, *home)
-    o = R("p1", slice(0, 256), part=slice(0, 40))
-    mmg([[(o, R("sel", NT), R("ones"))] + [(o, R("sel", t), R(z, t)) for t in range(NT - 1) for z in ("zo", "zm")]], stop=False)
-    mmg([[(o, R("sel", NT - 1), R("zo", NT - 1))]], start=False, stop=False)
-    mmg([[(o, R("sel", NT - 1), R("zm", NT - 1))]], start=False)
+    mul(R("ka"), IX(R("kds"), R("lvu")), 0.5)
+    for t in range(NT):
+        claim(t)
+        if t:
+            unpack(t)
+        kids(t)
+    state(0)
+    ts(R("z0"), R("zin", 0), col(17), None, A.min)
+    places(0, R("z0"))
+    for t in range(NT):
+        state(t + 1)
+        test(t)
+    o = B("y", 0, 256, slice(0, 40))
+    mm([(o, R("sel", NT + 1), C("ones", 0, 256))] + [(o, R("sel", t), R(z, t)) for t in range(NT - 1) for z in ("zo", "zm")], stop=False)
+    mm([(o, R("sel", NT - 1), R("zo", NT - 1))], start=False)
     ysb = R("ysb", part=slice(0, 40))
     cp(ysb, o)
-    op({"y": (60.0, lambda: g.sync.dma_start(T.y[:], ysb["ap"]).then_inc(T.sem.st, 16))}, [ysb], [], sem=(T.sem.st, 16, 2000))
+    end = dma([(T.y[:], ysb["ap"])], [ysb], [], 2000, "y")
+    return ops, uses, sent[0], ops[end]["sem"]
 
+
+def order_calls(ops, uses):
     n = len(ops)
-    succ = [[] for _ in ops]
-    for i, o in enumerate(ops):
-        for j in o["deps"]:
-            succ[j].append(i)
     cost = [{e: c for e, (c, f) in o["var"].items()} for o in ops]
     lat = [o["sem"][2] if o["sem"] else LAT for o in ops]
+    rs = np.random.RandomState(1)
 
-    pred = [list(o["deps"]) for o in ops]
-
-    def place(key, back, vbias):
-        before, behind = (succ, pred) if back else (pred, succ)
+    def place(deps, succ, key, back, vbias):
+        before, behind = (succ, deps) if back else (deps, succ)
         left = [len(x) for x in before]
         ready = [i for i in range(n) if not left[i]]
         busy, eng, start, fin = {e: [] for e in "vstpyn"}, [""] * n, [0.0] * n, [0.0] * n
@@ -535,7 +480,8 @@ def rank_program(g, core, T, topo):
                 t = 0.0
                 for j in before[i]:
                     a, b = (i, j) if back else (j, i)
-                    hard = ops[a]["sem"] or eng[j] != e or (ops[b]["deps"][a] and e != "t")
+                    raw = deps[b][a]
+                    hard = raw is not None and (ops[a]["sem"] or eng[j] != e or (raw and e != "t"))
                     t = max(t, fin[j] + (lat[a] if hard else 0.0))
                 k = 0
                 for k, (s0, s1) in enumerate(busy[e] + [(1e18, 1e18)]):
@@ -553,35 +499,84 @@ def rank_program(g, core, T, topo):
                     ready.append(j)
         return max(fin), eng, start, fin
 
-    if "plan" not in INFO:
-        rs, plan = np.random.RandomState(1), None
-        prio = [0.0] * n
-        for i in range(n - 1, -1, -1):
-            prio[i] = min(cost[i].values()) + lat[i] + max([prio[j] for j in succ[i]] + [0.0])
-        key = [-x - BONUS.get(o["ph"], 0.0) for x, o in zip(prio, ops)]
-        INFO["g"] = (prio, succ, [o["tag"] for o in ops])
-        for k in range(TRIES):
+    def search(deps, key, tries):
+        succ = [[] for _ in ops]
+        for i, d in enumerate(deps):
+            for j in d:
+                succ[j].append(i)
+        plan = None
+        for k in range(tries):
             vb = float(rs.choice(VB))
-            r = place(key, False, vb)
+            r = place(deps, succ, key, False, vb)
             if plan is None or r[0] < plan[0]:
                 plan = r
             if k % 3 == 0:
                 sh = rs.randn(40) * float(rs.choice([0, 1000, 3000])) * (rs.rand(40) < 0.3)
                 key = list(rs.rand(n) * float(rs.choice([100, 300, 1000])) + np.array(plan[2]) + sh[np.arange(n) * 40 // n])
             else:
-                b = place([-x for x in r[3]], True, vb)
+                b = place(deps, succ, [-x for x in r[3]], True, vb)
                 key = list(-np.array(b[3]))
-        INFO["plan"] = (plan[0], plan[1], sorted(((i, plan[2][i]) for i in range(n)), key=lambda x: (x[1], x[0])))
-    end, eng, order = INFO["plan"]
-    INFO["r"] = (ops, cost, lat)
-    INFO["order"] = [(st, eng[i], ops[i]["tag"], cost[i][eng[i]]) for i, st in order]
+        return plan
+
+    def banks(plan):
+        deps, bank, held = [dict(o["deps"]) for o in ops], {}, [None] * 8
+
+        def needs(a, b):
+            todo, seen = [a], {a}
+            while todo:
+                x = todo.pop()
+                if x == b:
+                    return True
+                for y in deps[x]:
+                    if y not in seen:
+                        seen.add(y)
+                        todo.append(y)
+            return False
+        for u in sorted(uses, key=lambda u: plan[2][uses[u][0]]):
+            free = sorted(range(8), key=lambda k: -1 if held[k] is None else plan[3][held[k]])
+            k = [k for k in free if held[k] is None or not needs(held[k], uses[u][0])][0]
+            if held[k] is not None:
+                deps[uses[u][0]][held[k]] = True
+            bank[u], held[k] = "p%d" % k, uses[u][-1]
+        return deps, bank
+
+    prio = [0.0] * n
+    for i in range(n - 1, -1, -1):
+        prio[i] += min(cost[i].values()) + lat[i]
+        for j in ops[i]["deps"]:
+            prio[j] = max(prio[j], prio[i])
+    plan = search([o["deps"] for o in ops], [-x for x in prio], TRIES)
+    INFO["free"] = plan[0]
+    best = None
+    for k in range(ROUNDS):
+        deps, bank = banks(plan)
+        plan = search(deps, list(plan[2]), TRIES)
+        if best is None or plan[0] < best[0][0]:
+            best = (plan, deps, bank)
+    plan, deps, bank = best
+    INFO["bank"] = bank
+    INFO["plan"] = (plan[0], plan[1], sorted(range(n), key=lambda i: (plan[2][i], i)), deps)
+    INFO["show"] = [(plan[2][i], plan[3][i], plan[1][i], ops[i]["tag"]) for i in range(n)]
+
+
+def rank_program(g, core, T, topo):
+    rank = T.rank_of(core)
+    if rank is None:
+        return
+    if "plan" not in INFO:
+        order_calls(*record(g, core, rank, T, topo)[:2])
+    ops, uses, sent, stored = record(g, core, rank, T, topo)
+    end, eng, order, deps = INFO["plan"]
+    Q = {"v": g.vector, "s": g.scalar, "t": g.tensor, "p": g, "y": g.sync}
 
     pos, seen, waits, need = {}, {}, [], set()
-    for k, (i, st) in enumerate(order):
+    for k, i in enumerate(order):
         pos[i] = k
         e, w = eng[i], {}
         if e != "n":
-            for j, raw in ops[i]["deps"].items():
+            for j, raw in deps[i].items():
+                if raw is None:
+                    continue
                 if ops[j]["sem"]:
                     if (e, j) not in seen:
                         seen[(e, j)] = 1
@@ -595,7 +590,7 @@ def rank_program(g, core, T, topo):
                     need.add(j)
         waits.append(w)
     count, cnt = {}, dict.fromkeys("vstp", 0)
-    for (i, st), w in zip(order, waits):
+    for i, w in zip(order, waits):
         e = eng[i]
         if e == "n":
             continue
@@ -609,5 +604,5 @@ def rank_program(g, core, T, topo):
             cnt[e] += 1
             count[i] = cnt[e]
             r.then_inc(T.sem[e], 1)
-    g.wait_ge(T.sem.snt, sent[0])
-    g.sync.wait_ge(T.sem.st, 16)
+    g.wait_ge(T.sem.snt, sent)
+    g.sync.wait_ge(stored[0], stored[1])

@@ -6,42 +6,41 @@ A = AluOpType
 F = ActivationFunctionType
 N, NT, PW, WIN = 8, 4, 342, 1120
 SHIFT = [0, 1, 3, 6]
-KID = [(0, 1), (0, 240), (0, 65536), (1, 1), (1, 240), (1, 65536), (2, 241), (2, 65536)]
-HM = [1, 240, 241, 65536, -1, -240, -241, -65536]
-OFFS = 112.0 * 65777
+STEP = 512.0
+MAGIC = 12582912.0
 
 _B = {}
 for _d, _l in (
-    ("bfloat16", dict(lfs=2048, ivs=1024, ones=512, bd8=8, bdw=256, n8=(8, 8), w3=(2, 8, 16), wd=64, wp=64, cneg=128, tp=256, wn1=256, wn2=256,
-                      e2=144, pm=136, tt=128, nu=128, nui=128, nbd=(8, 16), e1=256, e1m=256, ez=144, xx=(2, 8, 16), yy=(2, 8, 16), ww=(8, 16),
-                      rw=(8, 16), l1=128, l2=128, hm=(8, 8, 16), ids=(6, 128), zt=128, sel=(6, 8, 5), dt3=(64, 16), ct=1024, req=256,
-                      rq=(3, 256), ga=(4, 4096), ta=(4, 1536), tc=(4, 1536), sq=(4, 512), fit=(4, 256), iw=(4, 256), sg=(4, 256),
-                      fitm=(4, 256), ohm=(4, 256), nd=(2, 6, 96, 2), fpm=(4, 2, 96), oh=(4, 192), rs2=(4, 112), zm=(3, 256))),
-    ("float32", dict(cc=136, gc=256, ln=256, lm=96, pf=8, col=24, q4=4, oh2=2, rs=512, pm1=512, dl=512, pm2=512, ck=(64, 2), h32=(16, 16),
-                     hk=(4, 256), pr=(4, 256), res=112, cres=96, cz=256, kx=(4, 256), zin=(5, 256), ysb=256)),
-    ("float16", dict(wh=(4, 256), val=(4, 256), kw=(4, 256), ka=256, d0=256, z0=256, zo=(4, 256), zs=256, kr=(4, 384), kl=(3, 384))),
-    ("int32", dict(kds=1024, bks=1024, lvi=16, lbi=64, pi=8, sw=WIN, bi=96, pk=PW, pl=(3, PW), tb=(3, 2048))),
-    ("uint16", dict(lvu=16, lbu=64, lbr=(3, 16), wu=(4, 256), wl=(4, 16), off=(4, 16), ofc=(4, 16), ab=(4, 192))),
+    ("bfloat16", dict(lf2=4096, ivs=1024, ones=512, bd8=8, bdw=256, b4=(4, 16), n4=(4, 32), n8=(8, 8), w3=(2, 8, 16), wd=64, wp=64, cneg=128,
+                      tp=256, wn1=256, wn2=256, e2=144, pm=136, tt=128, t2=128, nu=128, nbd=128, e1=256, e1m=256, ez=144, xx=(4, 8, 16),
+                      yy=(4, 8, 16), ww=(8, 16), rw=(2, 12, 16), l1=(4, 16, 2), hm=(17, 8, 16), ids=(6, 128), zt=128, sel=(6, 8, 5), dt3=(64, 16),
+                      ct=1024, req=256, rq=(3, 256), ga=(4, 4096), ta=(4, 2, 1536), sq=(4, 512), fit=(4, 256), iw=(4, 256), fitm=(4, 256),
+                      ohm=(4, 256), nd=(4, 2, 96, 2), fpm=(4, 2, 96), oh=(4, 192), rs2=(4, 112), zm=(3, 256))),
+    ("float32", dict(cc=136, gc=256, g4=64, g32=128, ln=256, lm=96, pf=12, col=24, q4=4, oh2=2, rs=512, pm1=512, dl=512, pm2=512, ck=(2, 64),
+                     h32=(16, 16), hk=(4, 256), pr=(4, 256), res=112, cres=96, cz=256, kx=(4, 256), zin=(5, 256), ysb=256)),
+    ("float16", dict(wh=(4, 256), val=(4, 256), kw=(4, 256), ka=256, d0=256, z0=256, zo=(4, 256), zs=256, kr=(4, 320), kl=(3, 320),
+                     kv=(4, 64), ku=(3, 64))),
+    ("int32", dict(kds=1024, bks=1024, lvi=16, lbi=64, pi=13, sw=WIN, bi=96, pk=PW, pl=(3, PW), tb=6144)),
+    ("uint16", dict(lvu=16, lbu=64, lbr=(3, 16), wu=(4, 256), wl=(4, 16), off=(4, 16), ofc=(4, 16), ab=(4, 2, 96))),
 ):
     for _k, _s in _l.items():
         _B[_k] = ("sbuf", [128] + (list(_s) if isinstance(_s, tuple) else [_s]), _d)
-_B["pd"] = ("dram", [128 + 16 * SHIFT[-1], PW], "int32")
+_B["pd"] = ("dram", [240, PW], "int32")
 for _k in range(8):
     _B["p%d" % _k] = ("psum", [128, 512], "float32")
 SCRATCH = _B
 SEMAPHORES = (["v", "s", "t", "p", "snt"] + ["ld%d" % i for i in range(12)] +
-              [x + str(t) for x in ("lb", "rq", "pk", "kr") for t in (1, 2, 3)])
+              [x + str(t) for x in ("lb", "rq", "pk", "kr", "kv") for t in (1, 2, 3)])
 
-CY, PC, LAT, GC, SCT = 0.9, 0.45, 150.0, 1.56, 3.8
-CH, CUT, ROUNDS, TRIES = 1024, ((0, 32), (32, 64), (64, 96)), 8, 150
-VB = [1.0, 1.5, 2.0, 3.0]
+CY, PC, LAT, GC, SCT, DLAT, DRATE, RLAT, RRATE = 0.9, 0.45, 150.0, 1.56, 3.8, 1900.0, 300.0, 2000.0, 90.0
+CH, CUT, ROUNDS, TRIES, HEAT, SEED = 1024, ((0, 32), (32, 64), (64, 96)), 2, 9000, 100.0, 1
 INFO = {}
 
 
 def record(g, core, rank, T, topo):
     V, S, P = g.vector, g.scalar, g.tensor
     ops, acc, uses, sent, nld = [], {}, {}, [0], [0]
-    al = slice(None)
+    al, half = slice(None), (slice(0, 64), slice(64, 128))
 
     def R(name, *idx, part=al):
         shape = SCRATCH[name][1][1:]
@@ -52,7 +51,8 @@ def record(g, core, rank, T, topo):
         else:
             for k in el.tolist():
                 m |= 1 << k
-        return dict(ap=T[name][(part,) + idx], b=name, m=m, n=len(el), w=2 if "16" in SCRATCH[name][2] else 4, off=None, ps=False)
+        return dict(ap=T[name][(part,) + idx], b=name, m=m, n=len(el), w=2 if "16" in SCRATCH[name][2] else 4, off=None, ps=False,
+                    h=3 if part not in half else 1 + half.index(part))
 
     def C(name, a, b=None, s=None):
         return R(name, slice(a, a + 1 if b is None else b, s))
@@ -61,12 +61,12 @@ def record(g, core, rank, T, topo):
         return R(name, k, slice(a, b, s))
 
     def B(use, a, b, part=al, step=1):
-        return dict(ap=T[INFO.get("bank", {}).get(use, "p0")][part, a:b:step], b=use, m=1, n=len(range(a, b, step)), w=4, off=None, ps=True)
+        return dict(ap=T[INFO.get("bank", {}).get(use, "p0")][part, a:b:step], b=use, m=1, n=len(range(a, b, step)), w=4, off=None, ps=True, h=3)
 
     def IX(win, off):
         return dict(win, ap=win["ap"].indirect(off["ap"]), n=16 * off["n"], off=off)
 
-    def op(var, reads, writes, sem=None, after=(), behind=(), tag=""):
+    def op(var, reads, writes, sem=None, after=(), behind=(), tag="", move=0.0):
         i, deps = len(ops), {}
         reads = [r for r in reads if isinstance(r, dict)]
         reads = reads + [r["off"] for r in reads if r["off"]]
@@ -74,26 +74,26 @@ def record(g, core, rank, T, topo):
             l = acc.setdefault(x["b"], [])
             if x["ps"]:
                 uses.setdefault(x["b"], []).append(i)
-                for j, m, pw in l[::-1]:
+                for j, m, pw, h in l[::-1]:
                     if j != i:
                         deps[j] = deps.get(j, False) or pw or wr
                         break
-                for j, m, pw in l[::-1]:
+                for j, m, pw, h in l[::-1]:
                     if j != i and pw and not wr:
                         deps[j] = True
                         break
             else:
-                for j, m, pw in l:
-                    if j != i and (pw or wr) and m & x["m"]:
+                for j, m, pw, h in l:
+                    if j != i and (pw or wr) and m & x["m"] and h & x["h"]:
                         deps[j] = True
                 if wr:
-                    l[:] = [e for e in l if e[1] & ~x["m"]]
-            l.append((i, x["m"], wr))
+                    l[:] = [e for e in l if e[1] & ~x["m"] or e[3] & ~x["h"]]
+            l.append((i, x["m"], wr, x["h"]))
         for j in after:
             deps[j] = True
         for j in behind:
             deps.setdefault(j, None)
-        ops.append(dict(var=var, deps=deps, sem=sem, tag=tag or (writes[0]["b"] if writes else "")))
+        ops.append(dict(var=var, deps=deps, sem=sem, move=move, tag=tag or (writes[0]["b"] if writes else "")))
         return i
 
     def ap(x):
@@ -121,6 +121,9 @@ def record(g, core, rank, T, topo):
 
     def lin(o, i, a, b):
         return ts(o, i, a, b, A.mult, A.add, act=(F.Identity, b, a))
+
+    def relu(o, i):
+        return ts(o, i, 0.0, None, A.max, act=(F.Relu, 0.0, 1.0))
 
     def cp(o, i, s=True):
         var = {"v": (vc(o, i), lambda: V.tensor_copy(o["ap"], i["ap"]))}
@@ -169,14 +172,15 @@ def record(g, core, rank, T, topo):
 
     last = []
 
-    def dma(pairs, reads, writes, lat, tag=""):
+    def dma(pairs, reads, writes, size, tag="", after=()):
         s = T.sem["ld%d" % nld[0]]
         nld[0] += 1
 
         def f():
             for a, b in pairs:
                 g.sync.dma_start(a, b).then_inc(s, 16)
-        last[:] = [op({"y": (60.0 * len(pairs), f)}, reads, writes, sem=(s, 16 * len(pairs), lat), behind=last, tag=tag)]
+        last[:] = [op({"y": (60.0 * len(pairs), f)}, reads, writes, sem=(s, 16 * len(pairs), DLAT), after=after, behind=last, tag=tag,
+                      move=150 * len(pairs) + size / DRATE)]
         return last[0]
 
     def peer(d):
@@ -185,9 +189,7 @@ def record(g, core, rank, T, topo):
     def emask(d, a, b):
         return sum(1 << e for e in topo.engines(core, peer(d))[a:b])
 
-    sends = []
-
-    def send(src, trs, lat):
+    def send(src, trs, behind=()):
         def f():
             l = []
             for d, s, dst, sem, a, b in trs:
@@ -195,22 +197,22 @@ def record(g, core, rank, T, topo):
                 l.append(RemoteDMATransfer(dst_ids=[DstId(rid=rid, pnc=pid)], dma_engine_mask=emask(d, a, b), remote_sem=T.sem[sem],
                                            srcs=[s], dsts=[dst["ap"]]))
             g.remote_dma_fused(l, local_sem=T.sem.snt)
-        i = op({"p": (500.0, f)}, src, [], tag="send", behind=sends[-1:])
-        sends.append(i)
+        i = op({"p": (500.0, f)}, src, [], tag="send", behind=behind, move=400 + sum(128 * x[2]["n"] * x[2]["w"] for x in trs) / RRATE)
         for d, s, dst, sem, a, b in trs:
             sent[0] += b - a
-            op({"n": (0.0, None)}, [], [dst], sem=(T.sem[sem], b - a, lat), after=[i], tag="arr")
+            op({"n": (0.0, None)}, [], [dst], sem=(T.sem[sem], b - a, RLAT), after=[i], tag="arr")
+        return i
 
-    dma([(T.ivs[:], T.iv[:])], [], [R("ivs")], 2700)
-    dma([(T.lvi[:], T.lv[:]), (T.lbi[:, 0:16], T.lb[:])], [], [R("lvi"), C("lbi", 0, 16)], 3000)
-    dma([(T.bks[:], T.bk[:])], [], [R("bks")], 4300)
+    dma([(T.ivs[:], T.iv[:])], [], [R("ivs")], 1 << 18)
+    dma([(T.lvi[:], T.lv[:]), (T.lbi[:, 0:16], T.lb[:])], [], [R("lvi"), C("lbi", 0, 16)], 0)
     lb = []
     for t in (1, 2, 3):
         s = 16 * SHIFT[t]
         lb += [(T.lbi[s:128, 16 * t:16 * t + 16], T.lb[0:128 - s, :]), (T.lbi[0:s, 16 * t:16 * t + 16], T.lb[128 - s:128, :])]
-    dma(lb, [], [C("lbi", 16, 64)], 4500)
-    dma([(T.lfs[:], T.lf[:])], [], [R("lfs")], 5700)
-    dma([(T.kds[:], T.kd[:])], [], [R("kds")], 7200)
+    dma(lb, [], [C("lbi", 16, 64)], 0)
+    dma([(T.bks[:], T.bk[:])], [], [R("bks")], 1 << 19)
+    dma([(T.lf2[:, 0:2048], T.lf[:])], [], [C("lf2", 0, 2048)], 1 << 19)
+    dma([(T.kds[:], T.kd[:])], [], [R("kds")], 1 << 19)
 
     def col(k):
         return C("col", k)
@@ -220,11 +222,10 @@ def record(g, core, rank, T, topo):
     asel(R("bd8"), R("bd8"), A.is_ge, 0.0, [[-16, 8]], 0, 1), asel(R("bd8"), R("bd8"), A.is_ge, 0.0, [[16, 8]], 15, -1)
     bd8 = R("bd8")
     iota(R("cc"), [[1, 136]], -8, 0)
-    for k, (sh, m) in enumerate([(0, 1), (1, 1), (2, 1), (3, 1), (4, 7), (0, 15), (2, 3)]):
+    for k, (sh, m) in enumerate([(0, 1), (1, 1), (2, 1), (3, 1), (4, 7), (0, 15), (2, 3), (4, 3), (6, 1), (1, 63), (5, 3), (1, 15)]):
         ts(C("pi", k + 1), C("pi", 0), sh, m, A.arith_shift_right, A.bitwise_and)
-    cp(C("pf", 0, 4), C("pi", 1, 5), s=False), cp(C("pf", 4, 7), C("pi", 5, 8), s=False)
-    ts(C("pi", 1), C("pi", 0), 1, None, A.arith_shift_right), cp(C("pf", 7), C("pi", 1), s=False)
-    b3, pg, p16, p4, ph = C("pf", 3), C("pf", 4), C("pf", 5), C("pf", 6), C("pf", 7)
+    cp(C("pf", 0, 4), C("pi", 1, 5), s=False), cp(C("pf", 4, 12), C("pi", 5, 13), s=False)
+    b3, pg, p16, p4, ph = C("pf", 3), C("pf", 4), C("pf", 5), C("pf", 6), C("pf", 9)
     for b, v in enumerate((8.0, 64.0, 4096.0)):
         lin(col(b), C("pf", b), v - 1, 1.0), lin(col(3 + b), C("pf", b), 1 - v, v)
     lin(C("col", 6, 10), C("pf", 0, 4), -2.0, 1.0)
@@ -234,7 +235,7 @@ def record(g, core, rank, T, topo):
     mul(R("n8", al, slice(4, 8)), R("n8", al, slice(0, 4)), col(5)), mul(R("n8", al, slice(0, 4)), R("n8", al, slice(0, 4)), col(2))
     lo, hi = (R("w3", 0, al, slice(8 * k, 8 * k + 8)) for k in range(2))
     mul(lo, R("n8"), col(10)), ts(hi, R("n8"), b3, 2.0 ** 24, A.mult, A.mult), mul(R("wd"), R("n8"), col(9))
-    cp(R("w3", 1, al, slice(8, 16)), lo), cp(R("w3", 1, al, slice(0, 8)), hi)
+    mul(R("w3", 1, al, slice(8, 16)), lo, 2.0 ** -26), mul(R("w3", 1, al, slice(0, 8)), hi, 2.0 ** -26)
     ts(col(11), col(0), col(1), col(2), A.mult, A.mult)
     ts(R("wp"), C("cc", 8, 72), ph, col(11), A.is_equal, A.mult)
     ms(R("ones"), 1.0), ms(R("cneg"), -2.0 ** 41)
@@ -250,33 +251,43 @@ def record(g, core, rank, T, topo):
     oh0, oh1 = C("oh2", 0), C("oh2", 1)
     for k in (0, 1):
         mul(C("tp", k, 256, 2), C("bdw", k, 256, 2), C("q4", k))
-        ts(R("wn%d" % (k + 1)), R("bdw"), C("q4", 2 + k), 2.0 ** 24, A.mult, A.mult)
+        ts(R("wn%d" % (k + 1)), R("bdw"), C("q4", 2 + k), 2.0 ** (24 - 26 * k), A.mult, A.mult)
     asel(R("e2"), C("tp", 0, 144), A.is_ge, 0.0, [[0, 9], [1, 16]], -14, 0)
     ts(col(12), pg, 8.0, ph, A.mult, A.add), ts(R("pm"), R("cc"), col(12), None, A.is_equal)
     mul(R("nbd"), C("bdw", 0, 128), -1.0)
-    asel(R("nu"), R("nbd"), A.is_gt, 0.0), asel(R("nui"), R("nbd"), A.is_ge, 0.0), asel(R("tt"), R("nu"), A.not_equal, 1.0)
+    asel(R("nu"), R("nbd"), A.is_gt, 0.0), asel(R("tt"), R("nu"), A.not_equal, 1.0)
     asel(R("e1"), R("bdw"), A.is_equal, 0.0, [[0, 16], [1, 16]], -15, 0), mul(R("e1m"), R("e1"), p16)
+    iota(R("g4"), [[1, 4], [0, 16]], 0, 0)
+    ts(R("b4"), R("g4"), C("pf", 7), None, A.is_equal)
+    lin(col(13), C("pf", 8), -2.0, 1.0), lin(col(14), C("pf", 8), 2.0, -1.0)
     cp(R("hm", 0, al, 0), bd8)
+    for k in (0, 1):
+        mul(R("hm", 1 + k, slice(0, 4), 0), R("b4", al, 0), col(13 + k)), cp(R("hm", 1 + k, slice(4, 8), 0), R("b4", al, 0))
     for b in range(4):
-        mul(R("hm", 0, al, slice(1 << b, 2 << b)), R("hm", 0, al, slice(0, 1 << b)), col(6 + b))
+        mul(R("hm", slice(0, 3), al, slice(1 << b, 2 << b)), R("hm", slice(0, 3), al, slice(0, 1 << b)), col(6 + b))
     hh = R("hm", 0)
     for k in (0, 1):
         mul(R("h32", slice(8 * k, 8 * k + 8)), hh, 0.0625)
     for k in range(1, 6):
         mul(R("ids", k), ident, 16.0 ** k, more=(se(R("ids", k), R("zt"), A.not_equal, 16.0 ** k, ((1, 128),), 0, -1), [R("zt")]))
 
-    for k in range(1, 8):
-        mul(R("hm", k), hh, float(HM[k]))
-    ts(R("l1"), hh, 0.0, None, A.max, act=(F.Relu, 0.0, 1.0)), ts(R("l2"), R("hm", 4), 0.0, None, A.max, act=(F.Relu, 0.0, 1.0))
-    mul(col(13), oh0, OFFS), mul(col(14), oh0, -OFFS)
-    two, s2 = [[-16, 8], [0, 2]], slice(0, 2)
+    for k in (1, 2, 4):
+        mul(R("hm", slice(1 + 2 * k, 1 + 4 * k)), R("hm", slice(1, 1 + 2 * k)), STEP ** k)
+    for k in (0, 1):
+        relu(R("l1", al, al, k), R("hm", 1 + k, slice(0, 4)))
+    iota(R("g32"), [[1, 4], [0, 32]], 0, 0)
+    ts(R("n4"), R("g32"), C("pf", 10), -1.0, A.is_equal, A.mult)
+    asel(R("t2"), R("n4"), A.is_gt, 0.0), asel(R("t2"), R("t2"), A.not_equal, 1.0)
+    lin(col(18), C("pf", 0), 1.0, -1.0)
+    two, s2, mid = [[-16, 8], [0, 2]], slice(0, 2), slice(4, 8)
     ms(R("xx")), ms(R("yy")), ms(R("ww")), ms(R("rw")), ms(R("ez"))
-    iota(R("xx", 1, al, s2), [[0, 8], [1023, 2]], 1, 0), iota(R("ww", al, s2), [[0, 16]], -2 ** 21, 0)
+    iota(R("xx", 3, al, s2), [[0, 8], [1023, 2]], 1, 0), iota(R("ww", al, s2), [[0, 16]], -2 ** 21, 0)
     asel(R("ww", al, s2), R("ww", al, s2), A.is_equal, 0.0, two, -3, 1)
-    for h in (0, 1):
-        asel(R("xx", h, al, s2), R("xx", 1, al, s2), A.is_equal, 0.0, two, -8 * h, 1)
-        asel(R("yy", h, al, slice(3, 5)), C("ones", 0, 16), A.is_equal, 0.0, [[-16, 8], [-1, 2]], -8 * h, 1)
-    mul(R("rw", al, slice(0, 3)), R("nbd", al, slice(0, 3)), 2048.0), mul(R("rw", al, slice(3, 5)), R("nbd", al, slice(3, 5)), -2048.0)
+    for h in range(4):
+        asel(R("xx", h, al, s2), R("xx", 3, al, s2), A.is_equal, 0.0, two, -4 * h, 1)
+        asel(R("yy", h, al, slice(3, 5)), C("ones", 0, 16), A.is_equal, 0.0, [[-16, 8], [-1, 2]], -4 * h, 1)
+    mul(R("rw", 0, mid, slice(0, 3)), R("n4", al, slice(0, 3)), 2048.0), mul(R("rw", 0, mid, slice(3, 5)), R("n4", al, slice(3, 5)), -2048.0)
+    ts(R("rw", 1, mid, 5), R("n4", al, 0), C("pf", 11), -1.0, A.mult, A.mult), mul(R("rw", 1, mid, 6), R("n4", al, 0), col(18))
     ez = C("ez", 15, 128, 16)
     asel(ez, C("ones", 0, 8), A.is_equal, 0.0, [[-16, 8]], 0, 1), asel(ez, ez, A.not_equal, -1.0, [[-16, 8]], -1, 1)
     mul(R("d0"), C("ones", 0, 256), oh0)
@@ -294,7 +305,7 @@ def record(g, core, rank, T, topo):
     asel(R("sel", NT + 1), C("zt", 0, 40), A.not_equal, -1.0, far, 0, 1)
 
     cp(C("lbu", 0, 16), C("lbi", 0, 16), s=False), cp(C("lbu", 16, 64), C("lbi", 16, 64), s=False), cp(R("lvu"), R("lvi"), s=False)
-    send([C("lbu", 16, 64)], [(t, T.lbu[:, 16 * t:16 * t + 16], R("lbr", t - 1), "lb%d" % t, 2 * t, 2 * t + 2) for t in (1, 2, 3)], 4000)
+    sent_last = send([C("lbu", 16, 64)], [(t, T.lbu[:, 16 * t:16 * t + 16], R("lbr", t - 1), "lb%d" % t, 2 * t, 2 * t + 2) for t in (1, 2, 3)])
 
     ivc = [C("ivs", 128 * c, 128 * c + 128) for c in range(8)]
     ks, kd_, kp = B("ks", 0, 512), B("kd", 0, 512), B("kp", 0, 512)
@@ -309,36 +320,41 @@ def record(g, core, rank, T, topo):
     tt(R("dl"), kd_, R("dl"), A.add)
     scan(R("pm2"), R("rs"), R("dl"), A.add, A.min)
     cp(R("dt3", al, slice(8, 16)), kp)
-    for k, x in enumerate(("pm1", "pm2")):
-        x, r = C(x, 7, 512, 8), R("ck", al, k)
+    for k, (x, unit) in enumerate((("pm1", 2.0 ** 24), ("pm2", 1.0))):
+        x, r, m1, m2 = C(x, 7, 512, 8), R("ck", k), unit * 256 * MAGIC, unit * 65536 * MAGIC
         dg = [R("dt3", al, 4 * k + j) for j in range(3)]
-        cp(dg[0], x), tt(r, x, dg[0], A.subtract), cp(dg[1], r), tt(dg[2], r, dg[1], A.subtract)
+        ts(dg[0], x, m2, m2, A.add, A.subtract), ts(r, x, m1, m1, A.add, A.subtract)
+        tt(dg[1], r, dg[0], A.subtract), tt(dg[2], x, r, A.subtract)
     for h in (0, 1):
         mmg([[(B("kt%d" % h, 128 * c, 128 * c + 128), R("dt3", slice(32 * h + 8 * c, 32 * h + 8 * c + 8)), ident)] for c in range(4)])
         cp(C("ct", 512 * h, 512 * h + 512), B("kt%d" % h, 0, 512))
-    mul(R("req"), IX(R("ct"), R("lvu")), -1.0)
+    asked = mul(R("req"), IX(R("ct"), R("lvu")), -1.0)
     for t in (1, 2, 3):
-        send([R("req")], [(t, T.req[:], R("rq", t - 1), "rq%d" % t, 0, 8)], 2600 + 400 * t)
+        sent_last = send([R("req")], [(t, T.req[:], R("rq", t - 1), "rq%d" % t, 0, 8)], [sent_last])
 
-    mm([(B("pk", 0, min(PW, 2048 - PW * j)), R("ids", j), C("lfs", PW * j, min(PW * j + PW, 2048))) for j in range(6)])
+    mm([(B("pk", 0, min(PW, 2048 - PW * j)), R("ids", j), C("lf2", PW * j, min(PW * j + PW, 2048))) for j in range(6)])
     ts(R("pk"), B("pk", 0, PW), 7.0 * 0x111111, None, A.add)
     pd = dict(R("pk"), b="pd")
-    dma([(T.pd[0:128, :], T.pk[:]), (T.pd[128:128 + 16 * SHIFT[-1], :], T.pk[0:16 * SHIFT[-1], :])], [R("pk")], [pd], 2800)
+    dma([(T.pd[0:128, :], T.pk[:]), (T.pd[128:240, :], T.pk[0:112, :])], [R("pk")], [pd], 240 * 4 * PW)
+    dma([(T.lf2[half[k], 2048:4096], T.lf[half[1 - k], :]) for k in (0, 1)], [], [C("lf2", 2048, 4096)], 1 << 19, after=[asked])
     for t in (1, 2, 3):
-        send([pd], [(-t, T.pd[16 * SHIFT[t]:16 * SHIFT[t] + 128, :], R("pl", t - 1), "pk%d" % t, 0, 8)], 2500 + 2500 * t)
+        s = (16 * SHIFT[t] + 64) % 128
+        sent_last = send([pd], [(-t, T.pd[s:s + 128, :], R("pl", t - 1), "pk%d" % t, 0, 8)], [sent_last])
+    for a in (0, 1024):
+        ts(C("tb", 2048 + a, 3072 + a), C("lf2", a, a + 1024), 7.0, None, A.add, act=(F.Identity, 7.0, 1.0))
 
     def unpack(t):
         for j in range(6):
-            w = min(PW, 2048 - PW * j)
-            ts(D("tb", t - 1, PW * j, PW * j + w), D("pl", t - 1, 0, w), 4 * j, 15, A.arith_shift_right, A.bitwise_and)
+            a, w = 4096 * (1 - t % 2) + PW * j, min(PW, 2048 - PW * j)
+            ts(C("tb", a, a + w), D("pl", t - 1, 0, w), 4 * j, 15, A.arith_shift_right, A.bitwise_and)
 
     def claim(t):
         s = 16 * SHIFT[t]
         r = (128 - s) % 128
         rq = (lambda a, b: C("req", a, b)) if t == 0 else (lambda a, b: D("rq", t - 1, a, b))
         u0, u1, u2, u3 = ("c%d%d" % (k, t) for k in range(4))
-        cp(R("wu", t), IX(R("bks"), C("lbu", 0, 16) if t == 0 else R("lbr", t - 1)), s=False)
-        ts(R("wh", t), R("wu", t), 1.0, None, A.mult)
+        cp(R("wh", t), IX(R("bks"), C("lbu", 0, 16) if t == 0 else R("lbr", t - 1)))
+        cp(R("wu", t), R("wh", t), s=False)
         for c in range(0, 4096, CH):
             cp(D("ga", t, c, c + CH), IX(R("ct"), D("wu", t, c // 16, (c + CH) // 16)))
         for h in range(4):
@@ -353,29 +369,33 @@ def record(g, core, rank, T, topo):
         ts(R("val", t), b, -2047.0, 0.0, A.add, A.max, act=(F.Relu, -2047.0, 1.0))
         mm([(B(u1, 0, 16), C("e1", 15 - l, 143 - l), D("val", t, l, 256, 16)) for l in range(16)])
         ts(R("wl", t), B(u1, 0, 16), -1.0, 0.0, A.add, A.max)
+        mm([(B(u1, 64, 128), C("e1", 15 - 4 * h + s, 143 - 4 * h + s), D("val", t, 64 * h, 64 * h + 64)) for h in range(4)])
+        cp(R("kv", t), B(u1, 64, 128))
+        if t:
+            send([R("kv", t)], [(-t, T.kv[:, t], R("ku", t - 1), "kv%d" % t, 0, 8)])
         cp(R("iw", t), IX(R("ivs"), R("wl", t))), cp(R("kw", t), IX(R("kds"), R("wl", t)))
         a, b = B(u2, 0, 256), B(u2, 256, 512)
-        mmg([[(a, C("wn1", r, r + 128), rq(0, 256)), (a, R("w3", 0), R("iw", t))],
-             [(b, C("wn2", r, r + 128), rq(0, 256)), (b, R("w3", 1), R("iw", t))]])
-        ts(R("sg", t), a, 0.0, None, A.not_equal, act=(F.Sign, 0.0, 1.0))
-        tt(R("fitm", t), b, R("sg", t), A.is_equal)
+        mm([(a, C("wn1", r, r + 128), rq(0, 256))], stop=False)
+        mm([(a, R("w3", 0), R("iw", t)), (a, C("wn2", r, r + 128), rq(0, 256)), (a, R("w3", 1), R("iw", t))], start=False)
+        ts(R("fitm", t), a, 0.0, None, A.is_equal)
         c = B(u3, 0, 256)
         mm([(c, hh, R("kw", t))])
         cp(R("hk", t), c)
         mm([(a, R("tt"), R("fitm", t))])
-        ts(R("ohm", t), a, 0.0, None, A.max, act=(F.Relu, 0.0, 1.0))
+        relu(R("ohm", t), a)
         mm([(b, hh, R("ohm", t))])
         tt(R("pr", t), b, R("hk", t), A.mult)
-        e = B(u3, 256, 384)
-        mm([(e, C(m, 15 - 8 * h - f + s, 143 - 8 * h - f + s), D(x, t, 128 * h, 128 * h + 128))
-            for h in (0, 1) for f, m, x in ((0, "e1", "val"), (1, "e1m", "ohm"))])
+        mm([(B(u3, 256, 320), C("e1m", 14 - 4 * h + s, 142 - 4 * h + s), D("ohm", t, 64 * h, 64 * h + 64)) for h in range(4)])
         mm([(c, R("h32", slice(SHIFT[t], SHIFT[t] + 8)), R("pr", t))])
-        cp(R("kr", t), B(u3, 0, 384))
+        cp(R("kr", t), B(u3, 0, 320))
         if t:
-            send([R("kr", t)], [(-t, T.kr[:, t], R("kl", t - 1), "kr%d" % t, 0, 8)], 3500)
+            send([R("kr", t)], [(-t, T.kr[:, t], R("kl", t - 1), "kr%d" % t, 0, 8)])
 
     def kl(t, a, b):
         return D("kr", 0, a, b) if t == 0 else D("kl", t - 1, a, b)
+
+    def ku(t):
+        return R("kv", 0) if t == 0 else R("ku", t - 1)
 
     def kids(t):
         o = B("x%d" % t, 0, 256)
@@ -383,9 +403,14 @@ def record(g, core, rank, T, topo):
         cp(R("kx", t), o)
 
     def state(z):
-        mmg([([(o, R("xx", h), kl(z, 256, 384))] if z < NT else []) + ([(o, R("yy", h), kl(z - 1, 256, 384))] if z else []) +
-             [(o, R("ww"), D("zo", old, 128 * h, 128 * h + 128)) for old in range(z - 1) if z < NT]
-             for h in (0, 1) for o in [B("z%d" % z, 128 * h, 128 * h + 128)]])
+        def q(h):
+            return B("z%d" % z, 64 * h, 64 * h + 64)
+        old = [(B("z%d" % z, 0, 256), R("ww"), R("zo", k)) for k in range(z - 1) if z < NT]
+        cur = [(q(h), R("yy", h), x) for h in range(4) for x in (ku(z - 1), kl(z - 1, 256, 320))] if z else []
+        if cur:
+            mm(old + cur, stop=z == NT)
+        if z < NT:
+            mm([(q(h), R("xx", h), ku(z)) for h in range(4)], start=not cur)
         tt(R("zin", z), B("z%d" % z, 0, 256), R("cz"), A.max)
 
     def places(t, z):
@@ -398,52 +423,49 @@ def record(g, core, rank, T, topo):
     def test(t):
         sw, kx, n = IX(R("sw"), R("off", t)), R("kx", t), 96
         i0 = op({"v": (60 + SCT * CY * 256, lambda: V.tensor_copy(sw["ap"], kx["ap"]))}, [kx, R("off", t)], [R("sw")])
-        ts(D("ab", t, 0, n), C("sw", 0, n), 1.0 / 2048, -1023.5 / 2048, A.mult, A.add)
+        win, a0 = (R("lf2"), 0) if t == 0 else (C("tb", 0, 4096), 2048) if t % 2 else (C("tb", 2048, 6144), 0)
         ts(R("bi"), C("sw", 0, n), 2047, None, A.bitwise_and)
-        cp(D("ab", t, n, 2 * n), R("bi"), s=False)
+        for k in (0, 1):
+            ts(R("ab", t, k, part=half[k]), R("sw", slice(0, n), part=half[k]), 1.0 / 2048, a0 - 1023.5 / 2048, A.mult, A.add)
+            ts(R("ab", t, k, part=half[1 - k]), R("bi", part=half[k]), 2048.0 - a0, None, A.add)
         for a, b in CUT:
-            cp(D("ta", t, 16 * a, 16 * b), IX(R("lfs"), D("ab", t, a, b)))
-            cp(D("tc", t, 16 * a, 16 * b), IX(R("tb", t - 1) if t else R("lfs"), D("ab", t, n + a, n + b)))
+            for k in (0, 1):
+                o, x = R("ta", t, k, slice(16 * a, 16 * b)), IX(win, R("ab", t, k, slice(a, b)))
+                ts(o, x, -7.0, None, A.add, act=(F.Identity, -7.0, 1.0)) if t else cp(o, x)
         for a, b in CUT:
-            w = 2 * (b - a)
-            for sn in (0, 1):
-                u = "d%d%d%d" % (t, sn, a)
-                for x, neg in (("ta", 1), ("tc", 2 * sn - 1)):
-                    mm([(B(u, w * j, w * j + w), R("hm", HM.index(neg * v)), D(x, t, 16 * a + d, 16 * b, 8)) for d, (j, v) in enumerate(KID)],
-                       start=x == "ta", stop=x == "tc")
-                ts(R("nd", t % 2, slice(sn, 6, 2), slice(a, b)), B(u, 0, 3 * w), col(14 - sn) if t else 0.0, None, A.not_equal,
-                   act=(F.Square, col(13 + sn) if t else 0.0, 1.0))
-            u = "n%d%d" % (t, a)
-            both, plus, minus = B(u, 0, w), B(u, 0, w // 2), B(u, w // 2, w)
-            mm([(both, R("l1"), R("nd", t % 2, slice(2 * j, 2 * j + 2), slice(a, b), h)) for h in (0, 1) for j in range(3)] +
-               [(both, R("l2"), R("nd", t % 2, slice(2 * j + 1, 2 * j + 3), slice(a, b), h)) for h in (0, 1) for j in range(2)] +
-               [(o, R("l2"), R("nd", t % 2, k, slice(a, b), h)) for h in (0, 1) for o, k in ((plus, 5), (minus, 0))])
-            ts(R("fpm", t, al, slice(a, b)), both, 0.5, None, A.is_lt, act=(F.Relu, 1.0, -1.0))
-        fp, fm, op_, om = R("fpm", t, 0), R("fpm", t, 1), D("oh", t, 0, n), D("oh", t, n, 2 * n)
+            w, u = 2 * (b - a), "d%d%d" % (t, a)
+            for k in (0, 1):
+                mm([(B(u, w * k, w * k + w), R("hm", 1 + 2 * d + k), R("ta", t, k, slice(16 * a + d, 16 * b, 8))) for d in range(7, -1, -1)])
+            ts(R("nd", t, al, slice(a, b)), B(u, 0, 2 * w), 0.0, None, A.not_equal, act=(F.Abs, 0.0, 1.0))
+            mm([(B(u, 256, 256 + w), R("l1"), R("nd", t, al, slice(a, b), h)) for h in (0, 1)])
+            ts(R("fpm", t, al, slice(a, b)), B(u, 256, 256 + w), 0.5, None, A.is_lt, act=(F.Relu, 1.0, -1.0))
         r = B("r%d" % t, 0, n)
+
+        def home(m, x):
+            return [(r, R("rw", m, slice(4 - 4 * k, 12 - 4 * k)), x(k)) for k in (0, 1)]
         if t < NT - 1:
             mm([(r, R("xx", 0), C("ones", 0, n))], stop=False, after=[i0])
-            mm([(r, R("rw"), fm), (r, R("rw"), fp)], start=False)
+            mm(home(0, lambda k: R("fpm", t, k)), start=False)
             tt(C("res", 0, n), r, R("cres"), A.max)
             tt(R("zo", t), IX(R("res"), R("ofc", t)), R("zin", t + 1), A.min)
             places(t + 1, R("zo", t))
-        a, b = B("f%d" % t, 0, n), B("f%d" % t, n, 2 * n)
-        mmg([[(a, R("tt"), fp), (a, R("nu"), fm)], [(b, R("tt"), fm), (b, R("nui"), fp)]])
-        ts(R("oh", t), B("f%d" % t, 0, 2 * n), 0.0, None, A.max, act=(F.Relu, 0.0, 1.0))
-        first = [(a, C("e1m", 10, 138), op_), (a, C("e1m", 10, 138), om), (a, C("e1", 9, 137), op_)]
+        r = B("f%d" % t, 0, n)
+        mm([(B("f%d" % t, 0, 2 * n), R("t2"), R("fpm", t))])
+        relu(R("oh", t), B("f%d" % t, 0, 2 * n))
+        first = home(1, lambda k: D("oh", t, n * k, n * k + n))
         if t < NT - 1:
             mm(first)
-            cp(D("rs2", t, 0, n), a)
+            cp(D("rs2", t, 0, n), r)
             cp(R("zm", t), IX(R("rs2", t), R("ofc", t)))
         else:
-            mm(first + [(a, R("rw"), op_), (a, R("rw"), om)])
-            tt(C("res", 0, n), a, R("cres"), A.max)
+            mm(first + home(0, lambda k: D("oh", t, n * k, n * k + n)))
+            tt(C("res", 0, n), r, R("cres"), A.max)
             tt(R("zo", t), IX(R("res"), R("ofc", t)), R("zin", t + 1), A.min)
 
     mul(R("ka"), IX(R("kds"), R("lvu")), 0.5)
     for t in range(NT):
         claim(t)
-        if t:
+        if t in (1, 2):
             unpack(t)
         kids(t)
     state(0)
@@ -452,12 +474,14 @@ def record(g, core, rank, T, topo):
     for t in range(NT):
         state(t + 1)
         test(t)
+        if t == 1:
+            unpack(3)
     o = B("y", 0, 256, slice(0, 40))
     mm([(o, R("sel", NT + 1), C("ones", 0, 256))] + [(o, R("sel", t), R(z, t)) for t in range(NT - 1) for z in ("zo", "zm")], stop=False)
     mm([(o, R("sel", NT - 1), R("zo", NT - 1))], start=False)
     ysb = R("ysb", part=slice(0, 40))
     cp(ysb, o)
-    end = dma([(T.y[:], ysb["ap"])], [ysb], [], 2000, "y")
+    end = dma([(T.y[:], ysb["ap"])], [ysb], [], 40960, "y")
     return ops, uses, sent[0], ops[end]["sem"]
 
 
@@ -465,58 +489,105 @@ def order_calls(ops, uses):
     n = len(ops)
     cost = [{e: c for e, (c, f) in o["var"].items()} for o in ops]
     lat = [o["sem"][2] if o["sem"] else LAT for o in ops]
-    rs = np.random.RandomState(1)
+    move = [o["move"] for o in ops]
+    rs = np.random.RandomState(SEED)
+    either = [i for i in range(n) if len(cost[i]) > 1]
 
-    def place(deps, succ, key, back, vbias):
-        before, behind = (succ, deps) if back else (deps, succ)
-        left = [len(x) for x in before]
-        ready = [i for i in range(n) if not left[i]]
-        busy, eng, start, fin = {e: [] for e in "vstpyn"}, [""] * n, [0.0] * n, [0.0] * n
-        while ready:
-            i = min(ready, key=lambda k: key[k])
-            ready.remove(i)
-            best = None
-            for e, c in cost[i].items():
-                t = 0.0
-                for j in before[i]:
-                    a, b = (i, j) if back else (j, i)
-                    raw = deps[b][a]
-                    hard = raw is not None and (ops[a]["sem"] or eng[j] != e or (raw and e != "t"))
-                    t = max(t, fin[j] + (lat[a] if hard else 0.0))
-                k = 0
-                for k, (s0, s1) in enumerate(busy[e] + [(1e18, 1e18)]):
-                    if t + c <= s0:
-                        break
-                    t = max(t, s1)
-                if best is None or t + c * (vbias if e == "v" else 1.0) < best[0]:
-                    best = (t + c * (vbias if e == "v" else 1.0), e, t, k)
-            x, e, t, k = best
-            busy[e].insert(k, (t, t + cost[i][e]))
-            eng[i], start[i], fin[i] = e, t, t + cost[i][e]
-            for j in behind[i]:
-                left[j] -= 1
-                if not left[j]:
-                    ready.append(j)
-        return max(fin), eng, start, fin
-
-    def search(deps, key, tries):
-        succ = [[] for _ in ops]
+    def graph(deps):
+        succ, left = [[] for _ in ops], [len(d) for d in deps]
         for i, d in enumerate(deps):
             for j in d:
                 succ[j].append(i)
-        plan = None
+        topo = [i for i in range(n) if not left[i]]
+        for i in topo:
+            for j in succ[i]:
+                left[j] -= 1
+                if not left[j]:
+                    topo.append(j)
+        kind = [{j: 0 if r is None else 1 if ops[j]["sem"] or move[j] else 3 if r else 2 for j, r in d.items()} for d in deps]
+        fw = [[(j, k, lat[j]) for j, k in d.items()] for d in kind]
+        bw = [[(j, kind[j][i], lat[i] + move[i]) for j in succ[i]] for i in range(n)]
+        return (topo, fw, move), (topo[::-1], bw, [0.0] * n)
+
+    def place(way, key, eng):
+        topo, before, mv = way
+        key = list(key)
+        for i in topo:
+            for j, k, l in before[i]:
+                if key[j] >= key[i]:
+                    key[i] = key[j] + 1e-3
+        busy, got, start, fin, held = {e: ([], [], []) for e in "vstpyn"}, [""] * n, [0.0] * n, [0.0] * n, [None] * n
+        done, dmas = [0.0] * n, 0.0
+        for i in sorted(range(n), key=lambda i: key[i]):
+            best = None
+            for e in (eng[i],) if eng else cost[i]:
+                c, t, h = cost[i][e], 0.0, None
+                for j, k, l in before[i]:
+                    x = done[j] + l if k == 1 or (k and got[j] != e) or (k == 3 and e != "t") else fin[j]
+                    if x > t:
+                        t, h = x, j
+                s0, s1, who = busy[e]
+                k = len(s1)
+                while k and s1[k - 1] > t:
+                    k -= 1
+                while k < len(s0) and t + c > s0[k]:
+                    t, h = s1[k], ~who[k]
+                    k += 1
+                x = t + c * (2.0 if e == "v" else 1.0)
+                if best is None or x < best[0]:
+                    best = (x, e, t, k, h)
+            x, e, t, k, held[i] = best
+            start[i], got[i] = t, e
+            fin[i] = done[i] = t + cost[i][e]
+            if mv[i]:
+                dmas = done[i] = max(dmas, fin[i]) + mv[i]
+            busy[e][0].insert(k, t), busy[e][1].insert(k, fin[i]), busy[e][2].insert(k, i)
+        return max(done) + 1e-4 * sum(fin), got, start, fin, held
+
+    def blocked(plan):
+        i, out = int(np.argmax(plan[3])), []
+        while plan[4][i] is not None:
+            h = plan[4][i]
+            if h < 0:
+                h = ~h
+                out.append((i, h))
+            i = h
+        return out
+
+    def search(deps, plan, tries):
+        fw, bw = graph(deps)
+        cur = best = place(fw, plan[2], plan[1])
+        pairs = blocked(cur)
         for k in range(tries):
-            vb = float(rs.choice(VB))
-            r = place(deps, succ, key, False, vb)
-            if plan is None or r[0] < plan[0]:
-                plan = r
-            if k % 3 == 0:
-                sh = rs.randn(40) * float(rs.choice([0, 1000, 3000])) * (rs.rand(40) < 0.3)
-                key = list(rs.rand(n) * float(rs.choice([100, 300, 1000])) + np.array(plan[2]) + sh[np.arange(n) * 40 // n])
+            key, eng, u = list(cur[2]), list(cur[1]), rs.rand()
+            if u < 0.05:
+                b = place(bw, [-x for x in cur[3]], eng)
+                key = [-x for x in b[3]]
+            elif u < 0.35 and pairs:
+                i, h = pairs[int(rs.randint(len(pairs)))]
+                x = i if rs.rand() < 0.5 else h
+                if len(cost[x]) > 1 and rs.rand() < 0.6:
+                    eng[x] = str(rs.choice([e for e in cost[x] if e != eng[x]]))
+                elif x == i:
+                    key[i] = key[h] - 1 - float(rs.exponential()) * 300
+                else:
+                    key[h] = key[i] + 1 + float(rs.exponential()) * 600
+            elif u < 0.55:
+                for i in rs.choice(either, int(rs.randint(1, 4))).tolist():
+                    eng[i] = str(rs.choice(list(cost[i])))
+            elif u < 0.85:
+                for i in rs.randint(0, n, int(rs.randint(1, 5))).tolist():
+                    key[i] += float(rs.randn()) * 1500
             else:
-                b = place(deps, succ, [-x for x in r[3]], True, vb)
-                key = list(-np.array(b[3]))
-        return plan
+                i, w, d = int(rs.randint(0, n)), int(rs.randint(2, 30)), float(rs.randn()) * 2000
+                key[i:i + w] = [x + d for x in key[i:i + w]]
+            r = place(fw, key, eng)
+            if r[0] < cur[0] + HEAT * (1 - k / tries) * float(rs.exponential()):
+                cur = r
+                pairs = blocked(cur)
+                if r[0] < best[0]:
+                    best = r
+        return best
 
     def banks(plan):
         deps, bank, held = [dict(o["deps"]) for o in ops], {}, [None] * 8
@@ -542,20 +613,20 @@ def order_calls(ops, uses):
 
     prio = [0.0] * n
     for i in range(n - 1, -1, -1):
-        prio[i] += min(cost[i].values()) + lat[i]
+        prio[i] += min(cost[i].values()) + lat[i] + move[i]
         for j in ops[i]["deps"]:
             prio[j] = max(prio[j], prio[i])
-    plan = search([o["deps"] for o in ops], [-x for x in prio], TRIES)
-    INFO["free"] = plan[0]
+    plan = search([o["deps"] for o in ops], (0, None, [-x for x in prio]), 2 * TRIES)
+    INFO["free"] = max(plan[3])
     best = None
     for k in range(ROUNDS):
         deps, bank = banks(plan)
-        plan = search(deps, list(plan[2]), TRIES)
+        plan = search(deps, plan, TRIES)
         if best is None or plan[0] < best[0][0]:
             best = (plan, deps, bank)
     plan, deps, bank = best
-    INFO["bank"] = bank
-    INFO["plan"] = (plan[0], plan[1], sorted(range(n), key=lambda i: (plan[2][i], i)), deps)
+    INFO["bank"], INFO["lat"] = bank, lat
+    INFO["plan"] = (max(plan[3]), plan[1], sorted(range(n), key=lambda i: (plan[2][i], i)), deps)
     INFO["show"] = [(plan[2][i], plan[3][i], plan[1][i], ops[i]["tag"]) for i in range(n)]
 
 

import numpy as np
from concourse.mybir import AluOpType, ActivationFunctionType
from concourse.bass import DstId, RemoteDMATransfer

A = AluOpType
F = ActivationFunctionType
N, NT, PW, WIN = 8, 4, 342, 1120
SHIFT = [0, 1, 3, 6]
STEP = 512.0
MAGIC = 12582912.0

_B = {}
for _d, _l in (
    ("bfloat16", dict(lf2=4096, ivs=1024, ones=512, bd8=8, bdw=256, b4=(4, 16), n4=(4, 32), n8=(8, 8), w3=(2, 8, 16), wd=64, wp=64, cneg=128,
                      tp=256, wn1=256, wn2=256, e2=144, pm=136, tt=128, t2=128, nu=128, nbd=128, e1=256, e1m=256, ez=144, xx=(4, 8, 16),
                      yy=(4, 8, 16), ww=(8, 16), rw=(2, 12, 16), l1=(4, 16, 2), hm=(17, 8, 16), ids=(6, 128), zt=128, sel=(6, 8, 5), dt3=(64, 16),
                      ct=1024, req=256, rq=(3, 256), ga=(4, 4096), ta=(4, 2, 1536), sq=(4, 512), fit=(4, 256), iw=(4, 256), fitm=(4, 256),
                      ohm=(4, 256), nd=(4, 2, 96, 2), fpm=(4, 2, 96), oh=(4, 192), rs2=(4, 112), zm=(3, 256))),
    ("float32", dict(cc=136, gc=256, g4=64, g32=128, ln=256, lm=96, pf=12, col=24, q4=4, oh2=2, rs=512, pm1=512, dl=512, pm2=512, ck=(2, 64),
                     h32=(16, 16), hk=(4, 256), pr=(4, 256), res=112, cres=96, cz=256, kx=(4, 256), zin=(5, 256), ysb=256)),
    ("float16", dict(wh=(4, 256), val=(4, 256), kw=(4, 256), ka=256, d0=256, z0=256, zo=(4, 256), zs=256, kr=(4, 320), kl=(3, 320),
                     kv=(4, 64), ku=(3, 64))),
    ("int32", dict(kds=1024, bks=1024, lvi=16, lbi=64, pi=13, sw=WIN, bi=96, pk=PW, pl=(3, PW), tb=6144)),
    ("uint16", dict(lvu=16, lbu=64, lbr=(3, 16), wu=(4, 256), wl=(4, 16), off=(4, 16), ofc=(4, 16), ab=(4, 2, 96))),
):
    for _k, _s in _l.items():
        _B[_k] = ("sbuf", [128] + (list(_s) if isinstance(_s, tuple) else [_s]), _d)
_B["pd"] = ("dram", [240, PW], "int32")
for _k in range(8):
    _B["p%d" % _k] = ("psum", [128, 512], "float32")
SCRATCH = _B
SEMAPHORES = (["v", "s", "t", "p", "snt"] + ["ld%d" % i for i in range(12)] +
              [x + str(t) for x in ("lb", "rq", "pk", "kr", "kv") for t in (1, 2, 3)])

CY, PC, LAT, GC, SCT, DLAT, DRATE, RLAT, RRATE = 0.9, 0.45, 150.0, 1.56, 3.8, 1900.0, 300.0, 2000.0, 90.0
CH, CUT, ROUNDS, TRIES, HEAT, SEED = 1024, ((0, 32), (32, 64), (64, 96)), 2, 9000, 100.0, 1
INFO = {}


def record(g, core, rank, T, topo):
    V, S, P = g.vector, g.scalar, g.tensor
    ops, acc, uses, sent, nld = [], {}, {}, [0], [0]
    al, half = slice(None), (slice(0, 64), slice(64, 128))

    def R(name, *idx, part=al):
        shape = SCRATCH[name][1][1:]
        el = np.arange(int(np.prod(shape))).reshape(shape)[idx].ravel()
        m = 0
        if el[-1] - el[0] + 1 == len(el):
            m = ((1 << len(el)) - 1) << int(el[0])
        else:
            for k in el.tolist():
                m |= 1 << k
        return dict(ap=T[name][(part,) + idx], b=name, m=m, n=len(el), w=2 if "16" in SCRATCH[name][2] else 4, off=None, ps=False,
                    h=3 if part not in half else 1 + half.index(part))

    def C(name, a, b=None, s=None):
        return R(name, slice(a, a + 1 if b is None else b, s))

    def D(name, k, a, b, s=None):
        return R(name, k, slice(a, b, s))

    def B(use, a, b, part=al, step=1):
        return dict(ap=T[INFO.get("bank", {}).get(use, "p0")][part, a:b:step], b=use, m=1, n=len(range(a, b, step)), w=4, off=None, ps=True, h=3)

    def IX(win, off):
        return dict(win, ap=win["ap"].indirect(off["ap"]), n=16 * off["n"], off=off)

    def op(var, reads, writes, sem=None, after=(), behind=(), tag="", move=0.0):
        i, deps = len(ops), {}
        reads = [r for r in reads if isinstance(r, dict)]
        reads = reads + [r["off"] for r in reads if r["off"]]
        for x, wr in [(r, False) for r in reads] + [(w, True) for w in writes]:
            l = acc.setdefault(x["b"], [])
            if x["ps"]:
                uses.setdefault(x["b"], []).append(i)
                for j, m, pw, h in l[::-1]:
                    if j != i:
                        deps[j] = deps.get(j, False) or pw or wr
                        break
                for j, m, pw, h in l[::-1]:
                    if j != i and pw and not wr:
                        deps[j] = True
                        break
            else:
                for j, m, pw, h in l:
                    if j != i and (pw or wr) and m & x["m"] and h & x["h"]:
                        deps[j] = True
                if wr:
                    l[:] = [e for e in l if e[1] & ~x["m"] or e[3] & ~x["h"]]
            l.append((i, x["m"], wr, x["h"]))
        for j in after:
            deps[j] = True
        for j in behind:
            deps.setdefault(j, None)
        ops.append(dict(var=var, deps=deps, sem=sem, move=move, tag=tag or (writes[0]["b"] if writes else "")))
        return i

    def ap(x):
        return x["ap"] if isinstance(x, dict) else x

    def vc(o, i, m=1.0):
        if i["off"]:
            return 60 + GC * CY * i["n"]
        return 30 + CY * max(64, m * i["n"] * (0.5 if m == 1.0 and o["w"] == 2 and i["w"] == 2 else 1.0))

    def sc(i):
        return 70 + CY * (GC * i["n"] if i["off"] else max(64, i["n"]))

    def ts(o, i, a, b, op0, op1=None, act=None, more=None):
        var = {"v": (vc(o, i), lambda: V.tensor_scalar(o["ap"], i["ap"], ap(a), ap(b), op0, op1) if op1 else
                     V.tensor_scalar(o["ap"], i["ap"], ap(a), None, op0))}
        if act:
            var["s"] = (sc(i), lambda: S.activation(o["ap"], i["ap"], act[0], bias=ap(act[1]), scale=ap(act[2])))
        if more:
            var["p"] = more[0]
        return op(var, [i, a, b] + list(act[1:] if act else []) + (more[1] if more else []), [o])

    def mul(o, i, a, more=None):
        return ts(o, i, a, None, A.mult, act=(F.Copy, 0.0, a), more=more)

    def lin(o, i, a, b):
        return ts(o, i, a, b, A.mult, A.add, act=(F.Identity, b, a))

    def relu(o, i):
        return ts(o, i, 0.0, None, A.max, act=(F.Relu, 0.0, 1.0))

    def cp(o, i, s=True):
        var = {"v": (vc(o, i), lambda: V.tensor_copy(o["ap"], i["ap"]))}
        if s:
            var["s"] = (sc(i), lambda: S.activation(o["ap"], i["ap"], F.Identity))
        return op(var, [i], [o])

    def tt(o, a, b, alu):
        return op({"v": (vc(o, a, 1.001 if a["ps"] else 2.0), lambda: V.tensor_tensor(o["ap"], a["ap"], b["ap"], alu))}, [a, b], [o])

    def scan(o, a, b, op0, op1):
        return op({"v": (vc(o, b), lambda: V.tensor_tensor_scan(o["ap"], a["ap"], b["ap"], 0.0, op0, op1))}, [a, b], [o])

    def io(o, pat, base, cm):
        fl = SCRATCH[o["b"]][2] != "int32"
        return (130 + 2 * CY * o["n"], lambda: g.iota(o["ap"], pat, base, cm, allow_small_or_imprecise_dtypes=True) if fl
                else g.iota(o["ap"], pat, base, cm))

    def iota(o, pat, base, cm):
        return op({"p": io(o, pat, base, cm)}, [], [o])

    def ms(o, c=0.0):
        var = {"v": (vc(o, o), lambda: V.memset(o["ap"], c))}
        if abs(c) < 2 ** 24:
            var["p"] = io(o, [[0, o["n"]]], int(c), 0)
        return op(var, [], [o])

    def se(o, i, cmp, fill, pat, base, cm):
        return (170 + 2 * CY * o["n"], lambda: g.affine_select(o["ap"], i["ap"], [list(x) for x in pat], cmp, fill, base, cm))

    def asel(o, i, cmp, fill, pat=((1, 128),), base=0, cm=-1):
        return op({"p": se(o, i, cmp, fill, pat, base, cm)}, [i], [o])

    def mmg(gs, start=True, stop=True, after=()):
        def f():
            for q in gs:
                for k, (o, a, b) in enumerate(q):
                    r = P.matmul(o["ap"], a["ap"], b["ap"], start and k == 0, stop and k == len(q) - 1)
            return r
        l = [x for q in gs for x in q]
        c = 30 + sum(PC * max(64, b["n"]) * (4 if b["w"] == 4 else 1) for o, a, b in l)
        return op({"t": (c, f)}, [x for o, a, b in l for x in (a, b)], [l[0][0]], after=after)

    def mm(l, **k):
        return mmg([l], **k)

    last = []

    def dma(pairs, reads, writes, size, tag="", after=()):
        s = T.sem["ld%d" % nld[0]]
        nld[0] += 1

        def f():
            for a, b in pairs:
                g.sync.dma_start(a, b).then_inc(s, 16)
        last[:] = [op({"y": (60.0 * len(pairs), f)}, reads, writes, sem=(s, 16 * len(pairs), DLAT), after=after, behind=last, tag=tag,
                      move=150 * len(pairs) + size / DRATE)]
        return last[0]

    def peer(d):
        return T.cores[(rank + d) % N]

    def emask(d, a, b):
        return sum(1 << e for e in topo.engines(core, peer(d))[a:b])

    def send(src, trs, behind=()):
        def f():
            l = []
            for d, s, dst, sem, a, b in trs:
                rid, pid = topo.addr(peer(d), core)
                l.append(RemoteDMATransfer(dst_ids=[DstId(rid=rid, pnc=pid)], dma_engine_mask=emask(d, a, b), remote_sem=T.sem[sem],
                                           srcs=[s], dsts=[dst["ap"]]))
            g.remote_dma_fused(l, local_sem=T.sem.snt)
        i = op({"p": (500.0, f)}, src, [], tag="send", behind=behind, move=400 + sum(128 * x[2]["n"] * x[2]["w"] for x in trs) / RRATE)
        for d, s, dst, sem, a, b in trs:
            sent[0] += b - a
            op({"n": (0.0, None)}, [], [dst], sem=(T.sem[sem], b - a, RLAT), after=[i], tag="arr")
        return i

    dma([(T.ivs[:], T.iv[:])], [], [R("ivs")], 1 << 18)
    dma([(T.lvi[:], T.lv[:]), (T.lbi[:, 0:16], T.lb[:])], [], [R("lvi"), C("lbi", 0, 16)], 0)
    lb = []
    for t in (1, 2, 3):
        s = 16 * SHIFT[t]
        lb += [(T.lbi[s:128, 16 * t:16 * t + 16], T.lb[0:128 - s, :]), (T.lbi[0:s, 16 * t:16 * t + 16], T.lb[128 - s:128, :])]
    dma(lb, [], [C("lbi", 16, 64)], 0)
    dma([(T.bks[:], T.bk[:])], [], [R("bks")], 1 << 19)
    dma([(T.lf2[:, 0:2048], T.lf[:])], [], [C("lf2", 0, 2048)], 1 << 19)
    dma([(T.kds[:], T.kd[:])], [], [R("kds")], 1 << 19)

    def col(k):
        return C("col", k)

    iota(C("pi", 0), [[0, 1]], 0, 1)
    iota(R("bd8"), [[0, 8]], 1, 0)
    asel(R("bd8"), R("bd8"), A.is_ge, 0.0, [[-16, 8]], 0, 1), asel(R("bd8"), R("bd8"), A.is_ge, 0.0, [[16, 8]], 15, -1)
    bd8 = R("bd8")
    iota(R("cc"), [[1, 136]], -8, 0)
    for k, (sh, m) in enumerate([(0, 1), (1, 1), (2, 1), (3, 1), (4, 7), (0, 15), (2, 3), (4, 3), (6, 1), (1, 63), (5, 3), (1, 15)]):
        ts(C("pi", k + 1), C("pi", 0), sh, m, A.arith_shift_right, A.bitwise_and)
    cp(C("pf", 0, 4), C("pi", 1, 5), s=False), cp(C("pf", 4, 12), C("pi", 5, 13), s=False)
    b3, pg, p16, p4, ph = C("pf", 3), C("pf", 4), C("pf", 5), C("pf", 6), C("pf", 9)
    for b, v in enumerate((8.0, 64.0, 4096.0)):
        lin(col(b), C("pf", b), v - 1, 1.0), lin(col(3 + b), C("pf", b), 1 - v, v)
    lin(C("col", 6, 10), C("pf", 0, 4), -2.0, 1.0)
    lin(col(10), b3, -2.0 ** 24, 2.0 ** 24)
    for m in range(4):
        ts(R("n8", al, m), bd8, col(3 * (m & 1)), col(1 + 3 * (m >> 1)), A.mult, A.mult)
    mul(R("n8", al, slice(4, 8)), R("n8", al, slice(0, 4)), col(5)), mul(R("n8", al, slice(0, 4)), R("n8", al, slice(0, 4)), col(2))
    lo, hi = (R("w3", 0, al, slice(8 * k, 8 * k + 8)) for k in range(2))
    mul(lo, R("n8"), col(10)), ts(hi, R("n8"), b3, 2.0 ** 24, A.mult, A.mult), mul(R("wd"), R("n8"), col(9))
    mul(R("w3", 1, al, slice(8, 16)), lo, 2.0 ** -26), mul(R("w3", 1, al, slice(0, 8)), hi, 2.0 ** -26)
    ts(col(11), col(0), col(1), col(2), A.mult, A.mult)
    ts(R("wp"), C("cc", 8, 72), ph, col(11), A.is_equal, A.mult)
    ms(R("ones"), 1.0), ms(R("cneg"), -2.0 ** 41)
    ms(R("rs")), ms(C("rs", 0, 512, 8), 1e20)
    ms(R("dt3", al, slice(3, 8, 4)))
    ms(R("zt"))
    asel(R("ids", 0), R("zt"), A.not_equal, 1.0)
    ident = R("ids", 0)

    iota(R("gc"), [[0, 2], [1, 8], [0, 16]], 0, 0)
    ts(R("bdw"), R("gc"), pg, None, A.is_equal)
    ts(R("q4"), C("cc", 8, 12), p4, None, A.is_equal), ts(R("oh2"), C("cc", 8, 10), p16, None, A.is_equal)
    oh0, oh1 = C("oh2", 0), C("oh2", 1)
    for k in (0, 1):
        mul(C("tp", k, 256, 2), C("bdw", k, 256, 2), C("q4", k))
        ts(R("wn%d" % (k + 1)), R("bdw"), C("q4", 2 + k), 2.0 ** (24 - 26 * k), A.mult, A.mult)
    asel(R("e2"), C("tp", 0, 144), A.is_ge, 0.0, [[0, 9], [1, 16]], -14, 0)
    ts(col(12), pg, 8.0, ph, A.mult, A.add), ts(R("pm"), R("cc"), col(12), None, A.is_equal)
    mul(R("nbd"), C("bdw", 0, 128), -1.0)
    asel(R("nu"), R("nbd"), A.is_gt, 0.0), asel(R("tt"), R("nu"), A.not_equal, 1.0)
    asel(R("e1"), R("bdw"), A.is_equal, 0.0, [[0, 16], [1, 16]], -15, 0), mul(R("e1m"), R("e1"), p16)
    iota(R("g4"), [[1, 4], [0, 16]], 0, 0)
    ts(R("b4"), R("g4"), C("pf", 7), None, A.is_equal)
    lin(col(13), C("pf", 8), -2.0, 1.0), lin(col(14), C("pf", 8), 2.0, -1.0)
    cp(R("hm", 0, al, 0), bd8)
    for k in (0, 1):
        mul(R("hm", 1 + k, slice(0, 4), 0), R("b4", al, 0), col(13 + k)), cp(R("hm", 1 + k, slice(4, 8), 0), R("b4", al, 0))
    for b in range(4):
        mul(R("hm", slice(0, 3), al, slice(1 << b, 2 << b)), R("hm", slice(0, 3), al, slice(0, 1 << b)), col(6 + b))
    hh = R("hm", 0)
    for k in (0, 1):
        mul(R("h32", slice(8 * k, 8 * k + 8)), hh, 0.0625)
    for k in range(1, 6):
        mul(R("ids", k), ident, 16.0 ** k, more=(se(R("ids", k), R("zt"), A.not_equal, 16.0 ** k, ((1, 128),), 0, -1), [R("zt")]))

    for k in (1, 2, 4):
        mul(R("hm", slice(1 + 2 * k, 1 + 4 * k)), R("hm", slice(1, 1 + 2 * k)), STEP ** k)
    for k in (0, 1):
        relu(R("l1", al, al, k), R("hm", 1 + k, slice(0, 4)))
    iota(R("g32"), [[1, 4], [0, 32]], 0, 0)
    ts(R("n4"), R("g32"), C("pf", 10), -1.0, A.is_equal, A.mult)
    asel(R("t2"), R("n4"), A.is_gt, 0.0), asel(R("t2"), R("t2"), A.not_equal, 1.0)
    lin(col(18), C("pf", 0), 1.0, -1.0)
    two, s2, mid = [[-16, 8], [0, 2]], slice(0, 2), slice(4, 8)
    ms(R("xx")), ms(R("yy")), ms(R("ww")), ms(R("rw")), ms(R("ez"))
    iota(R("xx", 3, al, s2), [[0, 8], [1023, 2]], 1, 0), iota(R("ww", al, s2), [[0, 16]], -2 ** 21, 0)
    asel(R("ww", al, s2), R("ww", al, s2), A.is_equal, 0.0, two, -3, 1)
    for h in range(4):
        asel(R("xx", h, al, s2), R("xx", 3, al, s2), A.is_equal, 0.0, two, -4 * h, 1)
        asel(R("yy", h, al, slice(3, 5)), C("ones", 0, 16), A.is_equal, 0.0, [[-16, 8], [-1, 2]], -4 * h, 1)
    mul(R("rw", 0, mid, slice(0, 3)), R("n4", al, slice(0, 3)), 2048.0), mul(R("rw", 0, mid, slice(3, 5)), R("n4", al, slice(3, 5)), -2048.0)
    ts(R("rw", 1, mid, 5), R("n4", al, 0), C("pf", 11), -1.0, A.mult, A.mult), mul(R("rw", 1, mid, 6), R("n4", al, 0), col(18))
    ez = C("ez", 15, 128, 16)
    asel(ez, C("ones", 0, 8), A.is_equal, 0.0, [[-16, 8]], 0, 1), asel(ez, ez, A.not_equal, -1.0, [[-16, 8]], -1, 1)
    mul(R("d0"), C("ones", 0, 256), oh0)
    iota(R("ln"), [[-1, 256]], 767, 0), iota(R("lm"), [[-1, 96]], 255, 0)
    ts(col(15), p16, 5.0, 16.0, A.is_ge, A.mult), ts(col(16), p16, 2.0, -1.0, A.is_ge, A.mult), ts(col(17), oh1, 1024.0, oh0, A.mult, A.add)
    lin(R("cz"), R("ln"), oh1, col(15)), lin(R("cres"), R("lm"), oh1, col(16))
    mul(C("res", 96, 112), C("ones", 0, 16), col(17)), ms(R("rs2", al, slice(96, 112)))
    iota(C("sw", 0, 96), [[0, 96]], 0, 0)
    one, far = R("sel", NT), [[-16, 8], [200, 5]]
    iota(one, [[0, 40]], 1, 0), iota(R("sel", NT, al, 4), [[0, 8]], 2, 0)
    asel(one, one, A.is_equal, 0.0, [[-16, 8], [-1, 5]], -2, 1)
    asel(R("sel", NT, al, slice(1, 5, 3)), R("sel", NT, al, slice(1, 5, 3)), A.not_equal, 1.0, two, -2, 1)
    for t in range(NT):
        asel(R("sel", t), one, A.not_equal, -1.0 - (rank + t) % N, far, -2, 1)
    asel(R("sel", NT + 1), C("zt", 0, 40), A.not_equal, -1.0, far, 0, 1)

    cp(C("lbu", 0, 16), C("lbi", 0, 16), s=False), cp(C("lbu", 16, 64), C("lbi", 16, 64), s=False), cp(R("lvu"), R("lvi"), s=False)
    sent_last = send([C("lbu", 16, 64)], [(t, T.lbu[:, 16 * t:16 * t + 16], R("lbr", t - 1), "lb%d" % t, 2 * t, 2 * t + 2) for t in (1, 2, 3)])

    ivc = [C("ivs", 128 * c, 128 * c + 128) for c in range(8)]
    ks, kd_, kp = B("ks", 0, 512), B("kd", 0, 512), B("kp", 0, 512)
    mm([(ks, R("cneg"), R("ones"))], stop=False)
    mm([(B("ks", 64 * c, 64 * c + 64), ivc[c], w) for c in range(8) for w in (lo, hi)], start=False)
    mmg([[(B("kd", 64 * c, 64 * c + 64), ivc[c], R("wd"))] for c in range(8)])
    mmg([[(B("kp", 64 * c, 64 * c + 64), ivc[c], R("wp"))] for c in range(8)])
    scan(R("pm1"), R("rs"), ks, A.add, A.min)
    op({"s": (sc(kd_), lambda: S.activation(kd_["ap"], kd_["ap"], F.Abs))}, [kd_], [kd_])
    for i in range(8):
        tt(C("dl", i, 512, 8), B("ks", i, 512, step=8), C("pm1", 7, 512, 8), A.subtract)
    tt(R("dl"), kd_, R("dl"), A.add)
    scan(R("pm2"), R("rs"), R("dl"), A.add, A.min)
    cp(R("dt3", al, slice(8, 16)), kp)
    for k, (x, unit) in enumerate((("pm1", 2.0 ** 24), ("pm2", 1.0))):
        x, r, m1, m2 = C(x, 7, 512, 8), R("ck", k), unit * 256 * MAGIC, unit * 65536 * MAGIC
        dg = [R("dt3", al, 4 * k + j) for j in range(3)]
        ts(dg[0], x, m2, m2, A.add, A.subtract), ts(r, x, m1, m1, A.add, A.subtract)
        tt(dg[1], r, dg[0], A.subtract), tt(dg[2], x, r, A.subtract)
    for h in (0, 1):
        mmg([[(B("kt%d" % h, 128 * c, 128 * c + 128), R("dt3", slice(32 * h + 8 * c, 32 * h + 8 * c + 8)), ident)] for c in range(4)])
        cp(C("ct", 512 * h, 512 * h + 512), B("kt%d" % h, 0, 512))
    asked = mul(R("req"), IX(R("ct"), R("lvu")), -1.0)
    for t in (1, 2, 3):
        sent_last = send([R("req")], [(t, T.req[:], R("rq", t - 1), "rq%d" % t, 0, 8)], [sent_last])

    mm([(B("pk", 0, min(PW, 2048 - PW * j)), R("ids", j), C("lf2", PW * j, min(PW * j + PW, 2048))) for j in range(6)])
    ts(R("pk"), B("pk", 0, PW), 7.0 * 0x111111, None, A.add)
    pd = dict(R("pk"), b="pd")
    dma([(T.pd[0:128, :], T.pk[:]), (T.pd[128:240, :], T.pk[0:112, :])], [R("pk")], [pd], 240 * 4 * PW)
    dma([(T.lf2[half[k], 2048:4096], T.lf[half[1 - k], :]) for k in (0, 1)], [], [C("lf2", 2048, 4096)], 1 << 19, after=[asked])
    for t in (1, 2, 3):
        s = (16 * SHIFT[t] + 64) % 128
        sent_last = send([pd], [(-t, T.pd[s:s + 128, :], R("pl", t - 1), "pk%d" % t, 0, 8)], [sent_last])
    for a in (0, 1024):
        ts(C("tb", 2048 + a, 3072 + a), C("lf2", a, a + 1024), 7.0, None, A.add, act=(F.Identity, 7.0, 1.0))

    def unpack(t):
        for j in range(6):
            a, w = 4096 * (1 - t % 2) + PW * j, min(PW, 2048 - PW * j)
            ts(C("tb", a, a + w), D("pl", t - 1, 0, w), 4 * j, 15, A.arith_shift_right, A.bitwise_and)

    def claim(t):
        s = 16 * SHIFT[t]
        r = (128 - s) % 128
        rq = (lambda a, b: C("req", a, b)) if t == 0 else (lambda a, b: D("rq", t - 1, a, b))
        u0, u1, u2, u3 = ("c%d%d" % (k, t) for k in range(4))
        cp(R("wh", t), IX(R("bks"), C("lbu", 0, 16) if t == 0 else R("lbr", t - 1)))
        cp(R("wu", t), R("wh", t), s=False)
        for c in range(0, 4096, CH):
            cp(D("ga", t, c, c + CH), IX(R("ct"), D("wu", t, c // 16, (c + CH) // 16)))
        for h in range(4):
            mmg([[(o, C("tp", r, r + 128), rq(64 * h, 64 * h + 64))] +
                 [(o, C("e2", 14 - 2 * k, 142 - 2 * k), D("ga", t, 1024 * h + 8 * u + k, 1024 * h + 1024, 16)) for k in range(8)]
                 for u in (0, 1) for o in [B(u0, 256 * u + 64 * h, 256 * u + 64 * h + 64)]])
        ts(R("sq", t), B(u0, 0, 512), 0.0, None, A.not_equal, act=(F.Square, 0.0, 1.0))
        a, b = B(u1, 0, 256), B(u1, 256, 512)
        mm([(a, C("pm", 8, 136), D("sq", t, 0, 256)), (a, C("pm", 0, 128), D("sq", t, 256, 512))])
        ts(R("fit", t), a, 0.0, 2048.0, A.is_equal, A.mult, act=(F.Relu, 2048.0, -2048.0))
        mm([(b, ident, R("wh", t)), (b, R("tt"), R("fit", t))])
        ts(R("val", t), b, -2047.0, 0.0, A.add, A.max, act=(F.Relu, -2047.0, 1.0))
        mm([(B(u1, 0, 16), C("e1", 15 - l, 143 - l), D("val", t, l, 256, 16)) for l in range(16)])
        ts(R("wl", t), B(u1, 0, 16), -1.0, 0.0, A.add, A.max)
        mm([(B(u1, 64, 128), C("e1", 15 - 4 * h + s, 143 - 4 * h + s), D("val", t, 64 * h, 64 * h + 64)) for h in range(4)])
        cp(R("kv", t), B(u1, 64, 128))
        if t:
            send([R("kv", t)], [(-t, T.kv[:, t], R("ku", t - 1), "kv%d" % t, 0, 8)])
        cp(R("iw", t), IX(R("ivs"), R("wl", t))), cp(R("kw", t), IX(R("kds"), R("wl", t)))
        a, b = B(u2, 0, 256), B(u2, 256, 512)
        mm([(a, C("wn1", r, r + 128), rq(0, 256))], stop=False)
        mm([(a, R("w3", 0), R("iw", t)), (a, C("wn2", r, r + 128), rq(0, 256)), (a, R("w3", 1), R("iw", t))], start=False)
        ts(R("fitm", t), a, 0.0, None, A.is_equal)
        c = B(u3, 0, 256)
        mm([(c, hh, R("kw", t))])
        cp(R("hk", t), c)
        mm([(a, R("tt"), R("fitm", t))])
        relu(R("ohm", t), a)
        mm([(b, hh, R("ohm", t))])
        tt(R("pr", t), b, R("hk", t), A.mult)
        mm([(B(u3, 256, 320), C("e1m", 14 - 4 * h + s, 142 - 4 * h + s), D("ohm", t, 64 * h, 64 * h + 64)) for h in range(4)])
        mm([(c, R("h32", slice(SHIFT[t], SHIFT[t] + 8)), R("pr", t))])
        cp(R("kr", t), B(u3, 0, 320))
        if t:
            send([R("kr", t)], [(-t, T.kr[:, t], R("kl", t - 1), "kr%d" % t, 0, 8)])

    def kl(t, a, b):
        return D("kr", 0, a, b) if t == 0 else D("kl", t - 1, a, b)

    def ku(t):
        return R("kv", 0) if t == 0 else R("ku", t - 1)

    def kids(t):
        o = B("x%d" % t, 0, 256)
        mm([(o, R("ids", 3), R("ka")), (o, ident, kl(t, 0, 256))])
        cp(R("kx", t), o)

    def state(z):
        def q(h):
            return B("z%d" % z, 64 * h, 64 * h + 64)
        old = [(B("z%d" % z, 0, 256), R("ww"), R("zo", k)) for k in range(z - 1) if z < NT]
        cur = [(q(h), R("yy", h), x) for h in range(4) for x in (ku(z - 1), kl(z - 1, 256, 320))] if z else []
        if cur:
            mm(old + cur, stop=z == NT)
        if z < NT:
            mm([(q(h), R("xx", h), ku(z)) for h in range(4)], start=not cur)
        tt(R("zin", z), B("z%d" % z, 0, 256), R("cz"), A.max)

    def places(t, z):
        scan(R("zs"), R("d0"), z, A.mult, A.add)
        o = B("l%d" % t, 0, 16)
        mm([(o, C("ez", 15 - l, 143 - l), C("zs", l, 256, 16)) for l in range(16)])
        ts(R("off", t), o, 1023.0, None, A.add)
        ts(R("ofc", t), R("off", t), 96.0, None, A.min)

    def test(t):
        sw, kx, n = IX(R("sw"), R("off", t)), R("kx", t), 96
        i0 = op({"v": (60 + SCT * CY * 256, lambda: V.tensor_copy(sw["ap"], kx["ap"]))}, [kx, R("off", t)], [R("sw")])
        win, a0 = (R("lf2"), 0) if t == 0 else (C("tb", 0, 4096), 2048) if t % 2 else (C("tb", 2048, 6144), 0)
        ts(R("bi"), C("sw", 0, n), 2047, None, A.bitwise_and)
        for k in (0, 1):
            ts(R("ab", t, k, part=half[k]), R("sw", slice(0, n), part=half[k]), 1.0 / 2048, a0 - 1023.5 / 2048, A.mult, A.add)
            ts(R("ab", t, k, part=half[1 - k]), R("bi", part=half[k]), 2048.0 - a0, None, A.add)
        for a, b in CUT:
            for k in (0, 1):
                o, x = R("ta", t, k, slice(16 * a, 16 * b)), IX(win, R("ab", t, k, slice(a, b)))
                ts(o, x, -7.0, None, A.add, act=(F.Identity, -7.0, 1.0)) if t else cp(o, x)
        for a, b in CUT:
            w, u = 2 * (b - a), "d%d%d" % (t, a)
            for k in (0, 1):
                mm([(B(u, w * k, w * k + w), R("hm", 1 + 2 * d + k), R("ta", t, k, slice(16 * a + d, 16 * b, 8))) for d in range(7, -1, -1)])
            ts(R("nd", t, al, slice(a, b)), B(u, 0, 2 * w), 0.0, None, A.not_equal, act=(F.Abs, 0.0, 1.0))
            mm([(B(u, 256, 256 + w), R("l1"), R("nd", t, al, slice(a, b), h)) for h in (0, 1)])
            ts(R("fpm", t, al, slice(a, b)), B(u, 256, 256 + w), 0.5, None, A.is_lt, act=(F.Relu, 1.0, -1.0))
        r = B("r%d" % t, 0, n)

        def home(m, x):
            return [(r, R("rw", m, slice(4 - 4 * k, 12 - 4 * k)), x(k)) for k in (0, 1)]
        if t < NT - 1:
            mm([(r, R("xx", 0), C("ones", 0, n))], stop=False, after=[i0])
            mm(home(0, lambda k: R("fpm", t, k)), start=False)
            tt(C("res", 0, n), r, R("cres"), A.max)
            tt(R("zo", t), IX(R("res"), R("ofc", t)), R("zin", t + 1), A.min)
            places(t + 1, R("zo", t))
        r = B("f%d" % t, 0, n)
        mm([(B("f%d" % t, 0, 2 * n), R("t2"), R("fpm", t))])
        relu(R("oh", t), B("f%d" % t, 0, 2 * n))
        first = home(1, lambda k: D("oh", t, n * k, n * k + n))
        if t < NT - 1:
            mm(first)
            cp(D("rs2", t, 0, n), r)
            cp(R("zm", t), IX(R("rs2", t), R("ofc", t)))
        else:
            mm(first + home(0, lambda k: D("oh", t, n * k, n * k + n)))
            tt(C("res", 0, n), r, R("cres"), A.max)
            tt(R("zo", t), IX(R("res"), R("ofc", t)), R("zin", t + 1), A.min)

    mul(R("ka"), IX(R("kds"), R("lvu")), 0.5)
    for t in range(NT):
        claim(t)
        if t in (1, 2):
            unpack(t)
        kids(t)
    state(0)
    ts(R("z0"), R("zin", 0), col(17), None, A.min)
    places(0, R("z0"))
    for t in range(NT):
        state(t + 1)
        test(t)
        if t == 1:
            unpack(3)
    o = B("y", 0, 256, slice(0, 40))
    mm([(o, R("sel", NT + 1), C("ones", 0, 256))] + [(o, R("sel", t), R(z, t)) for t in range(NT - 1) for z in ("zo", "zm")], stop=False)
    mm([(o, R("sel", NT - 1), R("zo", NT - 1))], start=False)
    ysb = R("ysb", part=slice(0, 40))
    cp(ysb, o)
    end = dma([(T.y[:], ysb["ap"])], [ysb], [], 40960, "y")
    return ops, uses, sent[0], ops[end]["sem"]


def order_calls(ops, uses):
    n = len(ops)
    cost = [{e: c for e, (c, f) in o["var"].items()} for o in ops]
    lat = [o["sem"][2] if o["sem"] else LAT for o in ops]
    move = [o["move"] for o in ops]
    rs = np.random.RandomState(SEED)
    either = [i for i in range(n) if len(cost[i]) > 1]

    def graph(deps):
        succ, left = [[] for _ in ops], [len(d) for d in deps]
        for i, d in enumerate(deps):
            for j in d:
                succ[j].append(i)
        topo = [i for i in range(n) if not left[i]]
        for i in topo:
            for j in succ[i]:
                left[j] -= 1
                if not left[j]:
                    topo.append(j)
        kind = [{j: 0 if r is None else 1 if ops[j]["sem"] or move[j] else 3 if r else 2 for j, r in d.items()} for d in deps]
        fw = [[(j, k, lat[j]) for j, k in d.items()] for d in kind]
        bw = [[(j, kind[j][i], lat[i] + move[i]) for j in succ[i]] for i in range(n)]
        return (topo, fw, move), (topo[::-1], bw, [0.0] * n)

    def place(way, key, eng):
        topo, before, mv = way
        key = list(key)
        for i in topo:
            for j, k, l in before[i]:
                if key[j] >= key[i]:
                    key[i] = key[j] + 1e-3
        busy, got, start, fin, held = {e: ([], [], []) for e in "vstpyn"}, [""] * n, [0.0] * n, [0.0] * n, [None] * n
        done, dmas = [0.0] * n, 0.0
        for i in sorted(range(n), key=lambda i: key[i]):
            best = None
            for e in (eng[i],) if eng else cost[i]:
                c, t, h = cost[i][e], 0.0, None
                for j, k, l in before[i]:
                    x = done[j] + l if k == 1 or (k and got[j] != e) or (k == 3 and e != "t") else fin[j]
                    if x > t:
                        t, h = x, j
                s0, s1, who = busy[e]
                k = len(s1)
                while k and s1[k - 1] > t:
                    k -= 1
                while k < len(s0) and t + c > s0[k]:
                    t, h = s1[k], ~who[k]
                    k += 1
                x = t + c * (2.0 if e == "v" else 1.0)
                if best is None or x < best[0]:
                    best = (x, e, t, k, h)
            x, e, t, k, held[i] = best
            start[i], got[i] = t, e
            fin[i] = done[i] = t + cost[i][e]
            if mv[i]:
                dmas = done[i] = max(dmas, fin[i]) + mv[i]
            busy[e][0].insert(k, t), busy[e][1].insert(k, fin[i]), busy[e][2].insert(k, i)
        return max(done) + 1e-4 * sum(fin), got, start, fin, held

    def blocked(plan):
        i, out = int(np.argmax(plan[3])), []
        while plan[4][i] is not None:
            h = plan[4][i]
            if h < 0:
                h = ~h
                out.append((i, h))
            i = h
        return out

    def search(deps, plan, tries):
        fw, bw = graph(deps)
        cur = best = place(fw, plan[2], plan[1])
        pairs = blocked(cur)
        for k in range(tries):
            key, eng, u = list(cur[2]), list(cur[1]), rs.rand()
            if u < 0.05:
                b = place(bw, [-x for x in cur[3]], eng)
                key = [-x for x in b[3]]
            elif u < 0.35 and pairs:
                i, h = pairs[int(rs.randint(len(pairs)))]
                x = i if rs.rand() < 0.5 else h
                if len(cost[x]) > 1 and rs.rand() < 0.6:
                    eng[x] = str(rs.choice([e for e in cost[x] if e != eng[x]]))
                elif x == i:
                    key[i] = key[h] - 1 - float(rs.exponential()) * 300
                else:
                    key[h] = key[i] + 1 + float(rs.exponential()) * 600
            elif u < 0.55:
                for i in rs.choice(either, int(rs.randint(1, 4))).tolist():
                    eng[i] = str(rs.choice(list(cost[i])))
            elif u < 0.85:
                for i in rs.randint(0, n, int(rs.randint(1, 5))).tolist():
                    key[i] += float(rs.randn()) * 1500
            else:
                i, w, d = int(rs.randint(0, n)), int(rs.randint(2, 30)), float(rs.randn()) * 2000
                key[i:i + w] = [x + d for x in key[i:i + w]]
            r = place(fw, key, eng)
            if r[0] < cur[0] + HEAT * (1 - k / tries) * float(rs.exponential()):
                cur = r
                pairs = blocked(cur)
                if r[0] < best[0]:
                    best = r
        return best

    def banks(plan):
        deps, bank, held = [dict(o["deps"]) for o in ops], {}, [None] * 8

        def needs(a, b):
            todo, seen = [a], {a}
            while todo:
                x = todo.pop()
                if x == b:
                    return True
                for y in deps[x]:
                    if y not in seen:
                        seen.add(y)
                        todo.append(y)
            return False
        for u in sorted(uses, key=lambda u: plan[2][uses[u][0]]):
            free = sorted(range(8), key=lambda k: -1 if held[k] is None else plan[3][held[k]])
            k = [k for k in free if held[k] is None or not needs(held[k], uses[u][0])][0]
            if held[k] is not None:
                deps[uses[u][0]][held[k]] = True
            bank[u], held[k] = "p%d" % k, uses[u][-1]
        return deps, bank

    prio = [0.0] * n
    for i in range(n - 1, -1, -1):
        prio[i] += min(cost[i].values()) + lat[i] + move[i]
        for j in ops[i]["deps"]:
            prio[j] = max(prio[j], prio[i])
    plan = search([o["deps"] for o in ops], (0, None, [-x for x in prio]), 2 * TRIES)
    INFO["free"] = max(plan[3])
    best = None
    for k in range(ROUNDS):
        deps, bank = banks(plan)
        plan = search(deps, plan, TRIES)
        if best is None or plan[0] < best[0][0]:
            best = (plan, deps, bank)
    plan, deps, bank = best
    INFO["bank"], INFO["lat"] = bank, lat
    INFO["plan"] = (max(plan[3]), plan[1], sorted(range(n), key=lambda i: (plan[2][i], i)), deps)
    INFO["show"] = [(plan[2][i], plan[3][i], plan[1][i], ops[i]["tag"]) for i in range(n)]


def rank_program(g, core, T, topo):
    rank = T.rank_of(core)
    if rank is None:
        return
    if "plan" not in INFO:
        order_calls(*record(g, core, rank, T, topo)[:2])
    ops, uses, sent, stored = record(g, core, rank, T, topo)
    end, eng, order, deps = INFO["plan"]
    Q = {"v": g.vector, "s": g.scalar, "t": g.tensor, "p": g, "y": g.sync}

    pos, seen, waits, need = {}, {}, [], set()
    for k, i in enumerate(order):
        pos[i] = k
        e, w = eng[i], {}
        if e != "n":
            for j, raw in deps[i].items():
                if raw is None:
                    continue
                if ops[j]["sem"]:
                    if (e, j) not in seen:
                        seen[(e, j)] = 1
                        w[("sem", j)] = j
                elif (eng[j] != e or (raw and e != "t")) and pos[j] > seen.get((e, eng[j]), -1):
                    if ("q", eng[j]) not in w or pos[w[("q", eng[j])]] < pos[j]:
                        w[("q", eng[j])] = j
            for (kind, x), j in w.items():
                if kind == "q":
                    seen[(e, x)] = pos[j]
                    need.add(j)
        waits.append(w)
    count, cnt = {}, dict.fromkeys("vstp", 0)
    for i, w in zip(order, waits):
        e = eng[i]
        if e == "n":
            continue
        for (kind, x), j in w.items():
            if kind == "q":
                Q[e].wait_ge(T.sem[x], count[j])
            else:
                Q[e].wait_ge(ops[j]["sem"][0], ops[j]["sem"][1])
        r = ops[i]["var"][e][1]()
        if i in need:
            cnt[e] += 1
            count[i] = cnt[e]
            r.then_inc(T.sem[e], 1)
    g.wait_ge(T.sem.snt, sent)
    g.sync.wait_ge(stored[0], stored[1])
